import numpy as np, ml_dtypes
CORES = [35,38,43,46]
N = 4
BF = ml_dtypes.bfloat16
def gentries(a):
    return np.ascontiguousarray(a.reshape(8, 16, -1).transpose(0, 2, 1)).reshape(8, -1)
def gtable(e):
    e = np.asarray(e); return np.ascontiguousarray(e.reshape(8, -1, 16).transpose(0, 2, 1)).reshape(128, -1).astype(np.int32)
W, L, K, CAP, NEED, RO = 4096, 128, 4, 64, 9, 4
def take(a, i):
    return np.take_along_axis(a, i.reshape(N, 8, -1), 2).reshape(i.shape)
def shade(rng, h):
    return np.clip(h[:, :, None, :] + rng.integers(-40, 41, (N, 8, 16, h.shape[2])), 0, 255)
def parts(rng):
    h = rng.integers(0, 256, (N, 8, W)); X = shade(rng, h); A = shade(rng, rng.integers(0, 256, (N, 8, L)))
    F = W // 32; pc = np.argsort(rng.random((N, 8, W)), axis=-1); fam = np.argsort(pc, axis=-1) // 32
    first = take(rng.integers(0, W, (N, 8, F)), fam)[:, :, None, :]; size = take(rng.choice(np.array([6, 12, 24, 96]), (N, 8, F)), fam)[:, :, None, :]
    I = take(np.argsort(h, axis=-1), (first + (rng.random((N, 8, 16, W)) * size).astype(np.int64)) % W)
    I = np.where(rng.random((N, 8, 16, W)) < 0.25, rng.integers(0, W, (N, 8, 16, W)), I)
    O = take(pc, 32 * rng.integers(0, F, (N, 8, 1, W)) + rng.integers(0, 32, (N, 8, K, W)))
    mixed = (rng.random((N, 8, 1, W)) < 0.4) | (rng.random((N, 8, K, W)) < 0.1)
    O = np.where(mixed, rng.integers(0, W, (N, 8, K, W)), O)
    return I, X, O, rng.integers(0, W, (N, 8, L)), A, rng.integers(600, 2000, (N, 8, RO))
def pack(I, X, O, g, A, T):
    return {"icol": np.ascontiguousarray(I.reshape(N, 128, W)).astype(np.int32), "pat": np.ascontiguousarray(X.reshape(N, 128, W)).astype(np.float32).astype(BF),
            "alt": np.ascontiguousarray(O.reshape(N, 8 * K, W)).astype(np.int32), "gate": np.stack([gtable(a) for a in g]),
            "acc0": np.ascontiguousarray(A.reshape(N, 128, L)).astype(np.float32).astype(BF), "th": np.ascontiguousarray(T).astype(np.int32)}
def setup_inputs(rng):
    return pack(*parts(rng))
def setup_inputs_spread(rng):
    I, X, O, g, A, T = parts(rng)
    X = np.minimum((np.exp2(8 * rng.random((N, 8, 1, W))) * rng.random((N, 8, 16, W))).astype(np.int64), 255)
    A = np.minimum((np.exp2(8 * rng.random((N, 8, 1, L))) * rng.random((N, 8, 16, L))).astype(np.int64), 255)
    I = np.minimum((W * rng.random((N, 8, 16, W)) ** rng.choice(np.array([1.0, 2.0, 4.0]), (N, 8, 1, W))).astype(np.int64), W - 1)
    O = np.minimum((W * rng.random((N, 8, K, W)) ** rng.choice(np.array([1.0, 2.0, 4.0]), (N, 8, 1, W))).astype(np.int64), W - 1)
    I[:, 1::2] = W - 1 - I[:, 1::2]; O[:, 2::4] = W - 1 - O[:, 2::4]
    T = np.minimum(np.exp2(5 + 7 * rng.random((N, 8, RO))).astype(np.int64), 4080)
    return pack(I, X, O, g, A, T)
def setup_inputs_ends(rng):
    e = np.array([0, W - 1])
    I = np.where(rng.random((N, 8, 1, W)) < 0.25, rng.integers(0, W, (N, 8, 16, W)), e[rng.integers(0, 2, (N, 8, 16, W))])
    O = np.where(rng.random((N, 8, K, W)) < 0.3, rng.integers(0, W, (N, 8, K, W)), e[rng.integers(0, 2, (N, 8, K, W))])
    g = np.where(rng.random((N, 8, L)) < 0.3, rng.integers(0, W, (N, 8, L)), e[rng.integers(0, 2, (N, 8, L))])
    X = 255 * np.where(rng.random((N, 8, 1, W)) < 0.5, rng.integers(0, 2, (N, 8, 1, W)), rng.integers(0, 2, (N, 8, 16, W)))
    A = 255 * np.where(rng.random((N, 8, 1, L)) < 0.5, rng.integers(0, 2, (N, 8, 1, L)), rng.integers(0, 2, (N, 8, 16, L)))
    T = 4080 * ((np.arange(N)[:, None, None] + np.arange(8)[:, None] + np.arange(RO)) % 2)
    T[:, 2, 1:] = 2040; T[:, 5, 1:] = 1785; T[1:N - 1, 6, 0] = 4079
    T[0, :, 0] = 0; T[N - 1, :, 0] = 4080
    X[..., 0] = 0; X[..., W - 1] = 255; A[..., 0] = 0; A[..., L - 1] = 255; g[..., 0] = 0; g[..., L - 1] = W - 1
    X[0, :, 1, :] = X[0, :, 0, :]; A[0, :, 0, :] = 0; A[0, :, 1, :] = 255
    I[N - 1, :, 15, :] = W - 1
    I[N - 1, :, :15, 0] = 0; I[N - 1, 1::2, 3, 0] = W - 1; I[N - 1, :, 0, W - 1] = W - 1; O[N - 1, :, 0, W - 1] = W - 1
    I[1, :, :, 2] = W - 1
    g[N - 1, :, 1] = 1; O[N - 1, :, :, 1] = 1; I[N - 1, :, 0, 1] = 1
    g[N - 1, :, 2] = W - 2; O[N - 1, :, :, W - 2] = W - 2; I[N - 1, :, 0, W - 2] = W - 2
    return pack(I, X, O, g, A, T)
def setup_inputs_corners(rng):
    I, X, O, g, A, T = parts(rng); h = W // 2; want = (0, 1, CAP - 1, CAP, CAP + 1, L, CAP, 2); c = np.arange(W)
    E = np.zeros((N, W), np.int64); warm = np.zeros((N, 40), np.int64); late = np.full(N, -1)
    for r in range(N):
        for u in range(8):
            n = want[(u + r + 5) % 8]; t0 = (0, 1, 7, 254, 255)[(u + 3 * r) % 5]
            q = rng.permutation(W); hot = q[:40].reshape(2, 20); cold = (q[40:h], q[h:])
            x = rng.integers(100, 256, (16, W)); i = rng.integers(0, 16, W)
            near = np.nonzero(rng.random(W) < 0.5)[0]; x[:, near] = 0; x[i[near], near] = t0; x[(i[near] + 1) % 16, near] = 1
            hs = q[:40]; x[:, hs] = 0; x[i[hs], hs] = t0 * rng.integers(0, 2, 40)
            flip = u % 2 == 1
            X[r, u] = 255 - x if flip else x; A[r, u] = 255 if flip else 0
            e = rng.permutation(W); sa = e[:W // 4]; sb = e[W // 4:h]; dd = e[h:]; sv = np.zeros(W, bool); sv[e[:h]] = True
            cl = rng.integers(0, 2, W); cl[sa] = 0; cl[sb] = 1
            nh = np.where(sv, rng.choice(np.array([NEED, NEED + 1, 16]), W), rng.choice(np.array([0, NEED - 2, NEED - 1]), W))
            rk = (np.arange(16)[:, None] * (2 * rng.integers(0, 8, W) + 1) + rng.integers(0, 16, W)) & 15
            hn = np.where(rk == 0, hot[cl, 0], hot[cl, rng.integers(0, 20, (16, W))])
            cn = np.where(cl == 0, cold[0][rng.integers(0, len(cold[0]), (16, W))], cold[1][rng.integers(0, len(cold[1]), (16, W))])
            I[r, u] = np.where(rk < nh, hn, cn)
            f = np.concatenate([np.array([W - 1, 0]), 1 + rng.permutation(W - 2)]); learn = np.zeros(W, bool); learn[f[:h]] = True
            p1 = rng.integers(0, K, W); p2 = (p1 + 1 + rng.integers(0, K - 1, W)) % K; way = rng.random(W)
            o = dd[rng.integers(0, h, (K, W))]
            one = learn & (way < 0.5); o[p1[one], c[one]] = e[rng.integers(0, h, W)][one]
            own = one & sv & (rng.random(W) < 0.3); o[p1[own], c[own]] = c[own]
            two = learn & (way >= 0.5); o[p1[two], c[two]] = sa[rng.integers(0, W // 4, W)][two]; o[p2[two], c[two]] = sa[rng.integers(0, W // 4, W)][two]
            full = learn & (way >= 0.75); o[:, full] = sb[rng.integers(0, W // 4, (K, W))][:, full]
            apart = ~learn & (way < 0.4); o[p1[apart], c[apart]] = sa[rng.integers(0, W // 4, W)][apart]; o[p2[apart], c[apart]] = sb[rng.integers(0, W // 4, W)][apart]
            O[r, u] = o
            lane = rng.permutation(L); g[r, u, lane[:n]] = f[:n]; g[r, u, lane[n:]] = f[h:h + L - n]
            if u == 7:
                E[r] = e; warm[r] = hs
                if n >= CAP: late[r] = np.sort(lane[:n])[CAP - 1]
            T[r, u, 0] = t0
            if (u + r) % 3 < 2: T[r, u, 1] = 4080 * ((u + r) % 3)
    for r in range(N):
        if late[r] < 0: continue
        z = (r + 1) % N; c0 = int(g[r, 7, late[r]]); s = E[r, :h]; b = s ^ 1
        far = np.max(np.add.reduce(np.abs(X[z, 7][:, I[z, 7][:, b]] - X[z, 7][:, b][:, None, :]), axis=0), axis=0)
        s = s[(far >= 2048) & ~np.isin(s, O[r, 7][:, g[r, 7]]) & ~np.isin(s, warm[r]) & ~np.isin(b, g[z, 7])]
        O[r, 7, :, c0] = E[r, h:][rng.integers(0, h, K)]; O[r, 7, int(rng.integers(0, K)), c0] = rng.choice(s)
    return pack(I, X, O, g, A, T)
def setup_inputs_ties(rng):
    I, X, O, g, A, T = parts(rng); B = 8; c = np.arange(W)
    base = rng.integers(0, 256, (N, 8, 16, B)); sort = np.argsort(rng.random((N, 8, W)), axis=-1) % B; lit = np.argsort(sort, axis=-1, kind="stable")
    rk = (np.arange(16)[:, None] * (2 * rng.integers(0, 8, (N, 8, 1, W)) + 1) + rng.integers(0, 16, (N, 8, 1, W))) & 15
    ty = np.where(rk < rng.integers(NEED - 1, NEED + 1, (N, 8, 1, W)), c % B, (c // B) % B)
    I = take(lit, ty * (W // B) + rng.integers(0, 6, (N, 8, 16, W)))
    X = np.take_along_axis(base, sort[:, :, None, :], 3)
    A = np.take_along_axis(base, rng.integers(0, B, (N, 8, 1, L)), 3); A[..., :16] = base[..., :1]
    O = np.where(rng.random((N, 8, 1, W)) < 0.6, O[:, :, :1] % 64 + 64 * rng.integers(0, W // 64, (N, 8, K, W)), O)
    T[:, :, 0] = np.clip(np.add.reduce(np.abs(base[..., 0] - base[..., 1]), axis=2) + (np.arange(N)[:, None] + np.arange(8)) % 3 - 1, 0, 4080)
    return pack(I, X, O, g, A, T)
def setup_inputs_clash(rng):
    I, X, O, g, A, T = parts(rng)
    q = np.argsort(rng.random((8, W // 2)), axis=-1)[:, :16]; s = np.ascontiguousarray(np.broadcast_to(np.concatenate([2 * q, 2 * q + 1], axis=1), (N, 8, 32)))
    I = np.where(rng.random((N, 8, 16, W)) < 0.8, take(s, rng.integers(0, 32, (N, 8, 16, W))), I)
    O = np.where(rng.random((N, 8, K, W)) < 0.7, take(s, rng.integers(0, 32, (N, 8, K, W))), O)
    g = take(s, rng.integers(0, 32, (N, 8, L))); T = rng.integers(1000, 2600, (N, 8, RO))
    v = rng.integers(0, 21, (N, 3, 16, W)); X[:, 1::3] = np.where(rng.random((N, 3, 1, W)) < 0.5, v, 255 - v)
    v = rng.integers(0, 21, (N, 3, 16, L)); A[:, 1::3] = np.where(rng.random((N, 3, 1, L)) < 0.5, v, 255 - v)
    T[:, 1::3] = rng.integers(3072, 3840, (N, 3, RO))
    return pack(I, X, O, g, A, T)
def check_inputs(d):
    bad = []
    for k, lo, hi in (("icol", 0, W - 1), ("pat", 0, 255), ("alt", 0, W - 1), ("gate", 0, W - 1), ("acc0", 0, 255), ("th", 0, 4080)):
        v = np.asarray(d[k]).astype(np.float64)
        if not (np.min(v) >= lo and np.max(v) <= hi): bad.append("range of " + k)
        elif np.any(v != np.floor(v)): bad.append("whole numbers in " + k)
    return bad
def pick(Xr, n):
    return Xr[np.arange(8).reshape((8,) + (1,) * (n.ndim - 1)), n]
def rewrite(Ir, Xr, c, v, use):
    n = np.take_along_axis(Ir, c[:, None, :], 2)
    far = np.add.reduce(np.abs(pick(Xr, n) - pick(Xr, c)[:, None]), axis=-1); p = np.argmax(far, axis=1)
    for g in range(8):
        j = np.nonzero(use[g])[0]; j = j[np.unique(c[g, j], return_index=True)[1]]
        Ir[g, p[g, j], c[g, j]] = v[g, j]
def reference(icol, pat, alt, gate, acc0, th):
    I = icol.astype(np.int32).reshape(N, 8, 16, W); O = alt.astype(np.int64).reshape(N, 8, K, W); T = th.astype(np.int64)
    X = np.ascontiguousarray(pat.astype(np.float32).astype(np.int32).reshape(N, 8, 16, W).transpose(0, 1, 3, 2))
    A = np.ascontiguousarray(acc0.astype(np.float32).astype(np.int32).reshape(N, 8, 16, L).transpose(0, 1, 3, 2))
    G = np.stack([gentries(a) for a in gate]).astype(np.int64)
    for t in range(RO):
        sent = []
        for r in range(N):
            g = G[r]; o = np.take_along_axis(O[r], g[:, None, :], 2)
            col = np.take_along_axis(I[r], o.reshape(8, 1, K * L), 2).reshape(8, 16, K, L)
            dist = np.add.reduce(np.abs(pick(X[r], col) - A[r][:, None, None, :, :]), axis=-1)
            sv = np.add.reduce((dist <= T[r, :, t].reshape(8, 1, 1, 1)).astype(np.int32), axis=1) >= NEED
            ns = np.add.reduce(sv.astype(np.int32), axis=1); first = np.argmax(sv, axis=1)
            fc = np.take_along_axis(col, first[:, None, None, :], 2)[:, :, 0, :]
            ok = np.ones((8, 16, L), bool)
            for k in range(K):
                ok &= np.any(fc[:, :, None, :] == col[:, None, :, k, :], axis=2) | ~sv[:, None, k, :]
            com = np.take_along_axis(fc, np.argmax(ok, axis=1)[:, None, :], 1)[:, 0].astype(np.int64)
            sole = np.take_along_axis(o, first[:, None, :], 1)[:, 0]
            lrn = (ns == 1) | ((ns >= 2) & np.any(ok, axis=1))
            m = np.where(ns == 1, sole, np.where(lrn, com, o[:, K - 1]))
            rewrite(I[r], X[r], g, m, lrn)
            a = np.zeros((8, CAP), np.int64); b = np.zeros((8, CAP), np.int64); use = np.zeros((8, CAP), bool)
            for u in range(8):
                j = np.nonzero(lrn[u])[0][:CAP]
                a[u, :len(j)] = m[u, j] ^ 1; b[u, :len(j)] = g[u, j] ^ 1; use[u, :len(j)] = True
            sent.append((a, b, use))
            A[r] = np.where(lrn[:, :, None], (A[r] + pick(X[r], m)) >> 1, np.abs(A[r] - pick(X[r], o[:, 0])))
            G[r] = ((m * g >> 4) + 37 * g + int(np.count_nonzero(lrn))) & (W - 1)
        for r in range(N):
            q = (r + 1 + t % (N - 1)) % N; a, b, use = sent[r]
            rewrite(I[q], X[q], a, b, use)
    yc = np.add.reduce(I * np.arange(1, 17, dtype=np.int32).reshape(1, 1, 16, 1), axis=2)
    return {"yc": yc.astype(np.float32), "ya": np.ascontiguousarray(A.transpose(0, 1, 3, 2)).reshape(N, 128, L).astype(np.float32), "yg": G.astype(np.float32)}

@@ -1,0 +1,689 @@
+from concourse.mybir import AluOpType, AxisListType, ActivationFunctionType
+
+RO = 4
+NV = 68
+NS = 128 - NV
+NG = 60
+NB = 2
+NA = 8
+NE = 4
+LATE = True
+N16 = 13
+HUGE = float(1 << 26)
+BK = 8192.0
+BIG = 65 * 2048.0
+FALL = 73728.0
+K0 = 3 * BIG + 61440.0 + 2048.0 + 8192.0
+MAGIC = 12582912.0
+
+F, B, H, I32, U = "float32", "bfloat16", "float16", "int32", "uint16"
+_S = {
+    "Ii": (4096, I32), "Iw": (4224, F), "Pw": (8192, B), "alti": (1024, I32), "altw": (1024, F), "iot": (4096, F),
+    "Ih": (256 * N16, H), "ycs": (256, F), "thi": (4, I32), "thf": (4, F), "thc": (4, F),
+    "pi": (1, I32), "pt": (8, I32), "pc": (16, F), "c16": (128, F), "cg": (128, F), "cc": (144, F), "c4": (128, F), "c8": (128, F),
+    "tmp": (128, F), "tm2": (128, F), "Z1": (144, B), "Z2": (144, B), "Zm": (144, B), "Zh": (144, B), "Zf": (144, F),
+    "idb": (128, B), "nid": (128, B), "bid": (128, B), "BO": (128, B), "BOf": (128, F), "B16": (8, B), "ones": (128, B),
+    "LmB": (128, B), "SelK": (512, B), "Rep": (128, B), "LF": (1024, B), "Lsig": (128, B), "Ldel": (128, B), "RE": (16, B),
+    "mT": (128, F), "QS": (8, F), "EXPL": (8, U), "EXPQ": (8, U), "dmin": (128, F), "dmax": (128, F), "k15": (128, F),
+    "s16": (512, F), "s4": (128, F), "ltile": (8, F), "dump": (8, F), "tri": (128, B), "id4": (4, B), "alph": (2, F), "one8": (8, F),
+    "ci": (8, I32), "cf": (8, F), "cu": (8, U), "lou": (8, U), "hiu": (8, U), "w1": (8, I32), "w2": (8, I32), "w3": (8, I32),
+    "A": (128, B), "nA": (128, B), "A16": (16 * NV, B), "Af": (128, F), "cR": (128, F), "mR": (128, F), "bR": (128, F),
+    "mj": (128, B), "Ogm": (128, H), "sc": (512, F), "sc4": (128, F), "OL": (32, F), "OLu": (32, U), "OSu": (32, U),
+    "Cu": (512, U), "CuS": (4 * NS, U), "Cw": (512, F), "Ch": (384, H), "D": (64 * NV, B), "Rl": (64 * NV, B), "GS": (64 * NS, B),
+    "near": (512, B), "x": (64, F), "idx": (8, U), "Fh": (128, H), "Xab": (1536, F), "E": (1536, B), "svX": (384, B), "z": (384, B),
+    "sk": (128, F), "lT": (128, F), "sv": (64, F), "y": (104, F), "mk": (8, I32), "mi": (8, I32), "lrn": (8, B), "v": (128, F),
+    "mu": (8, U), "selu": (8, U), "lru": (8, U), "ecol": (1, F), "vs": (8, F), "Ea": (1024, B), "Eb": (1024, B), "Lt": (2048, B), "iox": (4096, F), "mTK": (128, F), "idf": (128, F), "nif": (128, F), "tg2": (8, U),
+    "C2u": (128, U), "old": (128, F), "Xc": (128, B), "G2": (2048, B), "ab": (2048, B), "key": (128, F), "oh": (128, B),
+    "dif": (128, F), "tt": (128, F), "u": (128, F), "au": (128, F), "aR": (128, F),
+    "msg1": (16 * RO + 16, U), "msg2": (8 * RO, U), "land1": (16 * RO, U), "land2": (8 * RO, U),
+}
+_S.update({"B32": (8, B), "B16n": (8, B), "zero": (512, B)})
+ALIAS = {}
+for _p, _d, _l in (("kb", B, "Z1 Z2 Zm idb nid bid BO ones LmB tri B16 B32 B16n RE"), ("kf", F, "dmin dmax k15 mT s4 ltile dump one8 QS c4 c8 cg")):
+    _o = 0
+    for _k in _l.split():
+        ALIAS[_k] = (_p, _o, _S[_k][0]); _o += _S.pop(_k)[0]
+    _S[_p] = (_o, _d)
+SCRATCH = {k: ("sbuf", [128, v[0]], v[1]) for k, v in _S.items()}
+for _b in "ABCDEFGH":
+    SCRATCH["p" + _b] = ("psum", [128, 512], F)
+NDMA = 14
+SEMAPHORES = ["cV", "cS", "cP", "cG", "sent"] + ["d%d" % i for i in range(NDMA)] + ["a%d" % i for i in range(2 * RO)]
+CNT = {"V": "cV", "S": "cS", "P": "cP", "G": "cG"}
+CY, GA, SCA, PE, HOP = 1.04, 1.62, 3.95, 0.52, 110.0
+SEED = 1
+PASSES = 400
+MOVES = 1200
+HEAT = 50.0
+NOISE = 2500.0
+REPORT = {}
+
+
+def _two(name):
+    return name in _S and _S[name][1] in (B, H, U)
+
+
+def build(g, core, T, topo):
+    A_ = AluOpType
+    AF = ActivationFunctionType
+    ops, acc = [], {}
+    nd = [0]
+    now, seen = [-1], {}
+
+    def R(b, c0=0, c1=None, st=1, p0=0, p1=128):
+        if b in ALIAS:
+            return (ALIAS[b][0], ALIAS[b][1] + c0, ALIAS[b][1] + (ALIAS[b][2] if c1 is None else c1), st, p0, p1)
+        return (b, c0, SCRATCH[b][1][1] if c1 is None else c1, st, p0, p1)
+
+    def ind(w, o):
+        return ("@", w, o)
+
+    def ap(r):
+        if r[0] == "@":
+            return ap(r[1]).indirect(ap(r[2]))
+        if r[3] == 1:
+            return T[r[0]][r[4]:r[5], r[1]:r[2]]
+        return T[r[0]][r[4]:r[5], r[1]:r[2]:r[3]]
+
+    def n_of(r):
+        return 16 * (r[2][2] - r[2][1]) if r[0] == "@" else (r[2] - r[1] + r[3] - 1) // r[3]
+
+    def add(eng, fns, reads, writes, cost, kind="c", lat=0.0, after=(), sem=None):
+        rd, wr = [], []
+        for r in reads:
+            if isinstance(r, tuple):
+                rd += [r[1], r[2]] if r[0] == "@" else [r]
+        for r in writes:
+            if r[0] == "@":
+                wr.append(r[1]); rd.append(r[2])
+            else:
+                wr.append(r)
+        i = len(ops)
+        hard, soft = set(), set(after)
+        for r, w in [(r, False) for r in rd] + [(r, True) for r in wr]:
+            ps = SCRATCH[r[0]][0] == "psum"
+            for (j, c0, c1, wj) in acc.get(r[0], []):
+                ej = ops[j]["eng"]
+                if ps:
+                    if ej != eng or (eng != "P" and (w or wj)):
+                        hard.add(j)
+                    elif eng == "P":
+                        soft.add(j)
+                elif (w or wj) and c0 < r[2] and r[1] < c1:
+                    hard.add(j)
+        for r, w in [(r, False) for r in rd] + [(r, True) for r in wr]:
+            acc.setdefault(r[0], []).append((i, r[1], r[2], w))
+        name = "%s %s %d" % (eng, (wr or rd or [("",)])[0][0], now[0] < 0)
+        seen[name] = seen.get(name, 0) + 1
+        ops.append(dict(round=now[0], tag="%s %d" % (name, seen[name]), eng=eng, fns=fns, hard=hard, soft=soft - hard, cost=cost, kind=kind, lat=lat, sem=sem, w=(wr or rd or [("",)])[0][0]))
+        return i
+
+    def vcost(out, ins, tt=False):
+        if out[0] == "@":
+            return 50 + n_of(out) * SCA
+        if any(r[0] == "@" for r in ins):
+            return 50 + n_of(out) * GA
+        k = 1.0
+        if tt:
+            k = 1.0 if any(SCRATCH[r[0]][0] == "psum" for r in ins) else 2.0
+        elif all(_two(r[0]) for r in ins + [out]):
+            k = 0.5
+        return max(64.0, n_of(ins[0] if ins else out) * k) * CY
+
+    def sa(s):
+        return ap(s) if isinstance(s, tuple) else s
+
+    def cp(out, a):
+        return add("V", [lambda: g.vector.tensor_copy(ap(out), ap(a))], [a], [out], vcost(out, [a]))
+
+    def tt(out, a, b, op):
+        return add("V", [lambda: g.vector.tensor_tensor(ap(out), ap(a), ap(b), op)], [a, b], [out], vcost(out, [a, b], True))
+
+    def ts(out, a, s1, op0, s2=None, op1=None):
+        if op1 is None:
+            fn = lambda: g.vector.tensor_scalar(ap(out), ap(a), sa(s1), None, op0)
+        else:
+            fn = lambda: g.vector.tensor_scalar(ap(out), ap(a), sa(s1), sa(s2), op0, op1)
+        return add("V", [fn], [a, s1, s2], [out], vcost(out, [a]))
+
+    def scan(out, d0, d1, op0, op1, first=0.0):
+        return add("V", [lambda: g.vector.tensor_tensor_scan(ap(out), ap(d0), ap(d1), first, op0, op1)], [d0, d1], [out], vcost(out, [d0, d1]))
+
+    def mset(out, c):
+        return add("V", [lambda: g.vector.memset(ap(out), c)], [], [out], vcost(out, []))
+
+    def act_fn(out, a, f, bias, scale):
+        return lambda: g.scalar.activation(ap(out), ap(a), f, bias=sa(bias), scale=sa(scale))
+
+    def acost(out, a):
+        return 65 + n_of(out) * GA if a[0] == "@" else max(64.0, n_of(out)) * CY
+
+    def act(out, a, f=AF.Identity, bias=0.0, scale=1.0):
+        return add("S", [act_fn(out, a, f, bias, scale)], [a, bias, scale], [out], acost(out, a))
+
+    def acts(lst, after=()):
+        return add("S", [act_fn(*x) for x in lst], [r for x in lst for r in (x[1], x[3], x[4])], [x[0] for x in lst],
+                   sum(acost(x[0], x[1]) for x in lst), after=after)
+
+    def chain(ids):
+        for a, b in zip(ids, ids[1:]):
+            if a not in ops[b]["hard"]:
+                ops[b]["soft"].add(a)
+
+    def mm_fn(o, l, r, s0, s1):
+        return lambda: g.tensor.matmul(ap(o), ap(l), ap(r), s0, s1)
+
+    def mms(lst):
+        c = sum(max(min(64, n_of(x[1])), n_of(x[2])) * (4 if _S[x[1][0]][1] == F else 1) * PE for x in lst)
+        return add("P", [mm_fn(*x) for x in lst], [r for x in lst for r in (x[1], x[2])], [x[0] for x in lst], c)
+
+    def grp(out, prs):
+        return [(out, l, r, i == 0, i == len(prs) - 1) for i, (l, r) in enumerate(prs)]
+
+    def iota(out, pat, base, cm):
+        if _S[out[0]][1] == I32:
+            fn = lambda: g.iota(ap(out), pat, base, cm)
+        else:
+            fn = lambda: g.iota(ap(out), pat, base, cm, allow_small_or_imprecise_dtypes=True)
+        return add("G", [fn], [], [out], 160 + 2 * n_of(out) * CY)
+
+    def sel(out, a, pat, fill, base, cm):
+        return add("G", [lambda: g.affine_select(ap(out), ap(a), pat, A_.not_equal, fill, base, cm)], [a], [out], 200 + 2 * n_of(out) * CY)
+
+    def dma(q, o, i, reads, writes, lat):
+        s = "d%d" % nd[0]; nd[0] += 1
+        e = g.sync if q == "Y" else g.scalar
+        return add(q, [lambda: e.dma_start(o, i)], reads, writes, 100.0, "d", lat, sem=s)
+
+    rank = T.rank_of(core)
+    n = len(T.cores)
+    nsent = [0]
+
+    def send(t, k, src, dst):
+        peer = T.cores[(rank + 1 + t % (n - 1)) % n]
+        back = T.cores[(rank - 1 - t % (n - 1)) % n]
+        eng = topo.engines(core, peer)[:8]
+        rid, pid, _se = topo.addr(peer)
+        msk = sum(1 << e for e in eng)
+        nsent[0] += len(eng)
+        s = "a%d" % (2 * t + k)
+        i = add("G", [lambda: g.remote_dma(ap(dst), ap(src), T.sem[s], T.sem.sent, pid, rid, msk)], [src], [], 300.0, "r")
+        return add("-", [], [], [dst], 0.0, "a", 2500.0, after=[i], sem=(s, len(topo.engines(back, core)[:8])))
+
+    col = lambda b, j: R(b, j, j + 1)
+    eq, mu_, ad, sb = A_.is_equal, A_.mult, A_.add, A_.subtract
+
+    dma("Y", T.ci[:, :], T.gate[:, :], [], [R("ci")], 2000)
+    dma("Y", T.alti[:, :], T.alt[:, :], [], [R("alti")], 3000)
+    dma("S", T.A[:, :], T.acc0[:, :], [], [R("A")], 2200)
+    dma("S", T.thi[0:8, :], T.th[:, :], [], [R("thi")], 2200)
+    for j in range(4):
+        dma("Y", T.Ii[:, 1024 * j:1024 * j + 1024], T.icol[:, 1024 * j:1024 * j + 1024], [], [R("Ii", 1024 * j, 1024 * j + 1024)], 4500 + 1500 * j)
+    dma("S", T.Pw[:, 0:4096], T.pat[:, :], [], [R("Pw", 0, 4096)], 9000)
+
+    iota(R("pi"), [[0, 1]], 0, 1)
+    iota(R("cc"), [[1, 144]], 0, 0)
+    iota(R("cg"), [[1, 8], [0, 16]], 0, 0)
+    iota(R("c16"), [[0, 8], [1, 16]], 0, 0)
+    mset(R("zero"), 0.0)
+    iota(R("c4"), [[0, 32], [1, 4]], 0, 0)
+    iota(R("c8"), [[0, 16], [1, 8]], 0, 0)
+    for j in range(2):
+        iota(R("iot", 1024 * j, 1024 * j + 1024), [[1, 1024]], 1024 * j, 0)
+        act(R("iot", 2048 + 1024 * j, 3072 + 1024 * j), R("iot", 1024 * j, 1024 * j + 1024), bias=2048.0)
+    sh, an = A_.logical_shift_right, A_.bitwise_and
+    for j, (s, m) in enumerate([(0, 15), (4, 7), (0, 127), (0, 3), (2, 3), (1, 7), (3, 1), (0, 1)]):
+        ts(col("pt", j), R("pi"), s, sh, m, an)
+    cp(R("pc", 0, 7), R("pt", 0, 7))
+    ts(col("pc", 7), col("pt", 1), 16.0, mu_, 15.0, ad)
+    ts(col("pc", 9), col("pt", 0), -BK, mu_, 15 * BK + 1, ad)
+    ts(col("pc", 10), col("pt", 0), -BK, mu_, 15 * BK + 2048, ad)
+    ts(col("pc", 11), col("pt", 4), -BK, mu_, 3 * BK + 2048, ad)
+    ts(col("pc", 12), col("pt", 0), 1.0, ad)
+    ts(col("pc", 13), col("pt", 7), -2.0, mu_, 1.0, ad)
+    ts(col("pt", 7), R("pi"), 3, sh)
+    cp(col("pc", 8), col("pt", 7))
+    P = lambda j: col("pc", j)
+    c128 = R("cc", 0, 128); c16 = R("c16", 0, 128)
+    ts(R("BO"), R("cg"), P(1), eq)
+    ts(R("id4"), R("cc", 0, 4), P(3), eq)
+    for k in range(4):
+        ts(col("x", k), P(4), float(k), eq)
+        act(R("SelK", 128 * k, 128 * k + 128), R("BO"), scale=col("x", k))
+    ts(R("tmp"), R("c4"), P(4), eq)
+    tt(R("Rep"), R("tmp"), R("BO"), mu_)
+    ts(R("s16", 0, 128), c16, P(0), eq, HUGE, mu_)
+    act(R("mT"), R("s16", 0, 128), scale=1.0 / HUGE)
+    for j in (3, 2, 1, 0):
+        act(R("s16", 128 * j, 128 * j + 128), R("s16", 0, 128), bias=-BK)
+    act(R("s4"), R("tmp"), bias=-BK, scale=HUGE)
+    ts(R("Z1"), R("cc"), P(7), eq)
+    for nm, w in (("Z2", 2.0), ("Zm", -1.0), ("Zh", P(12)), ("Zf", P(12))):
+        act(R(nm), R("Z1"), scale=w)
+    z128 = R("zero", 0, 128)
+    for nm, w in (("idb", 1.0), ("nid", -1.0), ("bid", -BIG)):
+        sel(R(nm), z128, [[-1, 128]], w, 0, 1)
+    ts(R("BOf"), R("cg"), P(2), eq)
+    ts(R("QS"), R("cc", 0, 8), P(1), eq)
+    for nm, w in (("B16", 16.0), ("B32", 32.0), ("B16n", -16.0)):
+        act(R(nm), R("QS"), scale=w)
+    iota(R("ones"), [[0, 128]], 1, 0); iota(R("one8"), [[0, 8]], 1, 0)
+    iota(R("Iw", 4096, 4224), [[0, 128]], 0, 0)
+    mset(col("alph", 0), 1.0); mset(col("alph", 1), 0.4995)
+    act(R("mTK"), R("mT"), scale=K0 + FALL - 4096.0)
+    act(R("idf"), R("idb")); act(R("nif"), R("nid"))
+    iota(R("iox", 0, 1024), [[2, 512], [-1, 2]], 1, 0)
+    for j in range(1, 4):
+        act(R("iox", 1024 * j, 1024 * j + 1024), R("iox", 0, 1024), bias=1024.0 * j)
+    ts(R("x", 16, 32), R("cc", 0, 16), P(0), A_.is_gt)
+    ts(R("x", 32, 48), R("cc", 0, 16), P(0), eq)
+    tt(R("x", 16, 32), R("x", 16, 32), R("x", 32, 48), sb)
+    for h in range(4):
+        acts([(R("Lt", 128 * r, 128 * r + 128), R("BO"), AF.Identity, 0.0, col("x", 16 + r)) for r in range(4 * h, 4 * h + 4)])
+    ts(R("tm2"), c16, P(0), A_.is_le)
+    tt(R("LmB"), R("tm2"), R("BO"), mu_)
+    ts(R("tm2"), R("c8"), P(5), eq)
+    tt(R("tm2"), R("tm2"), R("BO"), mu_)
+    act(R("Lsig"), R("tm2"), scale=-1.0)
+    act(R("Ldel"), R("tm2"), scale=P(13))
+    pq = [[-16, 8], [-8, 2], [0, 8]]
+    for j in range(8):
+        sel(R("LF", 128 * j, 128 * j + 128), z128, pq, 2.0, -j, 1)
+    ts(R("RE"), R("cc", 0, 16), P(8), eq)
+    ts(R("EXPL"), R("cc", 0, 8), 16.0, mu_, 15.0, ad)
+    for nm, a, b in (("dmin", -4096, HUGE), ("dmax", 1, -HUGE)):
+        iota(R(nm), [[0, 128]], a, 0)
+        sel(R(nm), R(nm), [[0, 8], [1, 16]], b, 0, 0)
+    iota(R("k15"), [[0, 8], [-1, 16]], 15, 0)
+    ts(R("ltile"), R("cc", 0, 8), 16.0, mu_, P(0), ad)
+    ts(R("dump"), R("ltile"), 4096.0, ad)
+    cp(R("thf", p1=8), R("thi", p1=8))
+    mms(grp(R("pH", 0, 4), [(R("BOf", p1=8), R("thf", p1=8))]))
+    cp(R("thc"), R("pH", 0, 4))
+    ts(R("altw"), R("alti"), -2048.0, ad)
+    for j in range(4):
+        cp(R("Iw", 1024 * j, 1024 * j + 1024), R("Ii", 1024 * j, 1024 * j + 1024))
+    Iw = R("Iw", 0, 4096); Pw = R("Pw", 0, 4096)
+
+    cu = lambda t: R("msg1", 16 * t + 8, 16 * t + 16)
+
+    def prep(t):
+        cp(cu(t), R("ci"))
+        act(R("cR"), ind(R("iot"), cu(t)))
+        if t == RO:
+            return
+        cp(R("cf"), R("ci"))
+        ts(R("w1"), R("ci"), 1023, an); ts(R("w2"), R("ci"), 10, sh)
+        cp(R("lou"), R("w1")); cp(R("hiu"), R("w2"))
+        act(R("mj"), ind(R("id4"), R("hiu")))
+        tt(R("Ogm"), ind(R("altw"), R("lou")), R("mj"), mu_)
+        mms(grp(R("pB", 0, NS), [(R("Rep"), R("Ogm", NV, 128))]))
+        mms([x for k in range(4) for x in grp(R("pA", 128 * k, 128 * k + 128), [(R("SelK", 128 * k, 128 * k + 128), R("Ogm"))])])
+        scan(R("sc4", 0, NS), R("s4", 0, NS), R("pB", 0, NS), ad, A_.min)
+        ts(R("OSu", 0, NS // 4), R("sc4", 3, NS, 4), P(11), ad)
+        scan(R("sc"), R("s16"), R("pA"), ad, A_.min)
+        ts(R("OLu"), R("sc", 15, 512, 16), P(10), ad)
+        ts(R("OL"), R("sc", 15, 512, 16), P(10), ad, FALL, ad)
+        na = NA if t else 0
+        for p in range(na):
+            sel(R("A16", p, 16 * NV, 16), R("A", 0, NV), [[0, NV]], 0.0, 1, 0)
+        if na < 16:
+            acts([(R("A16", p, 16 * NV, 16), R("A", 0, NV), AF.Identity, 0.0, 1.0) for p in range(na, 16)])
+
+    def farthest(lst, split, bank):
+        cp(R("C2u"), ind(Iw, lst))
+        act(R("Xc"), ind(Pw, lst))
+        act(R("old"), ind(Iw, lst))
+        cuts = [0, NG, 128] if split else [0, 32, 64, 96, 128]
+        for h in range(len(cuts) - 1):
+            o, w = R("G2", 16 * cuts[h], 16 * cuts[h + 1]), ind(Pw, R("C2u", cuts[h], cuts[h + 1]))
+            if split and h == 0:
+                cp(o, w)
+            else:
+                act(o, w)
+
+        def rest():
+            for b in range(4 if split else 0):
+                pb = "p" + "CDEF"[b]
+                mms([(R(pb, 128 * j, 128 * j + 128), R("nid"), R("Xc"), j == 0, False) for j in range(4)])
+            for b in (0, 2, 1, 3):
+                pb = "p" + "CDEF"[b]
+                if split:
+                    mms([(R(pb, 128 * j, 128 * j + 128), R("idb"), R("G2", 4 * b + j, 2048, 16), False, j == 3) for j in range(4)])
+                else:
+                    for j in range(4):
+                        mms(grp(R(pb, 128 * j, 128 * j + 128), [(R("nid"), R("Xc")), (R("idb"), R("G2", 4 * b + j, 2048, 16))]))
+                if split and b >= NB:
+                    ts(R("ab", 512 * b, 512 * b + 512), R(pb), 0.0, A_.max)
+                else:
+                    act(R("ab", 512 * b, 512 * b + 512), R(pb), AF.Abs)
+            lin = range(4 * NB, 16) if split else []
+            if lin:
+                mms([(R("pG", p, 128, 16), R("Xc"), R("B16"), p == lin[0], False) for p in lin])
+                mms([(R("pG", p, 128, 16), R("G2", p, 2048, 16), R("B16n"), False, False) for p in lin])
+            for b in (0, 2, 1, 3):
+                mms([(R("pG", p, 128, 16), R("ab", 128 * p, 128 * p + 128), R("B32" if p in lin else "B16"), p == 0 and not lin, p == 15)
+                     for p in range(4 * b, 4 * b + 4)])
+            tt(R("key"), R("pG", 0, 128), R("k15"), ad)
+            scan(R("sk"), R("dmax"), R("pG", 0, 128), ad, A_.max)
+            tt(R("oh"), ind(R("sk"), R("EXPL")), R("key"), eq)
+            mms(grp(bank, [(R("oh"), R("idb"))]))
+        return rest
+
+    def differ(val, pd):
+        mms(grp(pd, [(R("nif"), R("old")), (R("idf"), val)]))
+        act(R("dif"), pd)
+
+    def write(bank, val, tgt, pd):
+        tt(R("tt"), bank, R("dif"), mu_)
+        tt(ind(R("Iw"), tgt), R("tt"), R("old"), ad)
+
+    def lowest(valR, valL, use, tgtL, out, bank, y0, eb):
+        one = lambda r, q: (r[0], r[1] + q, r[1] + q + 1, 1, 0, 128)
+        for h in range(2):
+            acts([(R(eb, 144 * q, 128 * q + 128), R(valR, 16 * q, 128), AF.Abs, one(valL, q), -1.0) for q in range(h, 8, 2)])
+        for q in range(NE if eb == "Ea" else 0):
+            ts(R(eb, 144 * q, 128 * q + 128), R(eb, 144 * q, 128 * q + 128), one(use, q), A_.is_lt)
+        for q in range(NE if eb == "Ea" else 0, 8, 2):
+            acts([(R(eb, 144 * j, 128 * j + 128), R(eb, 144 * j, 128 * j + 128), AF.Relu, one(use, j), -1.0) for j in (q, q + 1)])
+        mms([(R(bank, 128, 256), R("idb"), R("zero", 0, 128), True, False)])
+        for q in range(7):
+            mms([(R(bank, 144 + 16 * q, 256), R("BO"), R(eb, 144 * q + 16, 128 * q + 128), False, False)])
+        mms([(R(bank, 128 + r, 256, 16), R("Lt", 128 * r, 128 * r + 128), R(eb, r, 1024, 144), False, r == 15) for r in range(16)])
+        scan(R("sc4"), R("s16", 0, 128), R(bank, 128, 256), ad, A_.min)
+        ts(R("y", y0, y0 + 8), R("sc4", 15, 128, 16), P(9), ad, 8192.0, mu_)
+        tt(R("y", y0, y0 + 8), R("y", y0, y0 + 8), tgtL, ad)
+        tt(R("y", y0, y0 + 8), R("y", y0, y0 + 8), R("dump"), A_.min)
+        cp(out, R("y", y0, y0 + 8))
+
+    prep(0)
+    for t in range(RO):
+        now[0] = t; seen.clear()
+        chain([cp(R("CuS"), ind(Iw, R("OSu", 0, NS // 4))), cp(R("Cu"), ind(Iw, R("OLu")))])
+        rest2 = farthest(cu(t), False, R("pG", 384, 512))
+        if not LATE:
+            rest2()
+        ch = []
+        for l0 in range(0, NS, 16):
+            l1 = min(NS, l0 + 16)
+            for la in range(l0, l1, 4):
+                ch.append(acts([(R("GS", 64 * i, 64 * i + 64), ind(Pw, R("CuS", 4 * i, 4 * i + 4)), AF.Abs, col("A", NV + i), -1.0) for i in range(la, la + 4)]))
+            mms(grp(R("pB", 4 * l0, 4 * l1), [(R("Z1", 15 - p, 143 - p), R("GS", 64 * l0 + p, 64 * l1, 16)) for p in range(16)]))
+        chain(ch)
+        W = 16 * NV
+        ch = []
+        for k in range(4):
+            ch.append(tt(R("D", W * k, W * k + W), ind(Pw, R("Cu", 128 * k, 128 * k + NV)), R("A16"), sb))
+            chain(ch[-2:])
+            ts(R("Rl", W * k, W * k + W), R("D", W * k, W * k + W), 0.0, A_.max)
+            o = R("pA" if k % 2 else "pG", NV * k, NV * k + NV)
+            mms([(o, R("Zm", 15 - p, 143 - p), R("D", W * k + p, W * k + W, 16), p == 0, False) for p in range(16)])
+            mms([(o, R("Z2", 15 - p, 143 - p), R("Rl", W * k + p, W * k + W, 16), False, p == 15) for p in range(16)])
+            ts(R("near", 128 * k, 128 * k + NV), o, col("thc", t), A_.is_le)
+        if t == 0:
+            for j in range(4):
+                act(R("Pw", 4096 + 1024 * j, 5120 + 1024 * j), R("Pw", 1024 * j, 1024 * j + 1024), scale=-1.0)
+        ts(R("Ch"), R("Cu", 128, 512), -2048.0, ad)
+        cp(R("Cw", 0, 128), R("Cu", 0, 128)); cp(R("Cw", 128, 512), R("Cu", 0, 384))
+        mms(grp(R("pC", 0, 384), [(R("Ldel"), R("Ch"))]))
+        act(R("pF", 0, 384), R("pC", 0, 384), AF.Abs)
+        for k in range(4):
+            ts(R("near", 128 * k + NV, 128 * k + 128), R("pB", k, 4 * NS, 4), col("thc", t), A_.is_le)
+        mms(grp(R("pH", 0, 32), [(R("Z1", 15 - r, 143 - r), R("near", r, 512, 16)) for r in range(16)]))
+        ts(R("x", 0, 8), R("pH", 0, 8), 9.0, A_.is_lt, 256.0, mu_)
+        ts(R("x", 8, 16), R("pH", 8, 16), 9.0, A_.is_lt, 128.0, mu_)
+        ts(R("sv", 0, 32), R("pH", 0, 32), 9.0, A_.is_ge)
+        tt(R("x", 16, 24), R("x", 0, 8), R("x", 8, 16), ad)
+        tt(R("x", 24, 32), R("x", 16, 24), R("ltile"), ad)
+        cp(R("idx"), R("x", 24, 32))
+        ts(R("Fh"), ind(R("Cw"), R("idx")), -2048.0, ad)
+        mms([x for k in range(3) for x in grp(R("pA", 128 * k, 128 * k + 128), [(R("near", 128 * k + 128, 128 * k + 256), R("BO"))])])
+        act(R("svX"), R("pA", 0, 384), AF.Sign, -8.5)
+        tt(R("sv", 32, 64), R("sv", 0, 32), R("OL"), mu_)
+        tt(R("x", 48, 64), R("sv", 32, 48), R("sv", 48, 64), ad); tt(R("y", 8, 16), R("x", 48, 56), R("x", 56, 64), ad)
+        act(R("y", 88, 96), R("OL", 24, 32), bias=-4096.0)
+        act(R("y", 96, 104), R("OL", 24, 32), bias=FALL - 4096.0)
+        act(R("y", 32, 40), R("OL", 0, 8), bias=4096.0 - FALL)
+        tt(R("y", 16, 24), R("y", 8, 16), R("y", 96, 104), A_.min)
+        tt(R("y", 16, 24), R("y", 16, 24), R("y", 88, 96), A_.max)
+        ts(R("y", 24, 32), R("y", 8, 16), 1.0, A_.min, 2 * FALL - 4096.0, mu_)
+        for j in range(3):
+            mms([(R("p" + "CDE"[j], 0, 384), R("Lsig"), R("Ch"), True, False)])
+        for j in range(8):
+            pb = "p" + "CDE"[j % 3]; h = 384 * (j % 4)
+            if j >= 3:
+                mms([(R(pb, 0, 384), R("Lsig"), R("Ch"), True, False)])
+            mms([(R(pb, 128 * k, 128 * k + 128), R("LF", 128 * j, 128 * j + 128), R("Fh"), False, k == 2) for k in range(3)])
+            act(R("Xab", h, h + 384), R(pb, 0, 384), AF.Abs)
+            tt(R("E", h, h + 384), R("Xab", h, h + 384), R("pF", 0, 384), eq)
+            mms([x for k in range(3) for x in grp(R("pG", 128 * k + j, 128 * k + 128, 8), [(R("E", h + 128 * k, h + 128 * k + 128), R("RE"))])])
+        mms([(R("pB", 256, 264), R("mTK"), R("QS"), True, False)])
+        tt(R("z"), R("pG", 0, 384), R("svX"), A_.is_ge)
+        mms(grp(R("pH", 128, 256), [(R("Fh"), R("idb"))] + [(R("bid"), R("z", 128 * k, 128 * k + 128)) for k in range(3)]))
+        scan(R("sk"), R("dmin"), R("pH", 128, 256), ad, A_.min)
+        tt(R("lT"), ind(R("sk"), R("EXPL")), R("mT"), mu_)
+        mms([(R("pB", 256, 264), R("lT"), R("QS"), False, True)])
+        tt(R("mk"), R("pB", 256, 264), R("y", 16, 24), A_.min)
+        ts(R("w1"), R("mk"), 4094, an); ts(R("w2"), R("mk"), 1, an)
+        tt(R("w3"), R("w1"), R("w2"), sb)
+        a_l = R("msg1", 16 * t, 16 * t + 8)
+        ts(a_l, R("w3"), 1.0, ad)
+        send(t, 0, R("msg1", 16 * t, 16 * t + 16), R("land1", 16 * t, 16 * t + 16))
+        ts(R("mi"), R("mk"), 4095, an)
+        tt(R("lrn"), R("mk"), R("y", 24, 32), A_.is_lt)
+        act(R("mR"), ind(R("iox"), a_l))
+        mms(grp(R("pH", 40, 48), [(R("LmB"), R("lrn"))]) + grp(R("pH", 48, 56), [(R("BO"), R("lrn"))]) + grp(R("pH", 56, 64), [(R("ones"), R("lrn"))]))
+        scan(R("y", 40, 48), R("one8"), R("pH", 48, 56), mu_, sb, 64.0)
+        add("V", [lambda: g.vector.tensor_reduce(ap(R("ecol")), ap(R("pH", 56, 64)), AxisListType.X, ad)], [R("pH", 56, 64)], [R("ecol")], 67.0)
+        tt(R("y", 40, 48), R("y", 40, 48), R("pH", 40, 48), ad)
+        tt(R("y", 40, 48), R("y", 40, 48), R("lrn"), A_.min)
+        if LATE:
+            rest2()
+        differ(R("mR"), R("pB", 384, 512))
+        lowest("cR", R("cf"), R("lrn"), R("cf"), R("tg2"), "pB", 48, "Ea")
+        write(R("pG", 384, 512), R("mR"), R("tg2"), R("pB", 384, 512))
+        ts(R("y", 80, 88), R("w3"), 1.0, ad)
+        cp(R("vs"), R("mi"))
+        lowest("mR", R("vs"), R("y", 40, 48), R("y", 80, 88), R("msg2", 8 * t, 8 * t + 8), "pA", 64, "Eb")
+        send(t, 1, R("msg2", 8 * t, 8 * t + 8), R("land2", 8 * t, 8 * t + 8))
+        rest3 = farthest(R("land1", 16 * t, 16 * t + 8), True, R("pH", 0, 128))
+        act(R("bR"), ind(R("iox"), R("land1", 16 * t + 8, 16 * t + 16)))
+        tt(R("y", 0, 8), R("mi"), R("y", 32, 40), sb)
+        tt(R("y", 0, 8), R("y", 0, 8), R("lrn"), mu_)
+        tt(R("y", 0, 8), R("y", 0, 8), R("y", 32, 40), ad)
+        cp(R("selu"), R("y", 0, 8)); ts(R("lru"), R("lrn"), 1.0, mu_)
+        act(R("aR"), ind(R("alph"), R("lru")))
+        tt(R("u"), ind(R("Pw"), R("selu")), R("A"), ad)
+        act(R("au"), R("u"), AF.Abs)
+        tt(R("v"), R("au"), R("aR"), mu_)
+        act(R("v"), R("v"), bias=MAGIC)
+        if t == RO - 1:
+            act(R("Af"), R("v"), bias=-MAGIC)
+            dma("Y", T.ya[:, :], T.Af[:, :], [R("Af")], [], 2000)
+        else:
+            act(R("A"), R("v"), bias=-MAGIC)
+        tt(R("w1"), R("mi"), R("cf"), mu_)
+        ts(R("y", 8, 16), R("cf"), 37.0, mu_, R("ecol"), ad)
+        ts(R("w2"), R("w1"), 4, sh)
+        tt(R("w1"), R("w2"), R("y", 8, 16), ad)
+        ts(R("ci"), R("w1"), 4095, an)
+        prep(t + 1)
+        differ(R("bR"), R("pH", 384, 512))
+        rest3()
+        write(R("pH", 0, 128), R("bR"), R("land2", 8 * t, 8 * t + 8), R("pH", 384, 512))
+    dma("Y", T.yg[:, :], T.cR[0:128:16, :], [R("cR")], [], 2000)
+    for j in list(range(N16, 16)) + list(range(N16)):
+        o = R("pA", 0, 256)
+        if j < N16:
+            ts(R("Ih", 256 * j, 256 * j + 256), R("Iw", 256 * j, 256 * j + 256), -2048.0, ad)
+            mms([(o, R("Zh", 15 - j, 143 - j), R("Ih", 256 * j, 256 * j + 256), False, j == N16 - 1)])
+        else:
+            mms([(o, R("Zf", 15 - j, 143 - j), R("Iw", 256 * j, 256 * j + 256), j == N16, False)])
+    ts(col("x", 0), P(0), float(N16), A_.is_lt, 136.0 * 2048, mu_)
+    ts(R("ycs"), R("pA", 0, 256), col("x", 0), ad)
+    dma("Y", T.yc[:, :], T.ycs[:, :], [R("ycs")], [], 2000)
+    return ops, nsent[0]
+
+
+def place(ops, seq, pre, back):
+    st = [0.0] * len(ops)
+    busy = {}
+    for i in seq:
+        o = ops[i]
+        if back:
+            r = max([st[j] + ops[j]["cost"] + h for j, h in pre[i]] + [0.0]) + o["lat"]
+        else:
+            r = max([st[j] + ops[j]["cost"] + ops[j]["lat"] + h for j, h in pre[i]] + [0.0])
+        if o["eng"] != "-":
+            a, b = busy.setdefault(o["eng"], ([], []))
+            lo, hi = 0, len(b)
+            while lo < hi:
+                m = (lo + hi) // 2
+                if b[m] <= r:
+                    lo = m + 1
+                else:
+                    hi = m
+            while lo < len(a) and a[lo] < r + o["cost"]:
+                r = max(r, b[lo]); lo += 1
+            a.insert(lo, r); b.insert(lo, r + o["cost"])
+        st[i] = r
+    return st
+
+
+def schedule(ops):
+    if "order" in REPORT:
+        return REPORT["order"]
+    n = len(ops)
+    pre = [[] for _ in ops]; suc = [[] for _ in ops]
+    for i, o in enumerate(ops):
+        near = [(j, HOP) for j in o["hard"]] + [(j, 0.0) for j in o["soft"]]
+        pre[i] = near
+        for j, h in near:
+            suc[j].append((i, h))
+    state = [SEED * 2654435761 % (1 << 31) + 1]
+
+    def rand():
+        state[0] = state[0] * 48271 % 2147483647
+        return state[0] / 2147483647.0
+    best = None
+    seq = list(range(n))
+    for it in range(PASSES):
+        st = place(ops, seq, pre, False)
+        end = max(st[i] + ops[i]["cost"] + ops[i]["lat"] for i in range(n))
+        if best is None or end < best[1]:
+            best = (st, end)
+        elif it % 2 == 0:
+            st = best[0]
+        fin = [st[i] + ops[i]["cost"] + ops[i]["lat"] for i in range(n)]
+        c, w, a = rand() * best[1], 3000 + 12000 * rand(), NOISE * rand() * (it % 2 == 0)
+        bt = place(ops, topo_order(n, suc, pre, [-f + (a * rand() if abs(f - c) < w else 0.0) for f in fin]), suc, True)
+        seq = topo_order(n, pre, suc, [-(bt[i] + ops[i]["cost"]) + (a * rand() if abs(fin[i] - c) < w else 0.0) for i in range(n)])
+    st, end = best
+    cur = best
+    dur = [o["cost"] + o["lat"] for o in ops]
+    arcs = None
+    for it in range(MOVES):
+        s = cur[0]
+        if arcs is None:
+            ends = {(o["eng"], round(s[i] + o["cost"], 3)): i for i, o in enumerate(ops) if o["eng"] != "-"}
+            arcs, todo, met = [], [max(range(n), key=lambda i: s[i] + dur[i])], set()
+            while todo:
+                b = todo.pop()
+                if b in met:
+                    continue
+                met.add(b)
+                bind = [j for j, h in pre[b] if abs(s[j] + dur[j] + h - s[b]) < 0.01]
+                a = ends.get((ops[b]["eng"], round(s[b], 3)))
+                if not bind and a is not None:
+                    arcs.append((a, b)); bind = [a]
+                todo += bind
+        if not arcs:
+            break
+        key = list(s)
+        a, b = arcs[int(rand() * len(arcs))]
+        if rand() < 0.5:
+            key[a] = s[b] + 1.0 + (rand() < 0.5) * 3000.0 * rand()
+        else:
+            todo, lim = [b], s[a] - 1.0 - (rand() < 0.5) * 3000.0 * rand()
+            while todo:
+                k = todo.pop()
+                if key[k] > lim:
+                    key[k] = lim - 1e-3 * (n - k) / n
+                    todo += [j for j, _h in pre[k]]
+        s2 = place(ops, topo_order(n, pre, suc, key), pre, False)
+        e2 = max(s2[i] + dur[i] for i in range(n))
+        if e2 <= cur[1] + HEAT * (1.0 - it / MOVES) * rand():
+            cur, arcs = (s2, e2), None
+            if e2 < end:
+                st, end = cur
+    REPORT["order"] = (topo_order(n, pre, suc, st), end, st)
+    return REPORT["order"]
+
+
+def topo_order(n, pre, suc, key):
+    left = [len(p) for p in pre]
+    out, seen = [], [False] * n
+    for i in sorted(range(n), key=lambda x: key[x]):
+        seen[i] = True
+        if left[i] == 0:
+            todo = [i]
+            while todo:
+                k = todo.pop()
+                out.append(k)
+                for j, _h in suc[k]:
+                    left[j] -= 1
+                    if left[j] == 0 and seen[j]:
+                        todo.append(j)
+    return out
+
+
+def rank_program(g, core, T, topo):
+    if T.rank_of(core) is None:
+        return
+    ops, nsent = build(g, core, T, topo)
+    order, end, st = schedule(ops)
+    for i, o in enumerate(ops):
+        o["t"] = st[i]
+    REPORT["ops"] = ops; REPORT["end"] = end
+    q = {"V": g.vector, "S": g.scalar, "P": g.tensor, "G": g, "Y": g.sync}
+    cnt = {e: 0 for e in CNT}
+    known = {e: {} for e in q}
+    mark = {}
+    for i in order:
+        o = ops[i]; e = o["eng"]
+        if o["kind"] == "a":
+            mark[i] = (o["sem"][0], o["sem"][1], {})
+            continue
+        kn = known[e]
+        need = {}
+        for j in o["hard"]:
+            if ops[j]["kind"] == "r":
+                continue
+            s, v, _k = mark[j]
+            if kn.get(s, 0) < v and need.get(s, (0, None))[0] < v:
+                need[s] = (v, j)
+        for s, (v, j) in sorted(need.items(), key=lambda x: -ops[x[1][1]]["t"]):
+            if kn.get(s, 0) >= v:
+                continue
+            q[e].wait_ge(T.sem[s], v)
+            kn[s] = v
+            for s2, v2 in mark[j][2].items():
+                kn[s2] = max(kn.get(s2, 0), v2)
+        if o["kind"] == "c":
+            for f in o["fns"]:
+                f().then_inc(T.sem[CNT[e]], 1)
+                cnt[e] += 1
+            mark[i] = (CNT[e], cnt[e], dict(kn))
+        elif o["kind"] == "d":
+            o["fns"][0]().then_inc(T.sem[o["sem"]], 16)
+            mark[i] = (o["sem"], 16, dict(kn))
+        else:
+            o["fns"][0]()
+    for e in CNT:
+        g.wait_ge(T.sem[CNT[e]], cnt[e])
+    for o in ops:
+        if o["kind"] == "d":
+            g.wait_ge(T.sem[o["sem"]], 16)
+        elif o["kind"] == "a":
+            g.wait_ge(T.sem[o["sem"][0]], o["sem"][1])
+    g.wait_ge(T.sem.sent, nsent)

@@ -1,12 +1,14 @@
 from concourse.mybir import AluOpType, AxisListType, ActivationFunctionType
 
 RO = 4
-NV = 68
+NV = 72
 NS = 128 - NV
 NG = 60
 NB = 2
 NA = 8
 NE = 4
+NF = 4
+NB2 = 4
 LATE = True
 N16 = 13
 HUGE = float(1 << 26)
@@ -29,7 +31,7 @@ _S = {
     "ci": (8, I32), "cf": (8, F), "cu": (8, U), "lou": (8, U), "hiu": (8, U), "w1": (8, I32), "w2": (8, I32), "w3": (8, I32),
     "A": (128, B), "nA": (128, B), "A16": (16 * NV, B), "Af": (128, F), "cR": (128, F), "mR": (128, F), "bR": (128, F),
     "mj": (128, B), "Ogm": (128, H), "sc": (512, F), "sc4": (128, F), "OL": (32, F), "OLu": (32, U), "OSu": (32, U),
-    "Cu": (512, U), "CuS": (4 * NS, U), "Cw": (512, F), "Ch": (384, H), "D": (64 * NV, B), "Rl": (64 * NV, B), "GS": (64 * NS, B),
+    "Cu": (512, U), "CuS": (4 * NS, U), "Cw": (384, F), "Ch": (384, H), "D": (64 * NV, B), "Rl": (64 * NV, B), "GS": (64 * NS, B),
     "near": (512, B), "x": (64, F), "idx": (8, U), "Fh": (128, H), "Xab": (1536, F), "E": (1536, B), "svX": (384, B), "z": (384, B),
     "sk": (128, F), "lT": (128, F), "sv": (64, F), "y": (104, F), "mk": (8, I32), "mi": (8, I32), "lrn": (8, B), "v": (128, F),
     "mu": (8, U), "selu": (8, U), "lru": (8, U), "ecol": (1, F), "vs": (8, F), "Ea": (1024, B), "Eb": (1024, B), "Lt": (2048, B), "iox": (4096, F), "mTK": (128, F), "idf": (128, F), "nif": (128, F), "tg2": (8, U),
@@ -51,11 +53,16 @@ NDMA = 14
 SEMAPHORES = ["cV", "cS", "cP", "cG", "sent"] + ["d%d" % i for i in range(NDMA)] + ["a%d" % i for i in range(2 * RO)]
 CNT = {"V": "cV", "S": "cS", "P": "cP", "G": "cG"}
 CY, GA, SCA, PE, HOP = 1.04, 1.62, 3.95, 0.52, 110.0
+LAT1 = 2500.0
+LAT2 = 4500.0
+SWEEPS = 4
+WIDE = 14000.0
+TRIES = 300
 SEED = 1
-PASSES = 400
-MOVES = 1200
-HEAT = 50.0
-NOISE = 2500.0
+PASSES = 30
+MOVES = 0
+HEAT = 0.0
+NOISE = 3000.0
 REPORT = {}
 
 
@@ -208,7 +215,7 @@ def build(g, core, T, topo):
         nsent[0] += len(eng)
         s = "a%d" % (2 * t + k)
         i = add("G", [lambda: g.remote_dma(ap(dst), ap(src), T.sem[s], T.sem.sent, pid, rid, msk)], [src], [], 300.0, "r")
-        return add("-", [], [], [dst], 0.0, "a", 2500.0, after=[i], sem=(s, len(topo.engines(back, core)[:8])))
+        return add("-", [], [], [dst], 0.0, "a", (LAT1, LAT2)[k], after=[i], sem=(s, len(topo.engines(back, core)[:8])))
 
     col = lambda b, j: R(b, j, j + 1)
     eq, mu_, ad, sb = A_.is_equal, A_.mult, A_.add, A_.subtract
@@ -218,8 +225,9 @@ def build(g, core, T, topo):
     dma("S", T.A[:, :], T.acc0[:, :], [], [R("A")], 2200)
     dma("S", T.thi[0:8, :], T.th[:, :], [], [R("thi")], 2200)
     for j in range(4):
-        dma("Y", T.Ii[:, 1024 * j:1024 * j + 1024], T.icol[:, 1024 * j:1024 * j + 1024], [], [R("Ii", 1024 * j, 1024 * j + 1024)], 4500 + 1500 * j)
-    dma("S", T.Pw[:, 0:4096], T.pat[:, :], [], [R("Pw", 0, 4096)], 9000)
+        dma("Y", T.Ii[:, 1024 * j:1024 * j + 1024], T.icol[:, 1024 * j:1024 * j + 1024], [], [R("Ii", 1024 * j, 1024 * j + 1024)], 4000 + 1100 * j)
+    dma("Y", T.Pw[:, 0:4096], T.pat[:, :], [], [R("Pw", 0, 4096)], 9000)
+    chain([i for i, o in enumerate(ops) if o["eng"] == "Y"])
 
     iota(R("pi"), [[0, 1]], 0, 1)
     iota(R("cc"), [[1, 144]], 0, 0)
@@ -228,9 +236,9 @@ def build(g, core, T, topo):
     mset(R("zero"), 0.0)
     iota(R("c4"), [[0, 32], [1, 4]], 0, 0)
     iota(R("c8"), [[0, 16], [1, 8]], 0, 0)
-    for j in range(2):
+    for j in range(3):
         iota(R("iot", 1024 * j, 1024 * j + 1024), [[1, 1024]], 1024 * j, 0)
-        act(R("iot", 2048 + 1024 * j, 3072 + 1024 * j), R("iot", 1024 * j, 1024 * j + 1024), bias=2048.0)
+    act(R("iot", 3072, 4096), R("iot", 0, 1024), bias=3072.0)
     sh, an = A_.logical_shift_right, A_.bitwise_and
     for j, (s, m) in enumerate([(0, 15), (4, 7), (0, 127), (0, 3), (2, 3), (1, 7), (3, 1), (0, 1)]):
         ts(col("pt", j), R("pi"), s, sh, m, an)
@@ -272,9 +280,8 @@ def build(g, core, T, topo):
     mset(col("alph", 0), 1.0); mset(col("alph", 1), 0.4995)
     act(R("mTK"), R("mT"), scale=K0 + FALL - 4096.0)
     act(R("idf"), R("idb")); act(R("nif"), R("nid"))
-    iota(R("iox", 0, 1024), [[2, 512], [-1, 2]], 1, 0)
-    for j in range(1, 4):
-        act(R("iox", 1024 * j, 1024 * j + 1024), R("iox", 0, 1024), bias=1024.0 * j)
+    for j in range(4):
+        iota(R("iox", 1024 * j, 1024 * j + 1024), [[2, 512], [-1, 2]], 1024 * j + 1, 0)
     ts(R("x", 16, 32), R("cc", 0, 16), P(0), A_.is_gt)
     ts(R("x", 32, 48), R("cc", 0, 16), P(0), eq)
     tt(R("x", 16, 32), R("x", 16, 32), R("x", 32, 48), sb)
@@ -301,8 +308,7 @@ def build(g, core, T, topo):
     mms(grp(R("pH", 0, 4), [(R("BOf", p1=8), R("thf", p1=8))]))
     cp(R("thc"), R("pH", 0, 4))
     ts(R("altw"), R("alti"), -2048.0, ad)
-    for j in range(4):
-        cp(R("Iw", 1024 * j, 1024 * j + 1024), R("Ii", 1024 * j, 1024 * j + 1024))
+    conv = [cp(R("Iw", 512 * j, 512 * j + 512), R("Ii", 512 * j, 512 * j + 512)) for j in range(8)]
     Iw = R("Iw", 0, 4096); Pw = R("Pw", 0, 4096)
 
     cu = lambda t: R("msg1", 16 * t + 8, 16 * t + 16)
@@ -353,11 +359,11 @@ def build(g, core, T, topo):
                 else:
                     for j in range(4):
                         mms(grp(R(pb, 128 * j, 128 * j + 128), [(R("nid"), R("Xc")), (R("idb"), R("G2", 4 * b + j, 2048, 16))]))
-                if split and b >= NB:
+                if b >= (NB if split else NB2):
                     ts(R("ab", 512 * b, 512 * b + 512), R(pb), 0.0, A_.max)
                 else:
                     act(R("ab", 512 * b, 512 * b + 512), R(pb), AF.Abs)
-            lin = range(4 * NB, 16) if split else []
+            lin = range(4 * (NB if split else NB2), 16)
             if lin:
                 mms([(R("pG", p, 128, 16), R("Xc"), R("B16"), p == lin[0], False) for p in lin])
                 mms([(R("pG", p, 128, 16), R("G2", p, 2048, 16), R("B16n"), False, False) for p in lin])
@@ -371,7 +377,8 @@ def build(g, core, T, topo):
         return rest
 
     def differ(val, pd):
-        mms(grp(pd, [(R("nif"), R("old")), (R("idf"), val)]))
+        mms([(pd, R("idf"), val, True, False)])
+        mms([(pd, R("nif"), R("old"), False, True)])
         act(R("dif"), pd)
 
     def write(bank, val, tgt, pd):
@@ -382,9 +389,9 @@ def build(g, core, T, topo):
         one = lambda r, q: (r[0], r[1] + q, r[1] + q + 1, 1, 0, 128)
         for h in range(2):
             acts([(R(eb, 144 * q, 128 * q + 128), R(valR, 16 * q, 128), AF.Abs, one(valL, q), -1.0) for q in range(h, 8, 2)])
-        for q in range(NE if eb == "Ea" else 0):
+        for q in range(NE if eb == "Ea" else NF):
             ts(R(eb, 144 * q, 128 * q + 128), R(eb, 144 * q, 128 * q + 128), one(use, q), A_.is_lt)
-        for q in range(NE if eb == "Ea" else 0, 8, 2):
+        for q in range(NE if eb == "Ea" else NF, 8, 2):
             acts([(R(eb, 144 * j, 128 * j + 128), R(eb, 144 * j, 128 * j + 128), AF.Relu, one(use, j), -1.0) for j in (q, q + 1)])
         mms([(R(bank, 128, 256), R("idb"), R("zero", 0, 128), True, False)])
         for q in range(7):
@@ -397,6 +404,9 @@ def build(g, core, T, topo):
         cp(out, R("y", y0, y0 + 8))
 
     prep(0)
+    for i, o in enumerate(ops):
+        if o["w"] in ("OSu", "OLu"):
+            ops[conv[4]]["soft"].add(i)
     for t in range(RO):
         now[0] = t; seen.clear()
         chain([cp(R("CuS"), ind(Iw, R("OSu", 0, NS // 4))), cp(R("Cu"), ind(Iw, R("OLu")))])
@@ -421,19 +431,19 @@ def build(g, core, T, topo):
             mms([(o, R("Z2", 15 - p, 143 - p), R("Rl", W * k + p, W * k + W, 16), False, p == 15) for p in range(16)])
             ts(R("near", 128 * k, 128 * k + NV), o, col("thc", t), A_.is_le)
         if t == 0:
-            for j in range(4):
-                act(R("Pw", 4096 + 1024 * j, 5120 + 1024 * j), R("Pw", 1024 * j, 1024 * j + 1024), scale=-1.0)
+            for j in range(8):
+                ts(R("Pw", 4096 + 512 * j, 4608 + 512 * j), R("Pw", 512 * j, 512 * j + 512), -1.0, mu_)
         ts(R("Ch"), R("Cu", 128, 512), -2048.0, ad)
-        cp(R("Cw", 0, 128), R("Cu", 0, 128)); cp(R("Cw", 128, 512), R("Cu", 0, 384))
+        cp(R("Cw", 0, 384), R("Cu", 0, 384))
         mms(grp(R("pC", 0, 384), [(R("Ldel"), R("Ch"))]))
         act(R("pF", 0, 384), R("pC", 0, 384), AF.Abs)
         for k in range(4):
             ts(R("near", 128 * k + NV, 128 * k + 128), R("pB", k, 4 * NS, 4), col("thc", t), A_.is_le)
         mms(grp(R("pH", 0, 32), [(R("Z1", 15 - r, 143 - r), R("near", r, 512, 16)) for r in range(16)]))
-        ts(R("x", 0, 8), R("pH", 0, 8), 9.0, A_.is_lt, 256.0, mu_)
-        ts(R("x", 8, 16), R("pH", 8, 16), 9.0, A_.is_lt, 128.0, mu_)
+        ts(R("x", 0, 8), R("pH", 0, 8), 9.0, A_.is_lt, 128.0, mu_)
+        ts(R("x", 8, 16), R("pH", 8, 16), 9.0, A_.is_lt, 1.0, ad)
         ts(R("sv", 0, 32), R("pH", 0, 32), 9.0, A_.is_ge)
-        tt(R("x", 16, 24), R("x", 0, 8), R("x", 8, 16), ad)
+        tt(R("x", 16, 24), R("x", 0, 8), R("x", 8, 16), mu_)
         tt(R("x", 24, 32), R("x", 16, 24), R("ltile"), ad)
         cp(R("idx"), R("x", 24, 32))
         ts(R("Fh"), ind(R("Cw"), R("idx")), -2048.0, ad)
@@ -479,7 +489,9 @@ def build(g, core, T, topo):
         tt(R("y", 40, 48), R("y", 40, 48), R("lrn"), A_.min)
         if LATE:
             rest2()
-        differ(R("mR"), R("pB", 384, 512))
+        mms([(R("pA", 384, 512), R("nif"), R("old"), True, False)])
+        mms([(R("pA", 384, 512), R("idf"), R("mR"), False, True)])
+        act(R("dif"), R("pA", 384, 512))
         lowest("cR", R("cf"), R("lrn"), R("cf"), R("tg2"), "pB", 48, "Ea")
         write(R("pG", 384, 512), R("mR"), R("tg2"), R("pB", 384, 512))
         ts(R("y", 80, 88), R("w3"), 1.0, ad)
@@ -525,15 +537,58 @@ def build(g, core, T, topo):
     return ops, nsent[0]
 
 
-def place(ops, seq, pre, back):
+def window(ops, pre, suc, st, t0, t1, passes, rand):
+    n = len(ops)
+    dur = [o["cost"] + o["lat"] for o in ops]
+    tail, nxt, qe = [0.0] * n, {}, {}
+    for i in sorted(range(n), key=lambda x: -st[x]):
+        if st[i] < t1:
+            break
+        e = ops[i]["eng"]
+        tail[i] = max([dur[i] + h + tail[j] for j, h in suc[i]] + [dur[i], ops[i]["cost"] + (nxt.get(e, 0.0) if e != "-" else 0.0)])
+        nxt[e] = qe[e] = tail[i]
+    qe.pop("-", None)
+    w = [i for i in range(n) if t0 <= st[i] < t1]
+    at = {i: k for k, i in enumerate(w)}
+    sub = [ops[i] for i in w]
+    p2 = [[(at[j], h) for j, h in pre[i] if j in at] for i in w]
+    s2 = [[(at[j], h) for j, h in suc[i] if j in at] for i in w]
+    rel = [max([st[j] + dur[j] + h for j, h in pre[i] if j not in at] + [0.0]) for i in w]
+    out = [max([tail[j] + h for j, h in suc[i] if j not in at] + [0.0]) for i in w]
+    free = {}
+    for i in range(n):
+        if st[i] < t0 and ops[i]["eng"] != "-":
+            free[ops[i]["eng"]] = max(free.get(ops[i]["eng"], 0.0), st[i] + ops[i]["cost"])
+    m = len(w)
+    if m < 2:
+        return st
+    seq = topo_order(m, p2, s2, [st[i] for i in w])
+    best = None
+    for it in range(passes):
+        s = place(sub, seq, p2, False, rel, free)
+        v = max(max(s[k] + dur[i] + out[k], s[k] + sub[k]["cost"] + qe.get(sub[k]["eng"], 0.0)) for k, i in enumerate(w))
+        if best is None or v < best[1]:
+            best = (s, v)
+        elif it % 2 == 0:
+            s = best[0]
+        a = NOISE * rand() * rand() * (it % 2 == 0)
+        bt = place(sub, topo_order(m, s2, p2, [-s[k] - dur[i] + a * rand() for k, i in enumerate(w)]), s2, True, out, qe)
+        seq = topo_order(m, p2, s2, [-(bt[k] + sub[k]["cost"]) + a * rand() for k in range(m)])
+    key = [st[i] + (1e7 if st[i] >= t1 else 0.0) for i in range(n)]
+    for k, i in enumerate(w):
+        key[i] = max(t0, best[0][k])
+    return place(ops, topo_order(n, pre, suc, key), pre, False)
+
+
+def place(ops, seq, pre, back, rel=None, free=None):
     st = [0.0] * len(ops)
-    busy = {}
+    busy = {e: ([-1.0], [f]) for e, f in (free or {}).items()}
     for i in seq:
         o = ops[i]
         if back:
-            r = max([st[j] + ops[j]["cost"] + h for j, h in pre[i]] + [0.0]) + o["lat"]
+            r = max([st[j] + ops[j]["cost"] + h for j, h in pre[i]] + [rel[i] if rel else 0.0]) + o["lat"]
         else:
-            r = max([st[j] + ops[j]["cost"] + ops[j]["lat"] + h for j, h in pre[i]] + [0.0])
+            r = max([st[j] + ops[j]["cost"] + ops[j]["lat"] + h for j, h in pre[i]] + [rel[i] if rel else 0.0])
         if o["eng"] != "-":
             a, b = busy.setdefault(o["eng"], ([], []))
             lo, hi = 0, len(b)
@@ -556,7 +611,7 @@ def schedule(ops):
     n = len(ops)
     pre = [[] for _ in ops]; suc = [[] for _ in ops]
     for i, o in enumerate(ops):
-        near = [(j, HOP) for j in o["hard"]] + [(j, 0.0) for j in o["soft"]]
+        near = [(j, HOP) for j in o["hard"]] + [(j, -ops[j]["lat"]) for j in o["soft"]]
         pre[i] = near
         for j, h in near:
             suc[j].append((i, h))
@@ -565,19 +620,29 @@ def schedule(ops):
     def rand():
         state[0] = state[0] * 48271 % 2147483647
         return state[0] / 2147483647.0
-    best = None
-    seq = list(range(n))
+    best = walk = None
+    seq = topo_order(n, pre, suc, list(range(n)))
     for it in range(PASSES):
         st = place(ops, seq, pre, False)
         end = max(st[i] + ops[i]["cost"] + ops[i]["lat"] for i in range(n))
         if best is None or end < best[1]:
             best = (st, end)
+        if walk is None or end < walk[1] + HEAT * (1.0 - it / PASSES):
+            walk = (st, end)
         elif it % 2 == 0:
-            st = best[0]
+            st = walk[0]
         fin = [st[i] + ops[i]["cost"] + ops[i]["lat"] for i in range(n)]
         c, w, a = rand() * best[1], 3000 + 12000 * rand(), NOISE * rand() * (it % 2 == 0)
         bt = place(ops, topo_order(n, suc, pre, [-f + (a * rand() if abs(f - c) < w else 0.0) for f in fin]), suc, True)
         seq = topo_order(n, pre, suc, [-(bt[i] + ops[i]["cost"]) + (a * rand() if abs(fin[i] - c) < w else 0.0) for i in range(n)])
+    for it in range(SWEEPS):
+        t0 = -WIDE * rand()
+        while t0 < best[1]:
+            st = window(ops, pre, suc, best[0], t0, t0 + WIDE, TRIES, rand)
+            end = max(st[i] + ops[i]["cost"] + ops[i]["lat"] for i in range(n))
+            if end <= best[1]:
+                best = (st, end)
+            t0 += WIDE / 2
     st, end = best
     cur = best
     dur = [o["cost"] + o["lat"] for o in ops]

@@ -3,45 +3,49 @@ from concourse.mybir import AluOpType, AxisListType, ActivationFunctionType
 RO = 4
 NV = 72
 NS = 128 - NV
-NG = 60
-NB = 2
-NA = 8
+NA = 10
 NE = 4
-NF = 4
-NB2 = 4
-LATE = True
+NB2 = 0
+NG2 = 0
+EARLY = 0
+DCUT = 2
+SPLIT = True
 N16 = 13
+FILL = 2816
+SLOT = 448
 HUGE = float(1 << 26)
 BK = 8192.0
-BIG = 65 * 2048.0
-FALL = 73728.0
-K0 = 3 * BIG + 61440.0 + 2048.0 + 8192.0
+STEP = 16384.0
+BIG = 32 * STEP
+FALL = BIG + STEP
 MAGIC = 12582912.0
 
 F, B, H, I32, U = "float32", "bfloat16", "float16", "int32", "uint16"
 _S = {
-    "Ii": (4096, I32), "Iw": (4224, F), "Pw": (8192, B), "alti": (1024, I32), "altw": (1024, F), "iot": (4096, F),
+    "Ii": (4096, I32), "Iw": (4224, F), "Pw": (8192, B), "alti": (4096, I32), "iox": (4096, F),
     "Ih": (256 * N16, H), "ycs": (256, F), "thi": (4, I32), "thf": (4, F), "thc": (4, F),
-    "pi": (1, I32), "pt": (8, I32), "pc": (16, F), "c16": (128, F), "cg": (128, F), "cc": (144, F), "c4": (128, F), "c8": (128, F),
-    "tmp": (128, F), "tm2": (128, F), "Z1": (144, B), "Z2": (144, B), "Zm": (144, B), "Zh": (144, B), "Zf": (144, F),
-    "idb": (128, B), "nid": (128, B), "bid": (128, B), "BO": (128, B), "BOf": (128, F), "B16": (8, B), "ones": (128, B),
-    "LmB": (128, B), "SelK": (512, B), "Rep": (128, B), "LF": (1024, B), "Lsig": (128, B), "Ldel": (128, B), "RE": (16, B),
-    "mT": (128, F), "QS": (8, F), "EXPL": (8, U), "EXPQ": (8, U), "dmin": (128, F), "dmax": (128, F), "k15": (128, F),
-    "s16": (512, F), "s4": (128, F), "ltile": (8, F), "dump": (8, F), "tri": (128, B), "id4": (4, B), "alph": (2, F), "one8": (8, F),
-    "ci": (8, I32), "cf": (8, F), "cu": (8, U), "lou": (8, U), "hiu": (8, U), "w1": (8, I32), "w2": (8, I32), "w3": (8, I32),
-    "A": (128, B), "nA": (128, B), "A16": (16 * NV, B), "Af": (128, F), "cR": (128, F), "mR": (128, F), "bR": (128, F),
-    "mj": (128, B), "Ogm": (128, H), "sc": (512, F), "sc4": (128, F), "OL": (32, F), "OLu": (32, U), "OSu": (32, U),
-    "Cu": (512, U), "CuS": (4 * NS, U), "Cw": (384, F), "Ch": (384, H), "D": (64 * NV, B), "Rl": (64 * NV, B), "GS": (64 * NS, B),
-    "near": (512, B), "x": (64, F), "idx": (8, U), "Fh": (128, H), "Xab": (1536, F), "E": (1536, B), "svX": (384, B), "z": (384, B),
-    "sk": (128, F), "lT": (128, F), "sv": (64, F), "y": (104, F), "mk": (8, I32), "mi": (8, I32), "lrn": (8, B), "v": (128, F),
-    "mu": (8, U), "selu": (8, U), "lru": (8, U), "ecol": (1, F), "vs": (8, F), "Ea": (1024, B), "Eb": (1024, B), "Lt": (2048, B), "iox": (4096, F), "mTK": (128, F), "idf": (128, F), "nif": (128, F), "tg2": (8, U),
-    "C2u": (128, U), "old": (128, F), "Xc": (128, B), "G2": (2048, B), "ab": (2048, B), "key": (128, F), "oh": (128, B),
-    "dif": (128, F), "tt": (128, F), "u": (128, F), "au": (128, F), "aR": (128, F),
-    "msg1": (16 * RO + 16, U), "msg2": (8 * RO, U), "land1": (16 * RO, U), "land2": (8 * RO, U),
+    "pi": (1, I32), "pt": (8, I32), "pc": (16, F), "c16": (128, F), "cg": (128, F), "cc": (144, F), "c8": (128, F), "ex": (48, F),
+    "tm2": (128, F), "Z1": (144, B), "Z2": (144, B), "Zm": (144, B), "Zh": (144, B), "Zf": (144, F), "Zi": (144, B),
+    "idb": (128, B), "nid": (128, B), "bid": (128, B), "BO": (128, B), "nBO": (128, B), "BOf": (128, F), "B16": (8, B), "ones": (128, B),
+    "LmB": (128, B), "LF": (1024, B), "Lsig": (128, B), "Ldel": (128, B), "RE": (16, B), "Kc": (128, H), "K128": (8, B),
+    "mT": (128, F), "QS": (8, F), "EXPL": (8, U), "dmin": (128, F), "dmax": (128, F), "k15": (128, F), "key": (128, F), "ch": (8, H),
+    "s16": (128, F), "ltile": (8, F), "dump": (8, F), "dum3": (8, F), "Lt": (2048, B), "nEr": (2048, B), "idf": (128, F), "nif": (128, F),
+    "k2": (128, B), "k2048": (128, B), "B32": (8, B), "B16n": (8, B), "zero": (128, B),
+    "ci": (8, I32), "cf": (8, F), "cu": (8, U), "w1": (8, I32), "w2": (8, I32), "w3": (8, I32),
+    "A": (128, B), "A16": (16 * NV, B), "Af": (128, F), "cR": (128, F), "cxR": (128, F), "aR": (128, F),
+    "Og": (128, H), "Og4": (512, H), "sc4": (128, F), "sa": (64, F), "sb": (64, F), "OL": (32, F), "OLu": (32, U), "OSu": (32, U),
+    "Cu": (512, U), "CuS": (4 * NS, U), "Ch": (384, H), "D": (64 * NV, B), "Rl": (64 * NV, B), "GS": (64 * NS, B),
+    "near": (512, B), "hn": (24, F), "hd": (24, F), "hs": (24, F), "fou": (8, U), "Fh": (128, H),
+    "Xab": (1536, F), "E": (1536, B), "z": (384, B),
+    "sk": (128, F), "lT": (128, F), "sv": (64, F), "y": (112, F), "mk": (8, I32), "mi": (8, I32), "lrn": (8, B), "lk": (8, B), "mh": (8, H),
+    "v": (128, F), "mu": (8, U), "posu": (8, U), "selu": (8, U), "ecol": (1, F), "vs": (8, F), "Ea": (1024, B), "Eb": (256, B),
+    "tg2": (8, U), "tg3": (8, U), "C2u": (128, U), "old": (128, F), "Xc": (128, B), "G2": (2048, B), "ab": (2048, B), "oh": (128, B),
+    "C3u": (64, U), "ol3": (64, F), "X3": (64, B), "G3": (1024, B), "a3": (1024, B), "ohs": (128, F),
+    "dif": (64, F), "tt": (128, F), "u": (128, F), "au": (128, F),
+    "pairs": (SLOT * RO, F), "msg1": (8 * RO, U), "land1": (8 * RO, U), "land2": (72 * RO, F),
 }
-_S.update({"B32": (8, B), "B16n": (8, B), "zero": (512, B)})
 ALIAS = {}
-for _p, _d, _l in (("kb", B, "Z1 Z2 Zm idb nid bid BO ones LmB tri B16 B32 B16n RE"), ("kf", F, "dmin dmax k15 mT s4 ltile dump one8 QS c4 c8 cg")):
+for _p, _d, _l in (("kb", B, "Z1 Z2 Zm Zi idb nid bid BO nBO ones LmB B16 B32 B16n RE K128 k2 k2048"), ("kf", F, "dmin dmax mT ltile dump dum3 QS c8 cg")):
     _o = 0
     for _k in _l.split():
         ALIAS[_k] = (_p, _o, _S[_k][0]); _o += _S.pop(_k)[0]
@@ -49,19 +53,17 @@ for _p, _d, _l in (("kb", B, "Z1 Z2 Zm idb nid bid BO ones LmB tri B16 B32 B16n 
 SCRATCH = {k: ("sbuf", [128, v[0]], v[1]) for k, v in _S.items()}
 for _b in "ABCDEFGH":
     SCRATCH["p" + _b] = ("psum", [128, 512], F)
-NDMA = 14
+NDMA = 15
 SEMAPHORES = ["cV", "cS", "cP", "cG", "sent"] + ["d%d" % i for i in range(NDMA)] + ["a%d" % i for i in range(2 * RO)]
 CNT = {"V": "cV", "S": "cS", "P": "cP", "G": "cG"}
 CY, GA, SCA, PE, HOP = 1.04, 1.62, 3.95, 0.52, 110.0
 LAT1 = 2500.0
-LAT2 = 4500.0
+LAT2 = 3000.0
 SWEEPS = 4
 WIDE = 14000.0
 TRIES = 300
 SEED = 1
 PASSES = 30
-MOVES = 0
-HEAT = 0.0
 NOISE = 3000.0
 REPORT = {}
 
@@ -75,7 +77,7 @@ def build(g, core, T, topo):
     AF = ActivationFunctionType
     ops, acc = [], {}
     nd = [0]
-    now, seen = [-1], {}
+    now = [-1]
 
     def R(b, c0=0, c1=None, st=1, p0=0, p1=128):
         if b in ALIAS:
@@ -109,20 +111,18 @@ def build(g, core, T, topo):
         hard, soft = set(), set(after)
         for r, w in [(r, False) for r in rd] + [(r, True) for r in wr]:
             ps = SCRATCH[r[0]][0] == "psum"
-            for (j, c0, c1, wj) in acc.get(r[0], []):
+            for (j, c0, c1, wj, sj) in acc.get(r[0], []):
                 ej = ops[j]["eng"]
                 if ps:
                     if ej != eng or (eng != "P" and (w or wj)):
                         hard.add(j)
                     elif eng == "P":
                         soft.add(j)
-                elif (w or wj) and c0 < r[2] and r[1] < c1:
+                elif (w or wj) and c0 < r[2] and r[1] < c1 and not (sj == r[3] and (c0 - r[1]) % sj):
                     hard.add(j)
         for r, w in [(r, False) for r in rd] + [(r, True) for r in wr]:
-            acc.setdefault(r[0], []).append((i, r[1], r[2], w))
-        name = "%s %s %d" % (eng, (wr or rd or [("",)])[0][0], now[0] < 0)
-        seen[name] = seen.get(name, 0) + 1
-        ops.append(dict(round=now[0], tag="%s %d" % (name, seen[name]), eng=eng, fns=fns, hard=hard, soft=soft - hard, cost=cost, kind=kind, lat=lat, sem=sem, w=(wr or rd or [("",)])[0][0]))
+            acc.setdefault(r[0], []).append((i, r[1], r[2], w, r[3]))
+        ops.append(dict(round=now[0], eng=eng, fns=fns, hard=hard, soft=soft - hard, cost=cost, kind=kind, lat=lat, sem=sem, w=(wr or rd or [("",)])[0][0]))
         return i
 
     def vcost(out, ins, tt=False):
@@ -220,13 +220,19 @@ def build(g, core, T, topo):
     col = lambda b, j: R(b, j, j + 1)
     eq, mu_, ad, sb = A_.is_equal, A_.mult, A_.add, A_.subtract
 
+    mset(R("alti", 0, FILL), 0)
+    iota(R("alti", FILL, 4096), [[0, 4096 - FILL]], 0, 0)
     dma("Y", T.ci[:, :], T.gate[:, :], [], [R("ci")], 2000)
-    dma("Y", T.alti[:, :], T.alt[:, :], [], [R("alti")], 3000)
     dma("S", T.A[:, :], T.acc0[:, :], [], [R("A")], 2200)
     dma("S", T.thi[0:8, :], T.th[:, :], [], [R("thi")], 2200)
     for j in range(4):
-        dma("Y", T.Ii[:, 1024 * j:1024 * j + 1024], T.icol[:, 1024 * j:1024 * j + 1024], [], [R("Ii", 1024 * j, 1024 * j + 1024)], 4000 + 1100 * j)
-    dma("Y", T.Pw[:, 0:4096], T.pat[:, :], [], [R("Pw", 0, 4096)], 9000)
+        dma("Y", T.Ii[:, 1024 * j:1024 * j + 1024], T.icol[:, 1024 * j:1024 * j + 1024], [], [R("Ii", 1024 * j, 1024 * j + 1024)], 3000 + 1100 * j)
+    fill = [0, 1]
+    alts = [dma("Y", T.alti[k:128:16, :], T.alt[k:32:4, :], [], [], 4500) for k in range(4)]
+    for i in alts:
+        ops[i]["hard"].update(fill)
+        acc["alti"].append((i, 0, 4096, True, 1))
+    dma("Y", T.Pw[:, 0:4096], T.pat[:, :], [], [R("Pw", 0, 4096)], 6600)
     chain([i for i, o in enumerate(ops) if o["eng"] == "Y"])
 
     iota(R("pi"), [[0, 1]], 0, 1)
@@ -234,185 +240,199 @@ def build(g, core, T, topo):
     iota(R("cg"), [[1, 8], [0, 16]], 0, 0)
     iota(R("c16"), [[0, 8], [1, 16]], 0, 0)
     mset(R("zero"), 0.0)
-    iota(R("c4"), [[0, 32], [1, 4]], 0, 0)
     iota(R("c8"), [[0, 16], [1, 8]], 0, 0)
-    for j in range(3):
-        iota(R("iot", 1024 * j, 1024 * j + 1024), [[1, 1024]], 1024 * j, 0)
-    act(R("iot", 3072, 4096), R("iot", 0, 1024), bias=3072.0)
+    for j in range(4):
+        iota(R("iox", 1024 * j, 1024 * j + 1024), [[2, 512], [-1, 2]], 1024 * j + 1, 0)
     sh, an = A_.logical_shift_right, A_.bitwise_and
-    for j, (s, m) in enumerate([(0, 15), (4, 7), (0, 127), (0, 3), (2, 3), (1, 7), (3, 1), (0, 1)]):
+    for j, (s, m) in enumerate([(0, 15), (4, 7), (0, 127), (1, 7), (3, 15), (0, 1)]):
         ts(col("pt", j), R("pi"), s, sh, m, an)
-    cp(R("pc", 0, 7), R("pt", 0, 7))
-    ts(col("pc", 7), col("pt", 1), 16.0, mu_, 15.0, ad)
-    ts(col("pc", 9), col("pt", 0), -BK, mu_, 15 * BK + 1, ad)
-    ts(col("pc", 10), col("pt", 0), -BK, mu_, 15 * BK + 2048, ad)
-    ts(col("pc", 11), col("pt", 4), -BK, mu_, 3 * BK + 2048, ad)
-    ts(col("pc", 12), col("pt", 0), 1.0, ad)
-    ts(col("pc", 13), col("pt", 7), -2.0, mu_, 1.0, ad)
-    ts(col("pt", 7), R("pi"), 3, sh)
-    cp(col("pc", 8), col("pt", 7))
+    cp(R("pc", 0, 6), R("pt", 0, 6))
     P = lambda j: col("pc", j)
-    c128 = R("cc", 0, 128); c16 = R("c16", 0, 128)
+    act(P(6), P(2), bias=12.0)
+    act(P(7), P(1), bias=15.0, scale=16.0)
+    ts(P(8), P(0), 4.0, A_.is_lt)
+    act(P(9), P(0), bias=15 * BK, scale=-BK)
+    act(P(10), P(0), bias=15 * BK + 1, scale=-BK)
+    act(P(12), P(0), bias=1.0)
+    act(P(13), P(5), bias=1.0, scale=-2.0)
+    ts(P(14), P(0), float(N16), A_.is_lt, 136.0 * 2048, mu_)
+    c16 = R("c16", 0, 128)
     ts(R("BO"), R("cg"), P(1), eq)
-    ts(R("id4"), R("cc", 0, 4), P(3), eq)
-    for k in range(4):
-        ts(col("x", k), P(4), float(k), eq)
-        act(R("SelK", 128 * k, 128 * k + 128), R("BO"), scale=col("x", k))
-    ts(R("tmp"), R("c4"), P(4), eq)
-    tt(R("Rep"), R("tmp"), R("BO"), mu_)
-    ts(R("s16", 0, 128), c16, P(0), eq, HUGE, mu_)
-    act(R("mT"), R("s16", 0, 128), scale=1.0 / HUGE)
-    for j in (3, 2, 1, 0):
-        act(R("s16", 128 * j, 128 * j + 128), R("s16", 0, 128), bias=-BK)
-    act(R("s4"), R("tmp"), bias=-BK, scale=HUGE)
+    act(R("nBO"), R("BO"), scale=-1.0)
+    ts(R("s16"), c16, P(0), eq, HUGE, mu_)
+    act(R("mT"), R("s16"), scale=1.0 / HUGE)
+    act(R("s16"), R("s16"), bias=-BK)
     ts(R("Z1"), R("cc"), P(7), eq)
+    ts(R("Zi"), R("cc"), P(6), eq, P(8), mu_)
     for nm, w in (("Z2", 2.0), ("Zm", -1.0), ("Zh", P(12)), ("Zf", P(12))):
         act(R(nm), R("Z1"), scale=w)
-    z128 = R("zero", 0, 128)
-    for nm, w in (("idb", 1.0), ("nid", -1.0), ("bid", -BIG)):
-        sel(R(nm), z128, [[-1, 128]], w, 0, 1)
+    for nm, w in (("idb", 1.0), ("nid", -1.0), ("bid", BIG)):
+        sel(R(nm), R("zero"), [[-1, 128]], w, 0, 1)
     ts(R("BOf"), R("cg"), P(2), eq)
     ts(R("QS"), R("cc", 0, 8), P(1), eq)
     for nm, w in (("B16", 16.0), ("B32", 32.0), ("B16n", -16.0)):
         act(R(nm), R("QS"), scale=w)
-    iota(R("ones"), [[0, 128]], 1, 0); iota(R("one8"), [[0, 8]], 1, 0)
+    iota(R("ones"), [[0, 128]], 1, 0); iota(R("k2"), [[0, 128]], 2, 0); iota(R("k2048"), [[0, 128]], -2048, 0)
     iota(R("Iw", 4096, 4224), [[0, 128]], 0, 0)
-    mset(col("alph", 0), 1.0); mset(col("alph", 1), 0.4995)
-    act(R("mTK"), R("mT"), scale=K0 + FALL - 4096.0)
+    for t in range(RO):
+        iota(R("pairs", SLOT * t, SLOT * t + 128), [[-4096, 2], [1, 64]], 4096, 0)
+    iota(R("hn"), [[0, 24]], 0, 0)
     act(R("idf"), R("idb")); act(R("nif"), R("nid"))
-    for j in range(4):
-        iota(R("iox", 1024 * j, 1024 * j + 1024), [[2, 512], [-1, 2]], 1024 * j + 1, 0)
-    ts(R("x", 16, 32), R("cc", 0, 16), P(0), A_.is_gt)
-    ts(R("x", 32, 48), R("cc", 0, 16), P(0), eq)
-    tt(R("x", 16, 32), R("x", 16, 32), R("x", 32, 48), sb)
+    ts(R("ex", 0, 16), R("cc", 0, 16), P(0), eq)
+    ts(R("ex", 16, 32), R("cc", 0, 16), P(0), A_.is_gt)
+    tt(R("ex", 32, 48), R("ex", 16, 32), R("ex", 0, 16), sb)
     for h in range(4):
-        acts([(R("Lt", 128 * r, 128 * r + 128), R("BO"), AF.Identity, 0.0, col("x", 16 + r)) for r in range(4 * h, 4 * h + 4)])
-    ts(R("tm2"), c16, P(0), A_.is_le)
+        acts([(R("Lt", 128 * r, 128 * r + 128), R("BO"), AF.Identity, 0.0, col("ex", 32 + r)) for r in range(4 * h, 4 * h + 4)])
+        acts([(R("nEr", 128 * r, 128 * r + 128), R("nBO"), AF.Identity, 0.0, col("ex", r)) for r in range(4 * h, 4 * h + 4)])
+    ts(R("tm2"), c16, P(0), A_.is_gt)
     tt(R("LmB"), R("tm2"), R("BO"), mu_)
-    ts(R("tm2"), R("c8"), P(5), eq)
+    ts(R("tm2"), R("c8"), P(3), eq)
     tt(R("tm2"), R("tm2"), R("BO"), mu_)
     act(R("Lsig"), R("tm2"), scale=-1.0)
     act(R("Ldel"), R("tm2"), scale=P(13))
     pq = [[-16, 8], [-8, 2], [0, 8]]
     for j in range(8):
-        sel(R("LF", 128 * j, 128 * j + 128), z128, pq, 2.0, -j, 1)
-    ts(R("RE"), R("cc", 0, 16), P(8), eq)
+        sel(R("LF", 128 * j, 128 * j + 128), R("zero"), pq, 2.0, -j, 1)
+    ts(R("RE"), R("cc", 0, 16), P(4), eq, 16.0, mu_)
     ts(R("EXPL"), R("cc", 0, 8), 16.0, mu_, 15.0, ad)
-    for nm, a, b in (("dmin", -4096, HUGE), ("dmax", 1, -HUGE)):
-        iota(R(nm), [[0, 128]], a, 0)
-        sel(R(nm), R(nm), [[0, 8], [1, 16]], b, 0, 0)
-    iota(R("k15"), [[0, 8], [-1, 16]], 15, 0)
-    ts(R("ltile"), R("cc", 0, 8), 16.0, mu_, P(0), ad)
-    ts(R("dump"), R("ltile"), 4096.0, ad)
+    ts(R("dmin"), c16, 0.0, eq, HUGE, mu_)
+    act(R("dmax"), R("dmin"), bias=1.0, scale=-1.0)
+    act(R("k15"), c16, bias=15.0, scale=-1.0)
+    ts(R("Kc"), c16, STEP / 128, mu_, (BIG + 2 * STEP + 2048) / 128, ad)
+    act(R("ltile"), R("cc", 0, 8), bias=P(0), scale=16.0)
+    act(R("dump"), R("ltile"), bias=2048.0)
+    act(R("dum3"), R("ltile"), bias=4160.0)
+    act(R("K128"), R("ltile"), bias=128.0)
     cp(R("thf", p1=8), R("thi", p1=8))
     mms(grp(R("pH", 0, 4), [(R("BOf", p1=8), R("thf", p1=8))]))
     cp(R("thc"), R("pH", 0, 4))
-    ts(R("altw"), R("alti"), -2048.0, ad)
-    conv = [cp(R("Iw", 512 * j, 512 * j + 512), R("Ii", 512 * j, 512 * j + 512)) for j in range(8)]
-    Iw = R("Iw", 0, 4096); Pw = R("Pw", 0, 4096)
-
-    cu = lambda t: R("msg1", 16 * t + 8, 16 * t + 16)
+    for j in range(8):
+        cp(R("Iw", 512 * j, 512 * j + 512), R("Ii", 512 * j, 512 * j + 512))
+    Iw = R("Iw"); Pw = R("Pw", 0, 4096)
+    mat = lambda b, r: R(b, 128 * r, 128 * r + 128)
+    late = []
 
     def prep(t):
-        cp(cu(t), R("ci"))
-        act(R("cR"), ind(R("iot"), cu(t)))
+        ts(R("ch"), R("ci"), -2048.0, ad)
+        if t < RO:
+            cp(R("cu"), R("ci"))
+        mms([(R("pH", 256, 384), R("idb"), R("zero"), True, False)] +
+            [(R("pH", 256 + r, 384, 16), mat("nEr", r), R("ch"), False, r == 15) for r in range(16)])
         if t == RO:
+            act(R("cR"), R("pH", 256, 384), bias=2048.0, scale=-1.0)
             return
-        cp(R("cf"), R("ci"))
-        ts(R("w1"), R("ci"), 1023, an); ts(R("w2"), R("ci"), 10, sh)
-        cp(R("lou"), R("w1")); cp(R("hiu"), R("w2"))
-        act(R("mj"), ind(R("id4"), R("hiu")))
-        tt(R("Ogm"), ind(R("altw"), R("lou")), R("mj"), mu_)
-        mms(grp(R("pB", 0, NS), [(R("Rep"), R("Ogm", NV, 128))]))
-        mms([x for k in range(4) for x in grp(R("pA", 128 * k, 128 * k + 128), [(R("SelK", 128 * k, 128 * k + 128), R("Ogm"))])])
-        scan(R("sc4", 0, NS), R("s4", 0, NS), R("pB", 0, NS), ad, A_.min)
-        ts(R("OSu", 0, NS // 4), R("sc4", 3, NS, 4), P(11), ad)
-        scan(R("sc"), R("s16"), R("pA"), ad, A_.min)
-        ts(R("OLu"), R("sc", 15, 512, 16), P(10), ad)
-        ts(R("OL"), R("sc", 15, 512, 16), P(10), ad, FALL, ad)
+        ts(R("cf"), R("ci"), -2048.0, ad)
+        late.append(alike(R("pH", 256, 384), R("cf"), R("lrn"), 8, "Ea", 1.0))
+        ts(R("Og"), ind(R("alti"), R("cu")), -2048.0, ad)
+        mms([(R("pA", 300, 300 + NS // 4), R("Zi", 12 - 4 * a, 140 - 4 * a), R("Og", NV + a, 128, 4), a == 0, a == 3) for a in range(4)])
+        ts(R("OSu", 0, NS // 4), R("pA", 300, 300 + NS // 4), 2048.0, ad)
+        for k in range(4):
+            ts(mat("Og4", k), R("Og"), col("ex", k), mu_)
+        mms(grp(R("pG", 256, 288), [(R("Z1", 15 - r, 143 - r), R("Og4", r, 512, 16)) for r in range(16)]))
+        ts(R("OLu"), R("pG", 256, 288), 2048.0, ad)
+        act(R("OL"), R("pG", 256, 288), bias=2048.0 + FALL)
+        act(R("cxR"), ind(R("iox"), R("cu")))
+        tt(R("hd", 0, 24, 3), R("OL", 16, 24), R("OL", 8, 16), sb)
+        tt(R("hd", 1, 24, 3), R("OL", 8, 16), R("OL", 0, 8), sb)
+        act(R("hd", 2, 24, 3), R("OL", 0, 8), bias=-FALL)
+        act(R("y", 88, 96), R("OL", 24, 32), bias=-8192.0)
+        act(R("y", 96, 104), R("OL", 24, 32), bias=17 * STEP + 8192.0)
+        act(R("y", 32, 40), R("OL", 0, 8), bias=4096.0 - FALL)
         na = NA if t else 0
         for p in range(na):
             sel(R("A16", p, 16 * NV, 16), R("A", 0, NV), [[0, NV]], 0.0, 1, 0)
         if na < 16:
             acts([(R("A16", p, 16 * NV, 16), R("A", 0, NV), AF.Identity, 0.0, 1.0) for p in range(na, 16)])
 
-    def farthest(lst, split, bank):
+    def onehot(sums, lanes, out):
+        scan(R("sk", p1=lanes), R("dmax", p1=lanes), sums, ad, A_.max)
+        tt(R("key", p1=lanes), sums, R("k15", p1=lanes), ad)
+        tt(R("oh"), ind(R("sk"), R("EXPL")), R("key"), eq)
+        mms(grp(out, [(R("oh", p1=lanes), R("idb", 0, lanes, p1=lanes))]))
+
+    def farthest2():
+        lst = R("cu")
         cp(R("C2u"), ind(Iw, lst))
         act(R("Xc"), ind(Pw, lst))
         act(R("old"), ind(Iw, lst))
-        cuts = [0, NG, 128] if split else [0, 32, 64, 96, 128]
-        for h in range(len(cuts) - 1):
-            o, w = R("G2", 16 * cuts[h], 16 * cuts[h + 1]), ind(Pw, R("C2u", cuts[h], cuts[h + 1]))
-            if split and h == 0:
-                cp(o, w)
+        for h in range(4):
+            (cp if h < NG2 else act)(R("G2", 512 * h, 512 * h + 512), ind(Pw, R("C2u", 32 * h, 32 * h + 32)))
+
+        def bank(b, pb):
+            rows = range(4 * b, 4 * b + 4)
+            if b < NB2:
+                mms(grp(R(pb, 0, 128), [(R("idb"), R("Xc"))]))
+                for p in rows:
+                    tt(mat("ab", p), R("G2", p, 2048, 16), R(pb, 0, 128), A_.max)
             else:
-                act(o, w)
+                mms([x for p in rows for x in grp(mat(pb, p % 4), [(R("nid"), R("Xc")), (R("idb"), R("G2", p, 2048, 16))])])
+                act(R("ab", 512 * b, 512 * b + 512), R(pb), AF.Abs)
+
+        def first():
+            for b in range(EARLY):
+                bank(3 - b, "p" + "DE"[b % 2])
 
         def rest():
-            for b in range(4 if split else 0):
-                pb = "p" + "CDEF"[b]
-                mms([(R(pb, 128 * j, 128 * j + 128), R("nid"), R("Xc"), j == 0, False) for j in range(4)])
-            for b in (0, 2, 1, 3):
-                pb = "p" + "CDEF"[b]
-                if split:
-                    mms([(R(pb, 128 * j, 128 * j + 128), R("idb"), R("G2", 4 * b + j, 2048, 16), False, j == 3) for j in range(4)])
-                else:
-                    for j in range(4):
-                        mms(grp(R(pb, 128 * j, 128 * j + 128), [(R("nid"), R("Xc")), (R("idb"), R("G2", 4 * b + j, 2048, 16))]))
-                if b >= (NB if split else NB2):
-                    ts(R("ab", 512 * b, 512 * b + 512), R(pb), 0.0, A_.max)
-                else:
-                    act(R("ab", 512 * b, 512 * b + 512), R(pb), AF.Abs)
-            lin = range(4 * (NB if split else NB2), 16)
+            for b in range(EARLY, 4):
+                bank(3 - b, "p" + "CDEF"[b])
+            lin = range(4 * NB2)
             if lin:
-                mms([(R("pG", p, 128, 16), R("Xc"), R("B16"), p == lin[0], False) for p in lin])
-                mms([(R("pG", p, 128, 16), R("G2", p, 2048, 16), R("B16n"), False, False) for p in lin])
-            for b in (0, 2, 1, 3):
-                mms([(R("pG", p, 128, 16), R("ab", 128 * p, 128 * p + 128), R("B32" if p in lin else "B16"), p == 0 and not lin, p == 15)
-                     for p in range(4 * b, 4 * b + 4)])
-            tt(R("key"), R("pG", 0, 128), R("k15"), ad)
-            scan(R("sk"), R("dmax"), R("pG", 0, 128), ad, A_.max)
-            tt(R("oh"), ind(R("sk"), R("EXPL")), R("key"), eq)
-            mms(grp(bank, [(R("oh"), R("idb"))]))
+                mms([(R("pB", p, 128, 16), R(x, p if x == "G2" else 0, 2048 if x == "G2" else 128, 16 if x == "G2" else 1), R("B16n"), p == 0 and x == "Xc", False)
+                     for x in ("Xc", "G2") for p in lin])
+            for b in (3, 2, 1, 0):
+                mms([(R("pB", p, 128, 16), mat("ab", p), R("B32" if p in lin else "B16"), p == 12 and not lin, p == 3) for p in range(4 * b, 4 * b + 4)])
+            onehot(R("pB", 0, 128), 128, R("pB", 128, 256))
+            act(R("ohs"), R("pB", 128, 256))
+        return first, rest
+
+    def farthest3(lst):
+        cp(R("C3u"), ind(Iw, lst))
+        act(R("X3"), ind(R("Pw"), lst))
+        cp(R("G3", 0, 512), ind(Pw, R("C3u", 0, 32)))
+        act(R("G3", 512, 1024), ind(Pw, R("C3u", 32, 64)))
+        act(R("ol3"), ind(Iw, lst))
+        mms([(R("pD", p, 512, 16), R("nid"), R("X3", 32, 64), p == 0, False) for p in range(16)])
+        mms([(R("pC", p, 512, 16), R("idb"), R("X3", 0, 32), p == 0, p == 15) for p in range(16)])
+        mms([(R("pD"), R("idb"), R("G3", 512, 1024), False, True)])
+        act(R("a3", 512, 1024), R("pD"), AF.Abs)
+        tt(R("a3", 0, 512), R("G3", 0, 512), R("pC"), A_.max)
+        mms([(R("pE", p, 128, 16, 0, 32), R("G3", p, 512, 16), R("B16n"), p == 0, False) for p in range(16)])
+        mms([(R("pE", p, 128, 16, 0, 32), R("a3", p, 512, 16), R("B32"), False, p == 15) for p in range(16)])
+        mms([(R("pE", p, 128, 16, 32, 64), R("a3", 512 + p, 1024, 16), R("B16"), p == 0, p == 15) for p in range(16)])
+
+    def alike(valR, valL, use, nq, eb, sign):
+        w = 16 * nq
+        one = lambda r, q: (r[0], r[1] + q, r[1] + q + 1, 1, 0, 128)
+        blk = lambda q: R(eb, (w + 16) * q, w * q + w)
+        for h in range(2):
+            acts([(blk(q), R(valR[0], valR[1] + 16 * q, valR[1] + w), AF.Abs, one(valL, q), sign) for q in range(h, nq, 2)])
+
+        def rest():
+            nv = NE if use else 0
+            for q in range(nv):
+                ts(blk(q), blk(q), one(use, q), A_.is_lt)
+            for q in range(nv, nq, 2):
+                acts([(blk(j), blk(j), AF.Relu, one(use, j) if use else 1.0, -1.0) for j in (q, q + 1)])
         return rest
 
-    def differ(val, pd):
-        mms([(pd, R("idf"), val, True, False)])
-        mms([(pd, R("nif"), R("old"), False, True)])
-        act(R("dif"), pd)
-
-    def write(bank, val, tgt, pd):
-        tt(R("tt"), bank, R("dif"), mu_)
-        tt(ind(R("Iw"), tgt), R("tt"), R("old"), ad)
-
-    def lowest(valR, valL, use, tgtL, out, bank, y0, eb):
-        one = lambda r, q: (r[0], r[1] + q, r[1] + q + 1, 1, 0, 128)
-        for h in range(2):
-            acts([(R(eb, 144 * q, 128 * q + 128), R(valR, 16 * q, 128), AF.Abs, one(valL, q), -1.0) for q in range(h, 8, 2)])
-        for q in range(NE if eb == "Ea" else NF):
-            ts(R(eb, 144 * q, 128 * q + 128), R(eb, 144 * q, 128 * q + 128), one(use, q), A_.is_lt)
-        for q in range(NE if eb == "Ea" else NF, 8, 2):
-            acts([(R(eb, 144 * j, 128 * j + 128), R(eb, 144 * j, 128 * j + 128), AF.Relu, one(use, j), -1.0) for j in (q, q + 1)])
-        mms([(R(bank, 128, 256), R("idb"), R("zero", 0, 128), True, False)])
-        for q in range(7):
-            mms([(R(bank, 144 + 16 * q, 256), R("BO"), R(eb, 144 * q + 16, 128 * q + 128), False, False)])
-        mms([(R(bank, 128 + r, 256, 16), R("Lt", 128 * r, 128 * r + 128), R(eb, r, 1024, 144), False, r == 15) for r in range(16)])
-        scan(R("sc4"), R("s16", 0, 128), R(bank, 128, 256), ad, A_.min)
-        ts(R("y", y0, y0 + 8), R("sc4", 15, 128, 16), P(9), ad, 8192.0, mu_)
-        tt(R("y", y0, y0 + 8), R("y", y0, y0 + 8), tgtL, ad)
-        tt(R("y", y0, y0 + 8), R("y", y0, y0 + 8), R("dump"), A_.min)
-        cp(out, R("y", y0, y0 + 8))
+    def lowest(nq, eb, bank, c0, sc, tgt, spare, y0, out):
+        w = 16 * nq
+        mms([(R(bank, c0, c0 + w), R("idb"), R("zero", 0, w), True, False)])
+        for q in range(nq - 1):
+            mms([(R(bank, c0 + 16 + 16 * q, c0 + w), R("BO"), R(eb, (w + 16) * q + 16, w * q + w), False, False)])
+        mms([(R(bank, c0 + r, c0 + w, 16), mat("Lt", r), R(eb, r, w * nq, w + 16), False, r == 15) for r in range(16)])
+        scan(R(sc, 0, w), R("s16", 0, w), R(bank, c0, c0 + w), ad, A_.min)
+        y = R("y", y0, y0 + nq)
+        ts(y, R(sc, 15, w, 16), P(10), ad, 8192.0, mu_)
+        tt(y, y, tgt, ad)
+        tt(out, y, spare, A_.min)
 
     prep(0)
-    for i, o in enumerate(ops):
-        if o["w"] in ("OSu", "OLu"):
-            ops[conv[4]]["soft"].add(i)
     for t in range(RO):
-        now[0] = t; seen.clear()
+        now[0] = t
         chain([cp(R("CuS"), ind(Iw, R("OSu", 0, NS // 4))), cp(R("Cu"), ind(Iw, R("OLu")))])
-        rest2 = farthest(cu(t), False, R("pG", 384, 512))
-        if not LATE:
-            rest2()
+        first2, rest2 = farthest2()
+        first2()
         ch = []
         for l0 in range(0, NS, 16):
             l1 = min(NS, l0 + 16)
@@ -423,8 +443,10 @@ def build(g, core, T, topo):
         W = 16 * NV
         ch = []
         for k in range(4):
-            ch.append(tt(R("D", W * k, W * k + W), ind(Pw, R("Cu", 128 * k, 128 * k + NV)), R("A16"), sb))
-            chain(ch[-2:])
+            cuts = [0, NV] if k < DCUT else [0, NV // 2, NV]
+            for a, b in zip(cuts, cuts[1:]):
+                ch.append(tt(R("D", W * k + 16 * a, W * k + 16 * b), ind(Pw, R("Cu", 128 * k + a, 128 * k + b)), R("A16", 16 * a, 16 * b), sb))
+                chain(ch[-2:])
             ts(R("Rl", W * k, W * k + W), R("D", W * k, W * k + W), 0.0, A_.max)
             o = R("pA" if k % 2 else "pG", NV * k, NV * k + NV)
             mms([(o, R("Zm", 15 - p, 143 - p), R("D", W * k + p, W * k + W, 16), p == 0, False) for p in range(16)])
@@ -434,95 +456,105 @@ def build(g, core, T, topo):
             for j in range(8):
                 ts(R("Pw", 4096 + 512 * j, 4608 + 512 * j), R("Pw", 512 * j, 512 * j + 512), -1.0, mu_)
         ts(R("Ch"), R("Cu", 128, 512), -2048.0, ad)
-        cp(R("Cw", 0, 384), R("Cu", 0, 384))
         mms(grp(R("pC", 0, 384), [(R("Ldel"), R("Ch"))]))
         act(R("pF", 0, 384), R("pC", 0, 384), AF.Abs)
         for k in range(4):
             ts(R("near", 128 * k + NV, 128 * k + 128), R("pB", k, 4 * NS, 4), col("thc", t), A_.is_le)
-        mms(grp(R("pH", 0, 32), [(R("Z1", 15 - r, 143 - r), R("near", r, 512, 16)) for r in range(16)]))
-        ts(R("x", 0, 8), R("pH", 0, 8), 9.0, A_.is_lt, 128.0, mu_)
-        ts(R("x", 8, 16), R("pH", 8, 16), 9.0, A_.is_lt, 1.0, ad)
+        c1 = 16 if SPLIT else 32
+        mms(grp(R("pH", 0, c1), [(R("Z1", 15 - r, 143 - r), R("near", r, 16 * c1, 16)) for r in range(16)]))
+        ts(R("hn", 1, 24, 3), R("pH", 8, 16), 9.0, A_.is_lt)
+        ts(R("hn", 2, 24, 3), R("pH", 0, 8), 9.0, A_.is_lt)
+        scan(R("hs"), R("hn"), R("hd"), mu_, ad)
+        cp(R("fou"), R("hs", 2, 24, 3))
+        ts(R("Fh"), ind(Iw, R("fou")), -2048.0, ad)
+        if SPLIT:
+            mms(grp(R("pH", 16, 32), [(R("Z1", 15 - r, 143 - r), R("near", 256 + r, 512, 16)) for r in range(16)]))
         ts(R("sv", 0, 32), R("pH", 0, 32), 9.0, A_.is_ge)
-        tt(R("x", 16, 24), R("x", 0, 8), R("x", 8, 16), mu_)
-        tt(R("x", 24, 32), R("x", 16, 24), R("ltile"), ad)
-        cp(R("idx"), R("x", 24, 32))
-        ts(R("Fh"), ind(R("Cw"), R("idx")), -2048.0, ad)
-        mms([x for k in range(3) for x in grp(R("pA", 128 * k, 128 * k + 128), [(R("near", 128 * k + 128, 128 * k + 256), R("BO"))])])
-        act(R("svX"), R("pA", 0, 384), AF.Sign, -8.5)
         tt(R("sv", 32, 64), R("sv", 0, 32), R("OL"), mu_)
-        tt(R("x", 48, 64), R("sv", 32, 48), R("sv", 48, 64), ad); tt(R("y", 8, 16), R("x", 48, 56), R("x", 56, 64), ad)
-        act(R("y", 88, 96), R("OL", 24, 32), bias=-4096.0)
-        act(R("y", 96, 104), R("OL", 24, 32), bias=FALL - 4096.0)
-        act(R("y", 32, 40), R("OL", 0, 8), bias=4096.0 - FALL)
+        tt(R("y", 48, 64), R("sv", 32, 48), R("sv", 48, 64), ad); tt(R("y", 8, 16), R("y", 48, 56), R("y", 56, 64), ad)
         tt(R("y", 16, 24), R("y", 8, 16), R("y", 96, 104), A_.min)
         tt(R("y", 16, 24), R("y", 16, 24), R("y", 88, 96), A_.max)
-        ts(R("y", 24, 32), R("y", 8, 16), 1.0, A_.min, 2 * FALL - 4096.0, mu_)
+        ts(R("y", 24, 32), R("y", 8, 16), 1.0, A_.min, BIG + 18 * STEP, mu_)
+        cnt = [R("pG", 0, 128), R("pG", 128, 256), R("pA", 0, 128)]
         for j in range(3):
             mms([(R("p" + "CDE"[j], 0, 384), R("Lsig"), R("Ch"), True, False)])
         for j in range(8):
+            if j == 0:
+                mms([(cnt[k], mat("near", k + 1), R("nBO"), k != 1, False) for k in range(3)])
+            if j == 4:
+                mms([(R("pH", 128, 256), R("ones"), R("Kc"), True, False), (R("pH", 128, 256), R("Fh"), R("idb"), False, False)])
             pb = "p" + "CDE"[j % 3]; h = 384 * (j % 4)
             if j >= 3:
                 mms([(R(pb, 0, 384), R("Lsig"), R("Ch"), True, False)])
-            mms([(R(pb, 128 * k, 128 * k + 128), R("LF", 128 * j, 128 * j + 128), R("Fh"), False, k == 2) for k in range(3)])
+            mms([(R(pb, 128 * k, 128 * k + 128), mat("LF", j), R("Fh"), False, k == 2) for k in range(3)])
             act(R("Xab", h, h + 384), R(pb, 0, 384), AF.Abs)
             tt(R("E", h, h + 384), R("Xab", h, h + 384), R("pF", 0, 384), eq)
-            mms([x for k in range(3) for x in grp(R("pG", 128 * k + j, 128 * k + 128, 8), [(R("E", h + 128 * k, h + 128 * k + 128), R("RE"))])])
-        mms([(R("pB", 256, 264), R("mTK"), R("QS"), True, False)])
-        tt(R("z"), R("pG", 0, 384), R("svX"), A_.is_ge)
-        mms(grp(R("pH", 128, 256), [(R("Fh"), R("idb"))] + [(R("bid"), R("z", 128 * k, 128 * k + 128)) for k in range(3)]))
+            mms([(R(cnt[k][0], cnt[k][1] + j, cnt[k][2], 8), R("E", h + 128 * k, h + 128 * k + 128), R("RE"), False, j == 7 and k > 0) for k in range(3)])
+        ts(R("z", 0, 256), R("pG", 0, 256), -8.5, A_.is_lt)
+        act(R("z", 256, 384), R("pA", 0, 128), AF.Relu, -8.0, -1.0)
+        mms([(R("pH", 128, 256), R("bid"), mat("z", k), False, k == 1) for k in (2, 0, 1)])
         scan(R("sk"), R("dmin"), R("pH", 128, 256), ad, A_.min)
         tt(R("lT"), ind(R("sk"), R("EXPL")), R("mT"), mu_)
-        mms([(R("pB", 256, 264), R("lT"), R("QS"), False, True)])
-        tt(R("mk"), R("pB", 256, 264), R("y", 16, 24), A_.min)
-        ts(R("w1"), R("mk"), 4094, an); ts(R("w2"), R("mk"), 1, an)
-        tt(R("w3"), R("w1"), R("w2"), sb)
-        a_l = R("msg1", 16 * t, 16 * t + 8)
-        ts(a_l, R("w3"), 1.0, ad)
-        send(t, 0, R("msg1", 16 * t, 16 * t + 16), R("land1", 16 * t, 16 * t + 16))
-        ts(R("mi"), R("mk"), 4095, an)
+        mms(grp(R("pH", 256, 264), [(R("lT"), R("QS"))]))
+        mms([(R("pG", 0, 8), R("idb"), R("K128"), True, False)])
+        tt(R("mk"), R("pH", 256, 264), R("y", 16, 24), A_.min)
         tt(R("lrn"), R("mk"), R("y", 24, 32), A_.is_lt)
-        act(R("mR"), ind(R("iox"), a_l))
-        mms(grp(R("pH", 40, 48), [(R("LmB"), R("lrn"))]) + grp(R("pH", 48, 56), [(R("BO"), R("lrn"))]) + grp(R("pH", 56, 64), [(R("ones"), R("lrn"))]))
-        scan(R("y", 40, 48), R("one8"), R("pH", 48, 56), mu_, sb, 64.0)
-        add("V", [lambda: g.vector.tensor_reduce(ap(R("ecol")), ap(R("pH", 56, 64)), AxisListType.X, ad)], [R("pH", 56, 64)], [R("ecol")], 67.0)
-        tt(R("y", 40, 48), R("y", 40, 48), R("pH", 40, 48), ad)
-        tt(R("y", 40, 48), R("y", 40, 48), R("lrn"), A_.min)
-        if LATE:
-            rest2()
-        mms([(R("pA", 384, 512), R("nif"), R("old"), True, False)])
-        mms([(R("pA", 384, 512), R("idf"), R("mR"), False, True)])
-        act(R("dif"), R("pA", 384, 512))
-        lowest("cR", R("cf"), R("lrn"), R("cf"), R("tg2"), "pB", 48, "Ea")
-        write(R("pG", 384, 512), R("mR"), R("tg2"), R("pB", 384, 512))
-        ts(R("y", 80, 88), R("w3"), 1.0, ad)
-        cp(R("vs"), R("mi"))
-        lowest("mR", R("vs"), R("y", 40, 48), R("y", 80, 88), R("msg2", 8 * t, 8 * t + 8), "pA", 64, "Eb")
-        send(t, 1, R("msg2", 8 * t, 8 * t + 8), R("land2", 8 * t, 8 * t + 8))
-        rest3 = farthest(R("land1", 16 * t, 16 * t + 8), True, R("pH", 0, 128))
-        act(R("bR"), ind(R("iox"), R("land1", 16 * t + 8, 16 * t + 16)))
-        tt(R("y", 0, 8), R("mi"), R("y", 32, 40), sb)
-        tt(R("y", 0, 8), R("y", 0, 8), R("lrn"), mu_)
-        tt(R("y", 0, 8), R("y", 0, 8), R("y", 32, 40), ad)
-        cp(R("selu"), R("y", 0, 8)); ts(R("lru"), R("lrn"), 1.0, mu_)
-        act(R("aR"), ind(R("alph"), R("lru")))
+        ts(R("mi"), R("mk"), 4095, an)
+        tt(R("lk"), R("lrn"), R("K128"), mu_)
+        cp(R("mu"), R("mi"))
+        mms([(R("pG", 0, 8), R("LmB"), R("lrn"), False, False)] + [(R("pG", s, 8), R("BO"), R("lrn", 0, 8 - s), False, False) for s in range(1, 8)])
+        mms([(R("pG", 0, 8), R("nid"), R("lk"), False, True)])
+        cp(R("posu"), R("pG", 0, 8))
+        act(R("aR"), ind(R("iox"), R("mu")))
+        s0 = SLOT * t
+        cp(ind(R("pairs", s0, s0 + 384), R("posu")), R("aR"))
+        scan(R("sa"), R("s16", 0, 64), R("pairs", s0, s0 + 64), ad, A_.min)
+        ts(R("msg1", 8 * t, 8 * t + 4), R("sa", 15, 64, 16), P(9), ad)
+        send(t, 0, R("msg1", 8 * t, 8 * t + 4), R("land1", 8 * t, 8 * t + 4))
+        rest2()
+        ts(R("mh"), R("mi"), -2048.0, ad)
+        mms([(R("pA", 128, 256), R("idf"), R("old"), True, False), (R("pA", 128, 256), R("idb"), R("k2048"), False, False)])
+        mms([(R("pA", 128 + r, 256, 16), mat("nEr", r), R("mh"), False, r == 15) for r in range(16)])
+        late.pop()()
+        lowest(8, "Ea", "pB", 256, "sc4", R("cf"), R("dump"), 48, R("y", 48, 56))
+        ts(R("tg2"), R("y", 48, 56), 2048.0, ad)
+        tt(R("tt"), R("pA", 128, 256), R("ohs"), mu_)
+        tt(ind(Iw, R("tg2")), R("old"), R("tt"), sb)
+        act(R("vs", 0, 4), R("sa", 15, 64, 16), bias=P(9))
+        alike(R("pairs", s0, s0 + 64), R("vs"), None, 4, "Eb", -1.0)()
+        cp(ind(R("pairs", s0 + 64, s0 + SLOT), R("posu")), R("cxR"))
+        lowest(4, "Eb", "pG", 128, "sb", R("vs", 0, 4), R("dum3", 0, 4), 64, R("pairs", s0 + 128, s0 + 132))
+        send(t, 1, R("pairs", s0 + 64, s0 + 132), R("land2", 72 * t, 72 * t + 68))
+        farthest3(R("land1", 8 * t, 8 * t + 4))
+        mms(grp(R("pH", 56, 64), [(R("ones"), R("lrn"))]))
+        add("S", [lambda: g.scalar.activation(ap(R("y", 104, 112)), ap(R("pH", 56, 64)), AF.Identity, bias=256.0, accum_out=ap(R("ecol")))],
+            [R("pH", 56, 64)], [R("y", 104, 112), R("ecol")], 90.0)
+        act(R("y", 8, 16), R("cf"), bias=R("ecol"), scale=37.0)
+        tt(R("w1"), R("mi"), R("ci"), mu_)
+        ts(R("w2"), R("w1"), 4, sh)
+        tt(R("w1"), R("w2"), R("y", 8, 16), ad)
+        ts(R("ci"), R("w1"), 4095, an)
+        ts(R("w3"), R("mk"), 8192 + 4095, an)
+        tt(R("y", 0, 8), R("w3"), R("y", 32, 40), A_.min)
+        cp(R("selu"), R("y", 0, 8))
         tt(R("u"), ind(R("Pw"), R("selu")), R("A"), ad)
-        act(R("au"), R("u"), AF.Abs)
-        tt(R("v"), R("au"), R("aR"), mu_)
+        act(R("au"), R("u"), AF.Abs, scale=0.4995)
+        mms([(R("pH", 384, 512), R("idb"), R("k2"), True, False)] +
+            [(R("pH", 384 + r, 512, 16), mat("nEr", r), R("lrn"), False, r == 15) for r in range(16)])
+        tt(R("v"), R("au"), R("pH", 384, 512), mu_)
         act(R("v"), R("v"), bias=MAGIC)
         if t == RO - 1:
             act(R("Af"), R("v"), bias=-MAGIC)
             dma("Y", T.ya[:, :], T.Af[:, :], [R("Af")], [], 2000)
         else:
             act(R("A"), R("v"), bias=-MAGIC)
-        tt(R("w1"), R("mi"), R("cf"), mu_)
-        ts(R("y", 8, 16), R("cf"), 37.0, mu_, R("ecol"), ad)
-        ts(R("w2"), R("w1"), 4, sh)
-        tt(R("w1"), R("w2"), R("y", 8, 16), ad)
-        ts(R("ci"), R("w1"), 4095, an)
         prep(t + 1)
-        differ(R("bR"), R("pH", 384, 512))
-        rest3()
-        write(R("pH", 0, 128), R("bR"), R("land2", 8 * t, 8 * t + 8), R("pH", 384, 512))
+        mms([(R("pF", 64, 128), R("nif"), R("ol3"), True, False), (R("pF", 64, 128), R("idf"), R("land2", 72 * t, 72 * t + 64), False, True)])
+        act(R("dif"), R("pF", 64, 128))
+        cp(R("tg3", 0, 4), R("land2", 72 * t + 64, 72 * t + 68))
+        onehot(R("pE", 0, 128, 1, 0, 64), 64, R("pF", 0, 64))
+        tt(R("tt", 0, 64), R("pF", 0, 64), R("dif"), mu_)
+        tt(ind(Iw, R("tg3", 0, 4)), R("tt", 0, 64), R("ol3"), ad)
     dma("Y", T.yg[:, :], T.cR[0:128:16, :], [R("cR")], [], 2000)
     for j in list(range(N16, 16)) + list(range(N16)):
         o = R("pA", 0, 256)
@@ -531,8 +563,7 @@ def build(g, core, T, topo):
             mms([(o, R("Zh", 15 - j, 143 - j), R("Ih", 256 * j, 256 * j + 256), False, j == N16 - 1)])
         else:
             mms([(o, R("Zf", 15 - j, 143 - j), R("Iw", 256 * j, 256 * j + 256), j == N16, False)])
-    ts(col("x", 0), P(0), float(N16), A_.is_lt, 136.0 * 2048, mu_)
-    ts(R("ycs"), R("pA", 0, 256), col("x", 0), ad)
+    ts(R("ycs"), R("pA", 0, 256), P(14), ad)
     dma("Y", T.yc[:, :], T.ycs[:, :], [R("ycs")], [], 2000)
     return ops, nsent[0]
 
@@ -615,22 +646,23 @@ def schedule(ops):
         pre[i] = near
         for j, h in near:
             suc[j].append((i, h))
+    for i, o in enumerate(ops):
+        if o["kind"] == "a":
+            pre[i] = [(j, h) for j, h in pre[i]]
     state = [SEED * 2654435761 % (1 << 31) + 1]
 
     def rand():
         state[0] = state[0] * 48271 % 2147483647
         return state[0] / 2147483647.0
-    best = walk = None
+    best = None
     seq = topo_order(n, pre, suc, list(range(n)))
     for it in range(PASSES):
         st = place(ops, seq, pre, False)
         end = max(st[i] + ops[i]["cost"] + ops[i]["lat"] for i in range(n))
         if best is None or end < best[1]:
             best = (st, end)
-        if walk is None or end < walk[1] + HEAT * (1.0 - it / PASSES):
-            walk = (st, end)
         elif it % 2 == 0:
-            st = walk[0]
+            st = best[0]
         fin = [st[i] + ops[i]["cost"] + ops[i]["lat"] for i in range(n)]
         c, w, a = rand() * best[1], 3000 + 12000 * rand(), NOISE * rand() * (it % 2 == 0)
         bt = place(ops, topo_order(n, suc, pre, [-f + (a * rand() if abs(f - c) < w else 0.0) for f in fin]), suc, True)
@@ -643,45 +675,7 @@ def schedule(ops):
             if end <= best[1]:
                 best = (st, end)
             t0 += WIDE / 2
-    st, end = best
-    cur = best
-    dur = [o["cost"] + o["lat"] for o in ops]
-    arcs = None
-    for it in range(MOVES):
-        s = cur[0]
-        if arcs is None:
-            ends = {(o["eng"], round(s[i] + o["cost"], 3)): i for i, o in enumerate(ops) if o["eng"] != "-"}
-            arcs, todo, met = [], [max(range(n), key=lambda i: s[i] + dur[i])], set()
-            while todo:
-                b = todo.pop()
-                if b in met:
-                    continue
-                met.add(b)
-                bind = [j for j, h in pre[b] if abs(s[j] + dur[j] + h - s[b]) < 0.01]
-                a = ends.get((ops[b]["eng"], round(s[b], 3)))
-                if not bind and a is not None:
-                    arcs.append((a, b)); bind = [a]
-                todo += bind
-        if not arcs:
-            break
-        key = list(s)
-        a, b = arcs[int(rand() * len(arcs))]
-        if rand() < 0.5:
-            key[a] = s[b] + 1.0 + (rand() < 0.5) * 3000.0 * rand()
-        else:
-            todo, lim = [b], s[a] - 1.0 - (rand() < 0.5) * 3000.0 * rand()
-            while todo:
-                k = todo.pop()
-                if key[k] > lim:
-                    key[k] = lim - 1e-3 * (n - k) / n
-                    todo += [j for j, _h in pre[k]]
-        s2 = place(ops, topo_order(n, pre, suc, key), pre, False)
-        e2 = max(s2[i] + dur[i] for i in range(n))
-        if e2 <= cur[1] + HEAT * (1.0 - it / MOVES) * rand():
-            cur, arcs = (s2, e2), None
-            if e2 < end:
-                st, end = cur
-    REPORT["order"] = (topo_order(n, pre, suc, st), end, st)
+    REPORT["order"] = (topo_order(n, pre, suc, best[0]), best[1], best[0])
     return REPORT["order"]
 
 

@@ -1,15 +1,16 @@
 from concourse.mybir import AluOpType, AxisListType, ActivationFunctionType
 
 RO = 4
-NV = 72
+NV = 68
 NS = 128 - NV
-NA = 10
-NE = 4
-NB2 = 0
+NA = 12
+NE = 2
 NG2 = 0
 EARLY = 0
-DCUT = 2
+DCUT = 3
 SPLIT = True
+TURN = "CDEB"
+EBV = True
 N16 = 13
 FILL = 2816
 SLOT = 448
@@ -30,22 +31,22 @@ _S = {
     "LmB": (128, B), "LF": (1024, B), "Lsig": (128, B), "Ldel": (128, B), "RE": (16, B), "Kc": (128, H), "K128": (8, B),
     "mT": (128, F), "QS": (8, F), "EXPL": (8, U), "dmin": (128, F), "dmax": (128, F), "k15": (128, F), "key": (128, F), "ch": (8, H),
     "s16": (128, F), "ltile": (8, F), "dump": (8, F), "dum3": (8, F), "Lt": (2048, B), "nEr": (2048, B), "idf": (128, F), "nif": (128, F),
-    "k2": (128, B), "k2048": (128, B), "B32": (8, B), "B16n": (8, B), "zero": (128, B),
+    "oldh": (256, H), "B32": (8, B), "B16n": (8, B), "zero": (128, B),
     "ci": (8, I32), "cf": (8, F), "cu": (8, U), "w1": (8, I32), "w2": (8, I32), "w3": (8, I32),
     "A": (128, B), "A16": (16 * NV, B), "Af": (128, F), "cR": (128, F), "cxR": (128, F), "aR": (128, F),
     "Og": (128, H), "Og4": (512, H), "sc4": (128, F), "sa": (64, F), "sb": (64, F), "OL": (32, F), "OLu": (32, U), "OSu": (32, U),
     "Cu": (512, U), "CuS": (4 * NS, U), "Ch": (384, H), "D": (64 * NV, B), "Rl": (64 * NV, B), "GS": (64 * NS, B),
     "near": (512, B), "hn": (24, F), "hd": (24, F), "hs": (24, F), "fou": (8, U), "Fh": (128, H),
     "Xab": (1536, F), "E": (1536, B), "z": (384, B),
-    "sk": (128, F), "lT": (128, F), "sv": (64, F), "y": (112, F), "mk": (8, I32), "mi": (8, I32), "lrn": (8, B), "lk": (8, B), "mh": (8, H),
+    "sk": (128, F), "lT": (128, F), "sv": (64, F), "y": (112, F), "mk": (8, I32), "mi": (8, I32), "lrn": (8, B), "lk": (8, B), "mh": (16, H),
     "v": (128, F), "mu": (8, U), "posu": (8, U), "selu": (8, U), "ecol": (1, F), "vs": (8, F), "Ea": (1024, B), "Eb": (256, B),
-    "tg2": (8, U), "tg3": (8, U), "C2u": (128, U), "old": (128, F), "Xc": (128, B), "G2": (2048, B), "ab": (2048, B), "oh": (128, B),
+    "tg2": (8, U), "C2u": (128, U), "old": (128, F), "Xc": (128, B), "G2": (2048, B), "ab": (2048, B), "oh": (128, B),
     "C3u": (64, U), "ol3": (64, F), "X3": (64, B), "G3": (1024, B), "a3": (1024, B), "ohs": (128, F),
     "dif": (64, F), "tt": (128, F), "u": (128, F), "au": (128, F),
-    "pairs": (SLOT * RO, F), "msg1": (8 * RO, U), "land1": (8 * RO, U), "land2": (72 * RO, F),
+    "pairs": (SLOT * RO, F), "msg1": (8 * RO, U), "land1": (8 * RO, U), "land2": (64 * RO, F), "msg3": (8 * RO, U), "land3": (8 * RO, U),
 }
 ALIAS = {}
-for _p, _d, _l in (("kb", B, "Z1 Z2 Zm Zi idb nid bid BO nBO ones LmB B16 B32 B16n RE K128 k2 k2048"), ("kf", F, "dmin dmax mT ltile dump dum3 QS c8 cg")):
+for _p, _d, _l in (("kb", B, "Z1 Z2 Zm Zi idb nid bid BO nBO ones LmB B16 B32 B16n RE K128"), ("kf", F, "dmin dmax mT ltile dump dum3 QS c8 cg")):
     _o = 0
     for _k in _l.split():
         ALIAS[_k] = (_p, _o, _S[_k][0]); _o += _S.pop(_k)[0]
@@ -54,14 +55,21 @@ SCRATCH = {k: ("sbuf", [128, v[0]], v[1]) for k, v in _S.items()}
 for _b in "ABCDEFGH":
     SCRATCH["p" + _b] = ("psum", [128, 512], F)
 NDMA = 15
-SEMAPHORES = ["cV", "cS", "cP", "cG", "sent"] + ["d%d" % i for i in range(NDMA)] + ["a%d" % i for i in range(2 * RO)]
+SEMAPHORES = ["cV", "cS", "cP", "cG", "sent"] + ["d%d" % i for i in range(NDMA)] + ["a%d" % i for i in range(3 * RO)]
 CNT = {"V": "cV", "S": "cS", "P": "cP", "G": "cG"}
-CY, GA, SCA, PE, HOP = 1.04, 1.62, 3.95, 0.52, 110.0
+CY, GA, SCA, PE = 1.04, 1.62, 3.95, 0.52
+HOP = 110.0
 LAT1 = 2500.0
 LAT2 = 3000.0
-SWEEPS = 4
+LAT3 = 3300.0
+SWEEPS = 5
 WIDE = 14000.0
-TRIES = 300
+TRIES = 200
+WIDE2 = 12000.0
+STEPS = 4000
+TIE = 0.02
+REACH = 8
+HEAT = 300.0
 SEED = 1
 PASSES = 30
 NOISE = 3000.0
@@ -213,9 +221,9 @@ def build(g, core, T, topo):
         rid, pid, _se = topo.addr(peer)
         msk = sum(1 << e for e in eng)
         nsent[0] += len(eng)
-        s = "a%d" % (2 * t + k)
+        s = "a%d" % (3 * t + k)
         i = add("G", [lambda: g.remote_dma(ap(dst), ap(src), T.sem[s], T.sem.sent, pid, rid, msk)], [src], [], 300.0, "r")
-        return add("-", [], [], [dst], 0.0, "a", (LAT1, LAT2)[k], after=[i], sem=(s, len(topo.engines(back, core)[:8])))
+        return add("-", [], [], [dst], 0.0, "a", (LAT1, LAT2, LAT3)[k], after=[i], sem=(s, len(topo.engines(back, core)[:8])))
 
     col = lambda b, j: R(b, j, j + 1)
     eq, mu_, ad, sb = A_.is_equal, A_.mult, A_.add, A_.subtract
@@ -272,7 +280,7 @@ def build(g, core, T, topo):
     ts(R("QS"), R("cc", 0, 8), P(1), eq)
     for nm, w in (("B16", 16.0), ("B32", 32.0), ("B16n", -16.0)):
         act(R(nm), R("QS"), scale=w)
-    iota(R("ones"), [[0, 128]], 1, 0); iota(R("k2"), [[0, 128]], 2, 0); iota(R("k2048"), [[0, 128]], -2048, 0)
+    iota(R("ones"), [[0, 128]], 1, 0); ts(R("oldh", 128, 256), R("zero"), 2.0, ad)
     iota(R("Iw", 4096, 4224), [[0, 128]], 0, 0)
     for t in range(RO):
         iota(R("pairs", SLOT * t, SLOT * t + 128), [[-4096, 2], [1, 64]], 4096, 0)
@@ -316,8 +324,7 @@ def build(g, core, T, topo):
         ts(R("ch"), R("ci"), -2048.0, ad)
         if t < RO:
             cp(R("cu"), R("ci"))
-        mms([(R("pH", 256, 384), R("idb"), R("zero"), True, False)] +
-            [(R("pH", 256 + r, 384, 16), mat("nEr", r), R("ch"), False, r == 15) for r in range(16)])
+        mms([(R("pH", 256 + r, 384, 16), mat("nEr", r), R("ch"), r == 0, r == 15) for r in range(16)])
         if t == RO:
             act(R("cR"), R("pH", 256, 384), bias=2048.0, scale=-1.0)
             return
@@ -355,34 +362,27 @@ def build(g, core, T, topo):
         cp(R("C2u"), ind(Iw, lst))
         act(R("Xc"), ind(Pw, lst))
         act(R("old"), ind(Iw, lst))
+        ts(R("oldh", 0, 128), R("C2u"), -2048.0, ad)
         for h in range(4):
             (cp if h < NG2 else act)(R("G2", 512 * h, 512 * h + 512), ind(Pw, R("C2u", 32 * h, 32 * h + 32)))
 
         def bank(b, pb):
-            rows = range(4 * b, 4 * b + 4)
-            if b < NB2:
-                mms(grp(R(pb, 0, 128), [(R("idb"), R("Xc"))]))
-                for p in rows:
-                    tt(mat("ab", p), R("G2", p, 2048, 16), R(pb, 0, 128), A_.max)
-            else:
-                mms([x for p in rows for x in grp(mat(pb, p % 4), [(R("nid"), R("Xc")), (R("idb"), R("G2", p, 2048, 16))])])
-                act(R("ab", 512 * b, 512 * b + 512), R(pb), AF.Abs)
+            h, p0 = b // 2, 8 * (b % 2)
+            mms([(R(pb, p, 512, 8), R("nid"), R("Xc", 64 * h, 64 * h + 64), p == 0, False) for p in range(8)])
+            mms([(R(pb, p, 512, 8), R("idb"), R("G2", 1024 * h + p0 + p, 1024 * h + 1024, 16), False, p == 7) for p in range(8)])
+            o = R("ab", 128 * p0 + 512 * h, 128 * p0 + 512 * h + 512)
+            act(o, R(pb), AF.Abs)
 
         def first():
             for b in range(EARLY):
-                bank(3 - b, "p" + "DE"[b % 2])
+                bank(b, "p" + "DE"[b % 2])
 
         def rest():
             for b in range(EARLY, 4):
-                bank(3 - b, "p" + "CDEF"[b])
-            lin = range(4 * NB2)
-            if lin:
-                mms([(R("pB", p, 128, 16), R(x, p if x == "G2" else 0, 2048 if x == "G2" else 128, 16 if x == "G2" else 1), R("B16n"), p == 0 and x == "Xc", False)
-                     for x in ("Xc", "G2") for p in lin])
-            for b in (3, 2, 1, 0):
-                mms([(R("pB", p, 128, 16), mat("ab", p), R("B32" if p in lin else "B16"), p == 12 and not lin, p == 3) for p in range(4 * b, 4 * b + 4)])
+                bank(b, "p" + "CDEF"[b])
+            for p0 in (0, 8):
+                mms([(R("pB", p0 + p, 128, 16), R("ab", 128 * p0 + p, 128 * p0 + 1024, 8), R("B16"), p0 + p == 0, p0 + p == 15) for p in range(8)])
             onehot(R("pB", 0, 128), 128, R("pB", 128, 256))
-            act(R("ohs"), R("pB", 128, 256))
         return first, rest
 
     def farthest3(lst):
@@ -417,10 +417,8 @@ def build(g, core, T, topo):
 
     def lowest(nq, eb, bank, c0, sc, tgt, spare, y0, out):
         w = 16 * nq
-        mms([(R(bank, c0, c0 + w), R("idb"), R("zero", 0, w), True, False)])
-        for q in range(nq - 1):
-            mms([(R(bank, c0 + 16 + 16 * q, c0 + w), R("BO"), R(eb, (w + 16) * q + 16, w * q + w), False, False)])
-        mms([(R(bank, c0 + r, c0 + w, 16), mat("Lt", r), R(eb, r, w * nq, w + 16), False, r == 15) for r in range(16)])
+        mms([(R(bank, c0 + r, c0 + w, 16), mat("Lt", r), R(eb, r, w * nq, w + 16), r == 0, False) for r in range(16)])
+        mms([(R(bank, c0 + 16 + 16 * q, c0 + w), R("BO"), R(eb, (w + 16) * q + 16, w * q + w), False, q == nq - 2) for q in range(nq - 1)])
         scan(R(sc, 0, w), R("s16", 0, w), R(bank, c0, c0 + w), ad, A_.min)
         y = R("y", y0, y0 + nq)
         ts(y, R(sc, 15, w, 16), P(10), ad, 8192.0, mu_)
@@ -430,7 +428,7 @@ def build(g, core, T, topo):
     prep(0)
     for t in range(RO):
         now[0] = t
-        chain([cp(R("CuS"), ind(Iw, R("OSu", 0, NS // 4))), cp(R("Cu"), ind(Iw, R("OLu")))])
+        chain([cp(R("CuS", 0, 32), ind(Iw, R("OSu", 0, 2))), cp(R("CuS", 32, 4 * NS), ind(Iw, R("OSu", 2, NS // 4))), cp(R("Cu"), ind(Iw, R("OLu")))])
         first2, rest2 = farthest2()
         first2()
         ch = []
@@ -476,15 +474,15 @@ def build(g, core, T, topo):
         tt(R("y", 16, 24), R("y", 16, 24), R("y", 88, 96), A_.max)
         ts(R("y", 24, 32), R("y", 8, 16), 1.0, A_.min, BIG + 18 * STEP, mu_)
         cnt = [R("pG", 0, 128), R("pG", 128, 256), R("pA", 0, 128)]
-        for j in range(3):
-            mms([(R("p" + "CDE"[j], 0, 384), R("Lsig"), R("Ch"), True, False)])
+        for j in range(len(TURN)):
+            mms([(R("p" + TURN[j], 0, 384), R("Lsig"), R("Ch"), True, False)])
         for j in range(8):
             if j == 0:
                 mms([(cnt[k], mat("near", k + 1), R("nBO"), k != 1, False) for k in range(3)])
             if j == 4:
                 mms([(R("pH", 128, 256), R("ones"), R("Kc"), True, False), (R("pH", 128, 256), R("Fh"), R("idb"), False, False)])
-            pb = "p" + "CDE"[j % 3]; h = 384 * (j % 4)
-            if j >= 3:
+            pb = "p" + TURN[j % len(TURN)]; h = 384 * (j % 4)
+            if j >= len(TURN):
                 mms([(R(pb, 0, 384), R("Lsig"), R("Ch"), True, False)])
             mms([(R(pb, 128 * k, 128 * k + 128), mat("LF", j), R("Fh"), False, k == 2) for k in range(3)])
             act(R("Xab", h, h + 384), R(pb, 0, 384), AF.Abs)
@@ -511,24 +509,32 @@ def build(g, core, T, topo):
         scan(R("sa"), R("s16", 0, 64), R("pairs", s0, s0 + 64), ad, A_.min)
         ts(R("msg1", 8 * t, 8 * t + 4), R("sa", 15, 64, 16), P(9), ad)
         send(t, 0, R("msg1", 8 * t, 8 * t + 4), R("land1", 8 * t, 8 * t + 4))
-        rest2()
-        ts(R("mh"), R("mi"), -2048.0, ad)
-        mms([(R("pA", 128, 256), R("idf"), R("old"), True, False), (R("pA", 128, 256), R("idb"), R("k2048"), False, False)])
-        mms([(R("pA", 128 + r, 256, 16), mat("nEr", r), R("mh"), False, r == 15) for r in range(16)])
-        late.pop()()
-        lowest(8, "Ea", "pB", 256, "sc4", R("cf"), R("dump"), 48, R("y", 48, 56))
-        ts(R("tg2"), R("y", 48, 56), 2048.0, ad)
-        tt(R("tt"), R("pA", 128, 256), R("ohs"), mu_)
-        tt(ind(Iw, R("tg2")), R("old"), R("tt"), sb)
-        act(R("vs", 0, 4), R("sa", 15, 64, 16), bias=P(9))
-        alike(R("pairs", s0, s0 + 64), R("vs"), None, 4, "Eb", -1.0)()
-        cp(ind(R("pairs", s0 + 64, s0 + SLOT), R("posu")), R("cxR"))
-        lowest(4, "Eb", "pG", 128, "sb", R("vs", 0, 4), R("dum3", 0, 4), 64, R("pairs", s0 + 128, s0 + 132))
-        send(t, 1, R("pairs", s0 + 64, s0 + 132), R("land2", 72 * t, 72 * t + 68))
-        farthest3(R("land1", 8 * t, 8 * t + 4))
         mms(grp(R("pH", 56, 64), [(R("ones"), R("lrn"))]))
         add("S", [lambda: g.scalar.activation(ap(R("y", 104, 112)), ap(R("pH", 56, 64)), AF.Identity, bias=256.0, accum_out=ap(R("ecol")))],
             [R("pH", 56, 64)], [R("y", 104, 112), R("ecol")], 90.0)
+        rest2()
+        ts(R("mh", 0, 8), R("mi"), -2048.0, ad)
+        tt(R("mh", 8, 16), R("mk"), R("y", 24, 32), A_.is_lt)
+        mms([(R("pA", 128, 384), R("idb"), R("oldh"), True, False)])
+        mms([(R("pA", 128 + r, 384, 16), mat("nEr", r), R("mh"), False, r == 15) for r in range(16)])
+        act(R("ohs"), R("pA", 128, 256))
+        late.pop()()
+        lowest(8, "Ea", "pG", 128, "sc4", R("cf"), R("dump"), 48, R("y", 48, 56))
+        ts(R("tg2"), R("y", 48, 56), 2048.0, ad)
+        tt(R("tt"), R("pB", 128, 256), R("ohs"), mu_)
+        tt(ind(Iw, R("tg2")), R("old"), R("tt"), sb)
+        act(R("vs", 0, 4), R("sa", 15, 64, 16), bias=P(9))
+        if EBV:
+            for q in range(4):
+                ts(R("Eb", 80 * q, 64 * q + 64), R("pairs", s0 + 16 * q, s0 + 64), col("vs", q), eq)
+        else:
+            alike(R("pairs", s0, s0 + 64), R("vs"), None, 4, "Eb", -1.0)()
+        cp(ind(R("pairs", s0 + 64, s0 + SLOT), R("posu")), R("cxR"))
+        send(t, 1, R("pairs", s0 + 64, s0 + 128), R("land2", 64 * t, 64 * t + 64))
+        lowest(4, "Eb", "pH", 64, "sb", R("vs", 0, 4), R("dum3", 0, 4), 64, R("y", 64, 68))
+        cp(R("msg3", 8 * t, 8 * t + 4), R("y", 64, 68))
+        send(t, 2, R("msg3", 8 * t, 8 * t + 4), R("land3", 8 * t, 8 * t + 4))
+        farthest3(R("land1", 8 * t, 8 * t + 4))
         act(R("y", 8, 16), R("cf"), bias=R("ecol"), scale=37.0)
         tt(R("w1"), R("mi"), R("ci"), mu_)
         ts(R("w2"), R("w1"), 4, sh)
@@ -539,9 +545,7 @@ def build(g, core, T, topo):
         cp(R("selu"), R("y", 0, 8))
         tt(R("u"), ind(R("Pw"), R("selu")), R("A"), ad)
         act(R("au"), R("u"), AF.Abs, scale=0.4995)
-        mms([(R("pH", 384, 512), R("idb"), R("k2"), True, False)] +
-            [(R("pH", 384 + r, 512, 16), mat("nEr", r), R("lrn"), False, r == 15) for r in range(16)])
-        tt(R("v"), R("au"), R("pH", 384, 512), mu_)
+        tt(R("v"), R("au"), R("pA", 256, 384), mu_)
         act(R("v"), R("v"), bias=MAGIC)
         if t == RO - 1:
             act(R("Af"), R("v"), bias=-MAGIC)
@@ -549,12 +553,11 @@ def build(g, core, T, topo):
         else:
             act(R("A"), R("v"), bias=-MAGIC)
         prep(t + 1)
-        mms([(R("pF", 64, 128), R("nif"), R("ol3"), True, False), (R("pF", 64, 128), R("idf"), R("land2", 72 * t, 72 * t + 64), False, True)])
+        mms([(R("pF", 64, 128), R("nif"), R("ol3"), True, False), (R("pF", 64, 128), R("idf"), R("land2", 64 * t, 64 * t + 64), False, True)])
         act(R("dif"), R("pF", 64, 128))
-        cp(R("tg3", 0, 4), R("land2", 72 * t + 64, 72 * t + 68))
         onehot(R("pE", 0, 128, 1, 0, 64), 64, R("pF", 0, 64))
         tt(R("tt", 0, 64), R("pF", 0, 64), R("dif"), mu_)
-        tt(ind(Iw, R("tg3", 0, 4)), R("tt", 0, 64), R("ol3"), ad)
+        tt(ind(Iw, R("land3", 8 * t, 8 * t + 4)), R("tt", 0, 64), R("ol3"), ad)
     dma("Y", T.yg[:, :], T.cR[0:128:16, :], [R("cR")], [], 2000)
     for j in list(range(N16, 16)) + list(range(N16)):
         o = R("pA", 0, 256)
@@ -595,6 +598,8 @@ def window(ops, pre, suc, st, t0, t1, passes, rand):
         return st
     seq = topo_order(m, p2, s2, [st[i] for i in w])
     best = None
+    if passes < 0:
+        best = anneal(sub, seq, p2, s2, rel, out, free, qe, -passes, rand)
     for it in range(passes):
         s = place(sub, seq, p2, False, rel, free)
         v = max(max(s[k] + dur[i] + out[k], s[k] + sub[k]["cost"] + qe.get(sub[k]["eng"], 0.0)) for k, i in enumerate(w))
@@ -609,6 +614,156 @@ def window(ops, pre, suc, st, t0, t1, passes, rand):
     for k, i in enumerate(w):
         key[i] = max(t0, best[0][k])
     return place(ops, topo_order(n, pre, suc, key), pre, False)
+
+
+def tabu(ops, seq, pre, suc, rel, out, free, qe, steps, rand):
+    n = len(ops)
+    c = [o["cost"] for o in ops]
+    d = [o["cost"] + o["lat"] for o in ops]
+    pa = [[(j, d[j] + h) for j, h in pre[i]] for i in range(n)]
+    sa = [[(j, d[i] + h) for j, h in suc[i]] for i in range(n)]
+    fixed = [set(j for j, _h in suc[i]) for i in range(n)]
+    before, after, last = [-1] * n, [-1] * n, {}
+    for i in seq:
+        e = ops[i]["eng"]
+        if e != "-":
+            if e in last:
+                before[i] = last[e]; after[last[e]] = i
+            last[e] = i
+    r0 = [max(rel[i], free.get(ops[i]["eng"], 0.0)) for i in range(n)]
+    q0 = [max(d[i] + out[i], c[i] + qe.get(ops[i]["eng"], 0.0)) for i in range(n)]
+    deg = [len(p) for p in pre]
+    best, banned, since = None, {}, 0
+    for it in range(steps):
+        left = [deg[i] + (before[i] >= 0) for i in range(n)]
+        order = [i for i in range(n) if not left[i]]
+        r = list(r0)
+        for i in order:
+            ri = r[i]
+            for j, w in sa[i]:
+                if ri + w > r[j]:
+                    r[j] = ri + w
+                left[j] -= 1
+                if not left[j]:
+                    order.append(j)
+            j = after[i]
+            if j >= 0:
+                if ri + c[i] > r[j]:
+                    r[j] = ri + c[i]
+                left[j] -= 1
+                if not left[j]:
+                    order.append(j)
+        q = list(q0)
+        for i in reversed(order):
+            v = q[i]
+            for j, w in sa[i]:
+                if w + q[j] > v:
+                    v = w + q[j]
+            j = after[i]
+            if j >= 0 and c[i] + q[j] > v:
+                v = c[i] + q[j]
+            q[i] = v
+        end = max(r[i] + q[i] for i in range(n))
+        since += 1
+        if best is None or end < best[1] - 0.01:
+            best, since = (r, end, list(before), list(after)), 0
+        elif since > STALL:
+            before, after, since, banned = list(best[2]), list(best[3]), 0, {}
+            continue
+        pick = None
+        for u in range(n):
+            v = after[u]
+            if v < 0 or r[u] + q[u] < end - 0.01 or r[u] + c[u] + q[v] < end - 0.01 or v in fixed[u]:
+                continue
+            a, b = before[u], after[v]
+            rv = max([r0[v], r[a] + c[a] if a >= 0 else 0.0] + [r[j] + w for j, w in pa[v]])
+            ru = max([r0[u], rv + c[v]] + [r[j] + w for j, w in pa[u]])
+            qu = max([q0[u], c[u] + q[b] if b >= 0 else 0.0] + [w + q[j] for j, w in sa[u]])
+            qv = max([q0[v], c[v] + qu] + [w + q[j] for j, w in sa[v]])
+            val = max(rv + qv, ru + qu)
+            if banned.get((u, v), -1) > it and val >= best[1]:
+                val += 1e6
+            val += JITTER * rand()
+            if pick is None or val < pick[0]:
+                pick = (val, u, v)
+        if pick is None:
+            break
+        _val, u, v = pick
+        a, b = before[u], after[v]
+        if a >= 0:
+            after[a] = v
+        if b >= 0:
+            before[b] = u
+        before[v], after[v], before[u], after[u] = a, u, v, b
+        banned[(v, u)] = it + 8 + int(12 * rand())
+    return best
+
+
+def anneal(ops, seq, pre, suc, rel, out, free, qe, steps, rand):
+    n = len(ops)
+    c = [o["cost"] for o in ops]
+    d = [o["cost"] + o["lat"] for o in ops]
+    sa = [[(j, d[i] + h) for j, h in suc[i]] for i in range(n)]
+    r0 = [max(rel[i], free.get(ops[i]["eng"], 0.0)) for i in range(n)]
+    q0 = [max(d[i] + out[i], c[i] + qe.get(ops[i]["eng"], 0.0)) for i in range(n)]
+    deg = [len(p) for p in pre]
+    qs = {}
+    for i in seq:
+        if ops[i]["eng"] != "-":
+            qs.setdefault(ops[i]["eng"], []).append(i)
+
+    def times():
+        left, after = list(deg), [-1] * n
+        for l in qs.values():
+            for a, b in zip(l, l[1:]):
+                after[a] = b; left[b] += 1
+        order = [i for i in range(n) if not left[i]]
+        r, by = list(r0), [-1] * n
+        for i in order:
+            ri = r[i]
+            for j, w in sa[i]:
+                if ri + w > r[j]:
+                    r[j] = ri + w; by[j] = i
+                left[j] -= 1
+                if not left[j]:
+                    order.append(j)
+            j = after[i]
+            if j >= 0:
+                if ri + c[i] > r[j]:
+                    r[j] = ri + c[i]; by[j] = i
+                left[j] -= 1
+                if not left[j]:
+                    order.append(j)
+        if len(order) < n:
+            return None
+        i = max(range(n), key=lambda x: r[x] + q0[x])
+        return r, r[i] + q0[i] + TIE * sum(r) / n, by, i, after
+    cur = best = times()
+    held = None
+    for it in range(steps):
+        if held is None:
+            held, i = [], cur[3]
+            while cur[2][i] >= 0:
+                if cur[4][cur[2][i]] == i:
+                    held.append((cur[2][i], i))
+                i = cur[2][i]
+        if not held:
+            break
+        a, b = held[int(rand() * len(held))]
+        l = qs[ops[a]["eng"]]
+        x = a if rand() < 0.5 else b
+        k = l.index(x)
+        s = 1 + int(REACH * rand() ** 2)
+        k2 = min(len(l) - 1, k + s) if x == a else max(0, k - s)
+        l.insert(k2, l.pop(k))
+        new = times()
+        if new is not None and new[1] <= cur[1] + HEAT * (1.0 - it / steps) * rand() ** 3:
+            cur, held = new, None
+            if new[1] < best[1]:
+                best = new
+        else:
+            l.insert(k, l.pop(k2))
+    return best
 
 
 def place(ops, seq, pre, back, rel=None, free=None):
@@ -641,14 +796,18 @@ def schedule(ops):
         return REPORT["order"]
     n = len(ops)
     pre = [[] for _ in ops]; suc = [[] for _ in ops]
+    reach = [0] * n
     for i, o in enumerate(ops):
-        near = [(j, HOP) for j in o["hard"]] + [(j, -ops[j]["lat"]) for j in o["soft"]]
+        far = 0
+        for j in o["hard"]:
+            far |= reach[j]
+        near = [(j, HOP) for j in o["hard"] if ops[j]["lat"] or not far >> j & 1] + [(j, -ops[j]["lat"]) for j in o["soft"] if not far >> j & 1]
+        for j in o["hard"]:
+            far |= 1 << j
+        reach[i] = far
         pre[i] = near
         for j, h in near:
             suc[j].append((i, h))
-    for i, o in enumerate(ops):
-        if o["kind"] == "a":
-            pre[i] = [(j, h) for j, h in pre[i]]
     state = [SEED * 2654435761 % (1 << 31) + 1]
 
     def rand():
@@ -668,13 +827,14 @@ def schedule(ops):
         bt = place(ops, topo_order(n, suc, pre, [-f + (a * rand() if abs(f - c) < w else 0.0) for f in fin]), suc, True)
         seq = topo_order(n, pre, suc, [-(bt[i] + ops[i]["cost"]) + (a * rand() if abs(fin[i] - c) < w else 0.0) for i in range(n)])
     for it in range(SWEEPS):
-        t0 = -WIDE * rand()
-        while t0 < best[1]:
-            st = window(ops, pre, suc, best[0], t0, t0 + WIDE, TRIES, rand)
-            end = max(st[i] + ops[i]["cost"] + ops[i]["lat"] for i in range(n))
-            if end <= best[1]:
-                best = (st, end)
-            t0 += WIDE / 2
+        for wide, tries in ((WIDE, TRIES), (WIDE2, -STEPS)):
+            t0 = -wide * rand()
+            while t0 < best[1] and tries:
+                st = window(ops, pre, suc, best[0], t0, t0 + wide, tries, rand)
+                end = max(st[i] + ops[i]["cost"] + ops[i]["lat"] for i in range(n))
+                if end <= best[1]:
+                    best = (st, end)
+                t0 += wide / 2
     REPORT["order"] = (topo_order(n, pre, suc, best[0]), best[1], best[0])
     return REPORT["order"]
 

from concourse.mybir import AluOpType, AxisListType, ActivationFunctionType

RO = 4
NV = 68
NS = 128 - NV
NA = 12
NE = 2
NG2 = 0
EARLY = 0
DCUT = 3
SPLIT = True
TURN = "CDEB"
EBV = True
N16 = 13
FILL = 2816
SLOT = 448
HUGE = float(1 << 26)
BK = 8192.0
STEP = 16384.0
BIG = 32 * STEP
FALL = BIG + STEP
MAGIC = 12582912.0

F, B, H, I32, U = "float32", "bfloat16", "float16", "int32", "uint16"
_S = {
    "Ii": (4096, I32), "Iw": (4224, F), "Pw": (8192, B), "alti": (4096, I32), "iox": (4096, F),
    "Ih": (256 * N16, H), "ycs": (256, F), "thi": (4, I32), "thf": (4, F), "thc": (4, F),
    "pi": (1, I32), "pt": (8, I32), "pc": (16, F), "c16": (128, F), "cg": (128, F), "cc": (144, F), "c8": (128, F), "ex": (48, F),
    "tm2": (128, F), "Z1": (144, B), "Z2": (144, B), "Zm": (144, B), "Zh": (144, B), "Zf": (144, F), "Zi": (144, B),
    "idb": (128, B), "nid": (128, B), "bid": (128, B), "BO": (128, B), "nBO": (128, B), "BOf": (128, F), "B16": (8, B), "ones": (128, B),
    "LmB": (128, B), "LF": (1024, B), "Lsig": (128, B), "Ldel": (128, B), "RE": (16, B), "Kc": (128, H), "K128": (8, B),
    "mT": (128, F), "QS": (8, F), "EXPL": (8, U), "dmin": (128, F), "dmax": (128, F), "k15": (128, F), "key": (128, F), "ch": (8, H),
    "s16": (128, F), "ltile": (8, F), "dump": (8, F), "dum3": (8, F), "Lt": (2048, B), "nEr": (2048, B), "idf": (128, F), "nif": (128, F),
    "oldh": (256, H), "B32": (8, B), "B16n": (8, B), "zero": (128, B),
    "ci": (8, I32), "cf": (8, F), "cu": (8, U), "w1": (8, I32), "w2": (8, I32), "w3": (8, I32),
    "A": (128, B), "A16": (16 * NV, B), "Af": (128, F), "cR": (128, F), "cxR": (128, F), "aR": (128, F),
    "Og": (128, H), "Og4": (512, H), "sc4": (128, F), "sa": (64, F), "sb": (64, F), "OL": (32, F), "OLu": (32, U), "OSu": (32, U),
    "Cu": (512, U), "CuS": (4 * NS, U), "Ch": (384, H), "D": (64 * NV, B), "Rl": (64 * NV, B), "GS": (64 * NS, B),
    "near": (512, B), "hn": (24, F), "hd": (24, F), "hs": (24, F), "fou": (8, U), "Fh": (128, H),
    "Xab": (1536, F), "E": (1536, B), "z": (384, B),
    "sk": (128, F), "lT": (128, F), "sv": (64, F), "y": (112, F), "mk": (8, I32), "mi": (8, I32), "lrn": (8, B), "lk": (8, B), "mh": (16, H),
    "v": (128, F), "mu": (8, U), "posu": (8, U), "selu": (8, U), "ecol": (1, F), "vs": (8, F), "Ea": (1024, B), "Eb": (256, B),
    "tg2": (8, U), "C2u": (128, U), "old": (128, F), "Xc": (128, B), "G2": (2048, B), "ab": (2048, B), "oh": (128, B),
    "C3u": (64, U), "ol3": (64, F), "X3": (64, B), "G3": (1024, B), "a3": (1024, B), "ohs": (128, F),
    "dif": (64, F), "tt": (128, F), "u": (128, F), "au": (128, F),
    "pairs": (SLOT * RO, F), "msg1": (8 * RO, U), "land1": (8 * RO, U), "land2": (64 * RO, F), "msg3": (8 * RO, U), "land3": (8 * RO, U),
}
ALIAS = {}
for _p, _d, _l in (("kb", B, "Z1 Z2 Zm Zi idb nid bid BO nBO ones LmB B16 B32 B16n RE K128"), ("kf", F, "dmin dmax mT ltile dump dum3 QS c8 cg")):
    _o = 0
    for _k in _l.split():
        ALIAS[_k] = (_p, _o, _S[_k][0]); _o += _S.pop(_k)[0]
    _S[_p] = (_o, _d)
SCRATCH = {k: ("sbuf", [128, v[0]], v[1]) for k, v in _S.items()}
for _b in "ABCDEFGH":
    SCRATCH["p" + _b] = ("psum", [128, 512], F)
NDMA = 15
SEMAPHORES = ["cV", "cS", "cP", "cG", "sent"] + ["d%d" % i for i in range(NDMA)] + ["a%d" % i for i in range(3 * RO)]
CNT = {"V": "cV", "S": "cS", "P": "cP", "G": "cG"}
CY, GA, SCA, PE = 1.04, 1.62, 3.95, 0.52
HOP = 110.0
LAT1 = 2500.0
LAT2 = 3000.0
LAT3 = 3300.0
SWEEPS = 5
WIDE = 14000.0
TRIES = 200
WIDE2 = 12000.0
STEPS = 4000
TIE = 0.02
REACH = 8
HEAT = 300.0
SEED = 1
PASSES = 30
NOISE = 3000.0
REPORT = {}


def _two(name):
    return name in _S and _S[name][1] in (B, H, U)


def build(g, core, T, topo):
    A_ = AluOpType
    AF = ActivationFunctionType
    ops, acc = [], {}
    nd = [0]
    now = [-1]

    def R(b, c0=0, c1=None, st=1, p0=0, p1=128):
        if b in ALIAS:
            return (ALIAS[b][0], ALIAS[b][1] + c0, ALIAS[b][1] + (ALIAS[b][2] if c1 is None else c1), st, p0, p1)
        return (b, c0, SCRATCH[b][1][1] if c1 is None else c1, st, p0, p1)

    def ind(w, o):
        return ("@", w, o)

    def ap(r):
        if r[0] == "@":
            return ap(r[1]).indirect(ap(r[2]))
        if r[3] == 1:
            return T[r[0]][r[4]:r[5], r[1]:r[2]]
        return T[r[0]][r[4]:r[5], r[1]:r[2]:r[3]]

    def n_of(r):
        return 16 * (r[2][2] - r[2][1]) if r[0] == "@" else (r[2] - r[1] + r[3] - 1) // r[3]

    def add(eng, fns, reads, writes, cost, kind="c", lat=0.0, after=(), sem=None):
        rd, wr = [], []
        for r in reads:
            if isinstance(r, tuple):
                rd += [r[1], r[2]] if r[0] == "@" else [r]
        for r in writes:
            if r[0] == "@":
                wr.append(r[1]); rd.append(r[2])
            else:
                wr.append(r)
        i = len(ops)
        hard, soft = set(), set(after)
        for r, w in [(r, False) for r in rd] + [(r, True) for r in wr]:
            ps = SCRATCH[r[0]][0] == "psum"
            for (j, c0, c1, wj, sj) in acc.get(r[0], []):
                ej = ops[j]["eng"]
                if ps:
                    if ej != eng or (eng != "P" and (w or wj)):
                        hard.add(j)
                    elif eng == "P":
                        soft.add(j)
                elif (w or wj) and c0 < r[2] and r[1] < c1 and not (sj == r[3] and (c0 - r[1]) % sj):
                    hard.add(j)
        for r, w in [(r, False) for r in rd] + [(r, True) for r in wr]:
            acc.setdefault(r[0], []).append((i, r[1], r[2], w, r[3]))
        ops.append(dict(round=now[0], eng=eng, fns=fns, hard=hard, soft=soft - hard, cost=cost, kind=kind, lat=lat, sem=sem, w=(wr or rd or [("",)])[0][0]))
        return i

    def vcost(out, ins, tt=False):
        if out[0] == "@":
            return 50 + n_of(out) * SCA
        if any(r[0] == "@" for r in ins):
            return 50 + n_of(out) * GA
        k = 1.0
        if tt:
            k = 1.0 if any(SCRATCH[r[0]][0] == "psum" for r in ins) else 2.0
        elif all(_two(r[0]) for r in ins + [out]):
            k = 0.5
        return max(64.0, n_of(ins[0] if ins else out) * k) * CY

    def sa(s):
        return ap(s) if isinstance(s, tuple) else s

    def cp(out, a):
        return add("V", [lambda: g.vector.tensor_copy(ap(out), ap(a))], [a], [out], vcost(out, [a]))

    def tt(out, a, b, op):
        return add("V", [lambda: g.vector.tensor_tensor(ap(out), ap(a), ap(b), op)], [a, b], [out], vcost(out, [a, b], True))

    def ts(out, a, s1, op0, s2=None, op1=None):
        if op1 is None:
            fn = lambda: g.vector.tensor_scalar(ap(out), ap(a), sa(s1), None, op0)
        else:
            fn = lambda: g.vector.tensor_scalar(ap(out), ap(a), sa(s1), sa(s2), op0, op1)
        return add("V", [fn], [a, s1, s2], [out], vcost(out, [a]))

    def scan(out, d0, d1, op0, op1, first=0.0):
        return add("V", [lambda: g.vector.tensor_tensor_scan(ap(out), ap(d0), ap(d1), first, op0, op1)], [d0, d1], [out], vcost(out, [d0, d1]))

    def mset(out, c):
        return add("V", [lambda: g.vector.memset(ap(out), c)], [], [out], vcost(out, []))

    def act_fn(out, a, f, bias, scale):
        return lambda: g.scalar.activation(ap(out), ap(a), f, bias=sa(bias), scale=sa(scale))

    def acost(out, a):
        return 65 + n_of(out) * GA if a[0] == "@" else max(64.0, n_of(out)) * CY

    def act(out, a, f=AF.Identity, bias=0.0, scale=1.0):
        return add("S", [act_fn(out, a, f, bias, scale)], [a, bias, scale], [out], acost(out, a))

    def acts(lst, after=()):
        return add("S", [act_fn(*x) for x in lst], [r for x in lst for r in (x[1], x[3], x[4])], [x[0] for x in lst],
                   sum(acost(x[0], x[1]) for x in lst), after=after)

    def chain(ids):
        for a, b in zip(ids, ids[1:]):
            if a not in ops[b]["hard"]:
                ops[b]["soft"].add(a)

    def mm_fn(o, l, r, s0, s1):
        return lambda: g.tensor.matmul(ap(o), ap(l), ap(r), s0, s1)

    def mms(lst):
        c = sum(max(min(64, n_of(x[1])), n_of(x[2])) * (4 if _S[x[1][0]][1] == F else 1) * PE for x in lst)
        return add("P", [mm_fn(*x) for x in lst], [r for x in lst for r in (x[1], x[2])], [x[0] for x in lst], c)

    def grp(out, prs):
        return [(out, l, r, i == 0, i == len(prs) - 1) for i, (l, r) in enumerate(prs)]

    def iota(out, pat, base, cm):
        if _S[out[0]][1] == I32:
            fn = lambda: g.iota(ap(out), pat, base, cm)
        else:
            fn = lambda: g.iota(ap(out), pat, base, cm, allow_small_or_imprecise_dtypes=True)
        return add("G", [fn], [], [out], 160 + 2 * n_of(out) * CY)

    def sel(out, a, pat, fill, base, cm):
        return add("G", [lambda: g.affine_select(ap(out), ap(a), pat, A_.not_equal, fill, base, cm)], [a], [out], 200 + 2 * n_of(out) * CY)

    def dma(q, o, i, reads, writes, lat):
        s = "d%d" % nd[0]; nd[0] += 1
        e = g.sync if q == "Y" else g.scalar
        return add(q, [lambda: e.dma_start(o, i)], reads, writes, 100.0, "d", lat, sem=s)

    rank = T.rank_of(core)
    n = len(T.cores)
    nsent = [0]

    def send(t, k, src, dst):
        peer = T.cores[(rank + 1 + t % (n - 1)) % n]
        back = T.cores[(rank - 1 - t % (n - 1)) % n]
        eng = topo.engines(core, peer)[:8]
        rid, pid, _se = topo.addr(peer)
        msk = sum(1 << e for e in eng)
        nsent[0] += len(eng)
        s = "a%d" % (3 * t + k)
        i = add("G", [lambda: g.remote_dma(ap(dst), ap(src), T.sem[s], T.sem.sent, pid, rid, msk)], [src], [], 300.0, "r")
        return add("-", [], [], [dst], 0.0, "a", (LAT1, LAT2, LAT3)[k], after=[i], sem=(s, len(topo.engines(back, core)[:8])))

    col = lambda b, j: R(b, j, j + 1)
    eq, mu_, ad, sb = A_.is_equal, A_.mult, A_.add, A_.subtract

    mset(R("alti", 0, FILL), 0)
    iota(R("alti", FILL, 4096), [[0, 4096 - FILL]], 0, 0)
    dma("Y", T.ci[:, :], T.gate[:, :], [], [R("ci")], 2000)
    dma("S", T.A[:, :], T.acc0[:, :], [], [R("A")], 2200)
    dma("S", T.thi[0:8, :], T.th[:, :], [], [R("thi")], 2200)
    for j in range(4):
        dma("Y", T.Ii[:, 1024 * j:1024 * j + 1024], T.icol[:, 1024 * j:1024 * j + 1024], [], [R("Ii", 1024 * j, 1024 * j + 1024)], 3000 + 1100 * j)
    fill = [0, 1]
    alts = [dma("Y", T.alti[k:128:16, :], T.alt[k:32:4, :], [], [], 4500) for k in range(4)]
    for i in alts:
        ops[i]["hard"].update(fill)
        acc["alti"].append((i, 0, 4096, True, 1))
    dma("Y", T.Pw[:, 0:4096], T.pat[:, :], [], [R("Pw", 0, 4096)], 6600)
    chain([i for i, o in enumerate(ops) if o["eng"] == "Y"])

    iota(R("pi"), [[0, 1]], 0, 1)
    iota(R("cc"), [[1, 144]], 0, 0)
    iota(R("cg"), [[1, 8], [0, 16]], 0, 0)
    iota(R("c16"), [[0, 8], [1, 16]], 0, 0)
    mset(R("zero"), 0.0)
    iota(R("c8"), [[0, 16], [1, 8]], 0, 0)
    for j in range(4):
        iota(R("iox", 1024 * j, 1024 * j + 1024), [[2, 512], [-1, 2]], 1024 * j + 1, 0)
    sh, an = A_.logical_shift_right, A_.bitwise_and
    for j, (s, m) in enumerate([(0, 15), (4, 7), (0, 127), (1, 7), (3, 15), (0, 1)]):
        ts(col("pt", j), R("pi"), s, sh, m, an)
    cp(R("pc", 0, 6), R("pt", 0, 6))
    P = lambda j: col("pc", j)
    act(P(6), P(2), bias=12.0)
    act(P(7), P(1), bias=15.0, scale=16.0)
    ts(P(8), P(0), 4.0, A_.is_lt)
    act(P(9), P(0), bias=15 * BK, scale=-BK)
    act(P(10), P(0), bias=15 * BK + 1, scale=-BK)
    act(P(12), P(0), bias=1.0)
    act(P(13), P(5), bias=1.0, scale=-2.0)
    ts(P(14), P(0), float(N16), A_.is_lt, 136.0 * 2048, mu_)
    c16 = R("c16", 0, 128)
    ts(R("BO"), R("cg"), P(1), eq)
    act(R("nBO"), R("BO"), scale=-1.0)
    ts(R("s16"), c16, P(0), eq, HUGE, mu_)
    act(R("mT"), R("s16"), scale=1.0 / HUGE)
    act(R("s16"), R("s16"), bias=-BK)
    ts(R("Z1"), R("cc"), P(7), eq)
    ts(R("Zi"), R("cc"), P(6), eq, P(8), mu_)
    for nm, w in (("Z2", 2.0), ("Zm", -1.0), ("Zh", P(12)), ("Zf", P(12))):
        act(R(nm), R("Z1"), scale=w)
    for nm, w in (("idb", 1.0), ("nid", -1.0), ("bid", BIG)):
        sel(R(nm), R("zero"), [[-1, 128]], w, 0, 1)
    ts(R("BOf"), R("cg"), P(2), eq)
    ts(R("QS"), R("cc", 0, 8), P(1), eq)
    for nm, w in (("B16", 16.0), ("B32", 32.0), ("B16n", -16.0)):
        act(R(nm), R("QS"), scale=w)
    iota(R("ones"), [[0, 128]], 1, 0); ts(R("oldh", 128, 256), R("zero"), 2.0, ad)
    iota(R("Iw", 4096, 4224), [[0, 128]], 0, 0)
    for t in range(RO):
        iota(R("pairs", SLOT * t, SLOT * t + 128), [[-4096, 2], [1, 64]], 4096, 0)
    iota(R("hn"), [[0, 24]], 0, 0)
    act(R("idf"), R("idb")); act(R("nif"), R("nid"))
    ts(R("ex", 0, 16), R("cc", 0, 16), P(0), eq)
    ts(R("ex", 16, 32), R("cc", 0, 16), P(0), A_.is_gt)
    tt(R("ex", 32, 48), R("ex", 16, 32), R("ex", 0, 16), sb)
    for h in range(4):
        acts([(R("Lt", 128 * r, 128 * r + 128), R("BO"), AF.Identity, 0.0, col("ex", 32 + r)) for r in range(4 * h, 4 * h + 4)])
        acts([(R("nEr", 128 * r, 128 * r + 128), R("nBO"), AF.Identity, 0.0, col("ex", r)) for r in range(4 * h, 4 * h + 4)])
    ts(R("tm2"), c16, P(0), A_.is_gt)
    tt(R("LmB"), R("tm2"), R("BO"), mu_)
    ts(R("tm2"), R("c8"), P(3), eq)
    tt(R("tm2"), R("tm2"), R("BO"), mu_)
    act(R("Lsig"), R("tm2"), scale=-1.0)
    act(R("Ldel"), R("tm2"), scale=P(13))
    pq = [[-16, 8], [-8, 2], [0, 8]]
    for j in range(8):
        sel(R("LF", 128 * j, 128 * j + 128), R("zero"), pq, 2.0, -j, 1)
    ts(R("RE"), R("cc", 0, 16), P(4), eq, 16.0, mu_)
    ts(R("EXPL"), R("cc", 0, 8), 16.0, mu_, 15.0, ad)
    ts(R("dmin"), c16, 0.0, eq, HUGE, mu_)
    act(R("dmax"), R("dmin"), bias=1.0, scale=-1.0)
    act(R("k15"), c16, bias=15.0, scale=-1.0)
    ts(R("Kc"), c16, STEP / 128, mu_, (BIG + 2 * STEP + 2048) / 128, ad)
    act(R("ltile"), R("cc", 0, 8), bias=P(0), scale=16.0)
    act(R("dump"), R("ltile"), bias=2048.0)
    act(R("dum3"), R("ltile"), bias=4160.0)
    act(R("K128"), R("ltile"), bias=128.0)
    cp(R("thf", p1=8), R("thi", p1=8))
    mms(grp(R("pH", 0, 4), [(R("BOf", p1=8), R("thf", p1=8))]))
    cp(R("thc"), R("pH", 0, 4))
    for j in range(8):
        cp(R("Iw", 512 * j, 512 * j + 512), R("Ii", 512 * j, 512 * j + 512))
    Iw = R("Iw"); Pw = R("Pw", 0, 4096)
    mat = lambda b, r: R(b, 128 * r, 128 * r + 128)
    late = []

    def prep(t):
        ts(R("ch"), R("ci"), -2048.0, ad)
        if t < RO:
            cp(R("cu"), R("ci"))
        mms([(R("pH", 256 + r, 384, 16), mat("nEr", r), R("ch"), r == 0, r == 15) for r in range(16)])
        if t == RO:
            act(R("cR"), R("pH", 256, 384), bias=2048.0, scale=-1.0)
            return
        ts(R("cf"), R("ci"), -2048.0, ad)
        late.append(alike(R("pH", 256, 384), R("cf"), R("lrn"), 8, "Ea", 1.0))
        ts(R("Og"), ind(R("alti"), R("cu")), -2048.0, ad)
        mms([(R("pA", 300, 300 + NS // 4), R("Zi", 12 - 4 * a, 140 - 4 * a), R("Og", NV + a, 128, 4), a == 0, a == 3) for a in range(4)])
        ts(R("OSu", 0, NS // 4), R("pA", 300, 300 + NS // 4), 2048.0, ad)
        for k in range(4):
            ts(mat("Og4", k), R("Og"), col("ex", k), mu_)
        mms(grp(R("pG", 256, 288), [(R("Z1", 15 - r, 143 - r), R("Og4", r, 512, 16)) for r in range(16)]))
        ts(R("OLu"), R("pG", 256, 288), 2048.0, ad)
        act(R("OL"), R("pG", 256, 288), bias=2048.0 + FALL)
        act(R("cxR"), ind(R("iox"), R("cu")))
        tt(R("hd", 0, 24, 3), R("OL", 16, 24), R("OL", 8, 16), sb)
        tt(R("hd", 1, 24, 3), R("OL", 8, 16), R("OL", 0, 8), sb)
        act(R("hd", 2, 24, 3), R("OL", 0, 8), bias=-FALL)
        act(R("y", 88, 96), R("OL", 24, 32), bias=-8192.0)
        act(R("y", 96, 104), R("OL", 24, 32), bias=17 * STEP + 8192.0)
        act(R("y", 32, 40), R("OL", 0, 8), bias=4096.0 - FALL)
        na = NA if t else 0
        for p in range(na):
            sel(R("A16", p, 16 * NV, 16), R("A", 0, NV), [[0, NV]], 0.0, 1, 0)
        if na < 16:
            acts([(R("A16", p, 16 * NV, 16), R("A", 0, NV), AF.Identity, 0.0, 1.0) for p in range(na, 16)])

    def onehot(sums, lanes, out):
        scan(R("sk", p1=lanes), R("dmax", p1=lanes), sums, ad, A_.max)
        tt(R("key", p1=lanes), sums, R("k15", p1=lanes), ad)
        tt(R("oh"), ind(R("sk"), R("EXPL")), R("key"), eq)
        mms(grp(out, [(R("oh", p1=lanes), R("idb", 0, lanes, p1=lanes))]))

    def farthest2():
        lst = R("cu")
        cp(R("C2u"), ind(Iw, lst))
        act(R("Xc"), ind(Pw, lst))
        act(R("old"), ind(Iw, lst))
        ts(R("oldh", 0, 128), R("C2u"), -2048.0, ad)
        for h in range(4):
            (cp if h < NG2 else act)(R("G2", 512 * h, 512 * h + 512), ind(Pw, R("C2u", 32 * h, 32 * h + 32)))

        def bank(b, pb):
            h, p0 = b // 2, 8 * (b % 2)
            mms([(R(pb, p, 512, 8), R("nid"), R("Xc", 64 * h, 64 * h + 64), p == 0, False) for p in range(8)])
            mms([(R(pb, p, 512, 8), R("idb"), R("G2", 1024 * h + p0 + p, 1024 * h + 1024, 16), False, p == 7) for p in range(8)])
            o = R("ab", 128 * p0 + 512 * h, 128 * p0 + 512 * h + 512)
            act(o, R(pb), AF.Abs)

        def first():
            for b in range(EARLY):
                bank(b, "p" + "DE"[b % 2])

        def rest():
            for b in range(EARLY, 4):
                bank(b, "p" + "CDEF"[b])
            for p0 in (0, 8):
                mms([(R("pB", p0 + p, 128, 16), R("ab", 128 * p0 + p, 128 * p0 + 1024, 8), R("B16"), p0 + p == 0, p0 + p == 15) for p in range(8)])
            onehot(R("pB", 0, 128), 128, R("pB", 128, 256))
        return first, rest

    def farthest3(lst):
        cp(R("C3u"), ind(Iw, lst))
        act(R("X3"), ind(R("Pw"), lst))
        cp(R("G3", 0, 512), ind(Pw, R("C3u", 0, 32)))
        act(R("G3", 512, 1024), ind(Pw, R("C3u", 32, 64)))
        act(R("ol3"), ind(Iw, lst))
        mms([(R("pD", p, 512, 16), R("nid"), R("X3", 32, 64), p == 0, False) for p in range(16)])
        mms([(R("pC", p, 512, 16), R("idb"), R("X3", 0, 32), p == 0, p == 15) for p in range(16)])
        mms([(R("pD"), R("idb"), R("G3", 512, 1024), False, True)])
        act(R("a3", 512, 1024), R("pD"), AF.Abs)
        tt(R("a3", 0, 512), R("G3", 0, 512), R("pC"), A_.max)
        mms([(R("pE", p, 128, 16, 0, 32), R("G3", p, 512, 16), R("B16n"), p == 0, False) for p in range(16)])
        mms([(R("pE", p, 128, 16, 0, 32), R("a3", p, 512, 16), R("B32"), False, p == 15) for p in range(16)])
        mms([(R("pE", p, 128, 16, 32, 64), R("a3", 512 + p, 1024, 16), R("B16"), p == 0, p == 15) for p in range(16)])

    def alike(valR, valL, use, nq, eb, sign):
        w = 16 * nq
        one = lambda r, q: (r[0], r[1] + q, r[1] + q + 1, 1, 0, 128)
        blk = lambda q: R(eb, (w + 16) * q, w * q + w)
        for h in range(2):
            acts([(blk(q), R(valR[0], valR[1] + 16 * q, valR[1] + w), AF.Abs, one(valL, q), sign) for q in range(h, nq, 2)])

        def rest():
            nv = NE if use else 0
            for q in range(nv):
                ts(blk(q), blk(q), one(use, q), A_.is_lt)
            for q in range(nv, nq, 2):
                acts([(blk(j), blk(j), AF.Relu, one(use, j) if use else 1.0, -1.0) for j in (q, q + 1)])
        return rest

    def lowest(nq, eb, bank, c0, sc, tgt, spare, y0, out):
        w = 16 * nq
        mms([(R(bank, c0 + r, c0 + w, 16), mat("Lt", r), R(eb, r, w * nq, w + 16), r == 0, False) for r in range(16)])
        mms([(R(bank, c0 + 16 + 16 * q, c0 + w), R("BO"), R(eb, (w + 16) * q + 16, w * q + w), False, q == nq - 2) for q in range(nq - 1)])
        scan(R(sc, 0, w), R("s16", 0, w), R(bank, c0, c0 + w), ad, A_.min)
        y = R("y", y0, y0 + nq)
        ts(y, R(sc, 15, w, 16), P(10), ad, 8192.0, mu_)
        tt(y, y, tgt, ad)
        tt(out, y, spare, A_.min)

    prep(0)
    for t in range(RO):
        now[0] = t
        chain([cp(R("CuS", 0, 32), ind(Iw, R("OSu", 0, 2))), cp(R("CuS", 32, 4 * NS), ind(Iw, R("OSu", 2, NS // 4))), cp(R("Cu"), ind(Iw, R("OLu")))])
        first2, rest2 = farthest2()
        first2()
        ch = []
        for l0 in range(0, NS, 16):
            l1 = min(NS, l0 + 16)
            for la in range(l0, l1, 4):
                ch.append(acts([(R("GS", 64 * i, 64 * i + 64), ind(Pw, R("CuS", 4 * i, 4 * i + 4)), AF.Abs, col("A", NV + i), -1.0) for i in range(la, la + 4)]))
            mms(grp(R("pB", 4 * l0, 4 * l1), [(R("Z1", 15 - p, 143 - p), R("GS", 64 * l0 + p, 64 * l1, 16)) for p in range(16)]))
        chain(ch)
        W = 16 * NV
        ch = []
        for k in range(4):
            cuts = [0, NV] if k < DCUT else [0, NV // 2, NV]
            for a, b in zip(cuts, cuts[1:]):
                ch.append(tt(R("D", W * k + 16 * a, W * k + 16 * b), ind(Pw, R("Cu", 128 * k + a, 128 * k + b)), R("A16", 16 * a, 16 * b), sb))
                chain(ch[-2:])
            ts(R("Rl", W * k, W * k + W), R("D", W * k, W * k + W), 0.0, A_.max)
            o = R("pA" if k % 2 else "pG", NV * k, NV * k + NV)
            mms([(o, R("Zm", 15 - p, 143 - p), R("D", W * k + p, W * k + W, 16), p == 0, False) for p in range(16)])
            mms([(o, R("Z2", 15 - p, 143 - p), R("Rl", W * k + p, W * k + W, 16), False, p == 15) for p in range(16)])
            ts(R("near", 128 * k, 128 * k + NV), o, col("thc", t), A_.is_le)
        if t == 0:
            for j in range(8):
                ts(R("Pw", 4096 + 512 * j, 4608 + 512 * j), R("Pw", 512 * j, 512 * j + 512), -1.0, mu_)
        ts(R("Ch"), R("Cu", 128, 512), -2048.0, ad)
        mms(grp(R("pC", 0, 384), [(R("Ldel"), R("Ch"))]))
        act(R("pF", 0, 384), R("pC", 0, 384), AF.Abs)
        for k in range(4):
            ts(R("near", 128 * k + NV, 128 * k + 128), R("pB", k, 4 * NS, 4), col("thc", t), A_.is_le)
        c1 = 16 if SPLIT else 32
        mms(grp(R("pH", 0, c1), [(R("Z1", 15 - r, 143 - r), R("near", r, 16 * c1, 16)) for r in range(16)]))
        ts(R("hn", 1, 24, 3), R("pH", 8, 16), 9.0, A_.is_lt)
        ts(R("hn", 2, 24, 3), R("pH", 0, 8), 9.0, A_.is_lt)
        scan(R("hs"), R("hn"), R("hd"), mu_, ad)
        cp(R("fou"), R("hs", 2, 24, 3))
        ts(R("Fh"), ind(Iw, R("fou")), -2048.0, ad)
        if SPLIT:
            mms(grp(R("pH", 16, 32), [(R("Z1", 15 - r, 143 - r), R("near", 256 + r, 512, 16)) for r in range(16)]))
        ts(R("sv", 0, 32), R("pH", 0, 32), 9.0, A_.is_ge)
        tt(R("sv", 32, 64), R("sv", 0, 32), R("OL"), mu_)
        tt(R("y", 48, 64), R("sv", 32, 48), R("sv", 48, 64), ad); tt(R("y", 8, 16), R("y", 48, 56), R("y", 56, 64), ad)
        tt(R("y", 16, 24), R("y", 8, 16), R("y", 96, 104), A_.min)
        tt(R("y", 16, 24), R("y", 16, 24), R("y", 88, 96), A_.max)
        ts(R("y", 24, 32), R("y", 8, 16), 1.0, A_.min, BIG + 18 * STEP, mu_)
        cnt = [R("pG", 0, 128), R("pG", 128, 256), R("pA", 0, 128)]
        for j in range(len(TURN)):
            mms([(R("p" + TURN[j], 0, 384), R("Lsig"), R("Ch"), True, False)])
        for j in range(8):
            if j == 0:
                mms([(cnt[k], mat("near", k + 1), R("nBO"), k != 1, False) for k in range(3)])
            if j == 4:
                mms([(R("pH", 128, 256), R("ones"), R("Kc"), True, False), (R("pH", 128, 256), R("Fh"), R("idb"), False, False)])
            pb = "p" + TURN[j % len(TURN)]; h = 384 * (j % 4)
            if j >= len(TURN):
                mms([(R(pb, 0, 384), R("Lsig"), R("Ch"), True, False)])
            mms([(R(pb, 128 * k, 128 * k + 128), mat("LF", j), R("Fh"), False, k == 2) for k in range(3)])
            act(R("Xab", h, h + 384), R(pb, 0, 384), AF.Abs)
            tt(R("E", h, h + 384), R("Xab", h, h + 384), R("pF", 0, 384), eq)
            mms([(R(cnt[k][0], cnt[k][1] + j, cnt[k][2], 8), R("E", h + 128 * k, h + 128 * k + 128), R("RE"), False, j == 7 and k > 0) for k in range(3)])
        ts(R("z", 0, 256), R("pG", 0, 256), -8.5, A_.is_lt)
        act(R("z", 256, 384), R("pA", 0, 128), AF.Relu, -8.0, -1.0)
        mms([(R("pH", 128, 256), R("bid"), mat("z", k), False, k == 1) for k in (2, 0, 1)])
        scan(R("sk"), R("dmin"), R("pH", 128, 256), ad, A_.min)
        tt(R("lT"), ind(R("sk"), R("EXPL")), R("mT"), mu_)
        mms(grp(R("pH", 256, 264), [(R("lT"), R("QS"))]))
        mms([(R("pG", 0, 8), R("idb"), R("K128"), True, False)])
        tt(R("mk"), R("pH", 256, 264), R("y", 16, 24), A_.min)
        tt(R("lrn"), R("mk"), R("y", 24, 32), A_.is_lt)
        ts(R("mi"), R("mk"), 4095, an)
        tt(R("lk"), R("lrn"), R("K128"), mu_)
        cp(R("mu"), R("mi"))
        mms([(R("pG", 0, 8), R("LmB"), R("lrn"), False, False)] + [(R("pG", s, 8), R("BO"), R("lrn", 0, 8 - s), False, False) for s in range(1, 8)])
        mms([(R("pG", 0, 8), R("nid"), R("lk"), False, True)])
        cp(R("posu"), R("pG", 0, 8))
        act(R("aR"), ind(R("iox"), R("mu")))
        s0 = SLOT * t
        cp(ind(R("pairs", s0, s0 + 384), R("posu")), R("aR"))
        scan(R("sa"), R("s16", 0, 64), R("pairs", s0, s0 + 64), ad, A_.min)
        ts(R("msg1", 8 * t, 8 * t + 4), R("sa", 15, 64, 16), P(9), ad)
        send(t, 0, R("msg1", 8 * t, 8 * t + 4), R("land1", 8 * t, 8 * t + 4))
        mms(grp(R("pH", 56, 64), [(R("ones"), R("lrn"))]))
        add("S", [lambda: g.scalar.activation(ap(R("y", 104, 112)), ap(R("pH", 56, 64)), AF.Identity, bias=256.0, accum_out=ap(R("ecol")))],
            [R("pH", 56, 64)], [R("y", 104, 112), R("ecol")], 90.0)
        rest2()
        ts(R("mh", 0, 8), R("mi"), -2048.0, ad)
        tt(R("mh", 8, 16), R("mk"), R("y", 24, 32), A_.is_lt)
        mms([(R("pA", 128, 384), R("idb"), R("oldh"), True, False)])
        mms([(R("pA", 128 + r, 384, 16), mat("nEr", r), R("mh"), False, r == 15) for r in range(16)])
        act(R("ohs"), R("pA", 128, 256))
        late.pop()()
        lowest(8, "Ea", "pG", 128, "sc4", R("cf"), R("dump"), 48, R("y", 48, 56))
        ts(R("tg2"), R("y", 48, 56), 2048.0, ad)
        tt(R("tt"), R("pB", 128, 256), R("ohs"), mu_)
        tt(ind(Iw, R("tg2")), R("old"), R("tt"), sb)
        act(R("vs", 0, 4), R("sa", 15, 64, 16), bias=P(9))
        if EBV:
            for q in range(4):
                ts(R("Eb", 80 * q, 64 * q + 64), R("pairs", s0 + 16 * q, s0 + 64), col("vs", q), eq)
        else:
            alike(R("pairs", s0, s0 + 64), R("vs"), None, 4, "Eb", -1.0)()
        cp(ind(R("pairs", s0 + 64, s0 + SLOT), R("posu")), R("cxR"))
        send(t, 1, R("pairs", s0 + 64, s0 + 128), R("land2", 64 * t, 64 * t + 64))
        lowest(4, "Eb", "pH", 64, "sb", R("vs", 0, 4), R("dum3", 0, 4), 64, R("y", 64, 68))
        cp(R("msg3", 8 * t, 8 * t + 4), R("y", 64, 68))
        send(t, 2, R("msg3", 8 * t, 8 * t + 4), R("land3", 8 * t, 8 * t + 4))
        farthest3(R("land1", 8 * t, 8 * t + 4))
        act(R("y", 8, 16), R("cf"), bias=R("ecol"), scale=37.0)
        tt(R("w1"), R("mi"), R("ci"), mu_)
        ts(R("w2"), R("w1"), 4, sh)
        tt(R("w1"), R("w2"), R("y", 8, 16), ad)
        ts(R("ci"), R("w1"), 4095, an)
        ts(R("w3"), R("mk"), 8192 + 4095, an)
        tt(R("y", 0, 8), R("w3"), R("y", 32, 40), A_.min)
        cp(R("selu"), R("y", 0, 8))
        tt(R("u"), ind(R("Pw"), R("selu")), R("A"), ad)
        act(R("au"), R("u"), AF.Abs, scale=0.4995)
        tt(R("v"), R("au"), R("pA", 256, 384), mu_)
        act(R("v"), R("v"), bias=MAGIC)
        if t == RO - 1:
            act(R("Af"), R("v"), bias=-MAGIC)
            dma("Y", T.ya[:, :], T.Af[:, :], [R("Af")], [], 2000)
        else:
            act(R("A"), R("v"), bias=-MAGIC)
        prep(t + 1)
        mms([(R("pF", 64, 128), R("nif"), R("ol3"), True, False), (R("pF", 64, 128), R("idf"), R("land2", 64 * t, 64 * t + 64), False, True)])
        act(R("dif"), R("pF", 64, 128))
        onehot(R("pE", 0, 128, 1, 0, 64), 64, R("pF", 0, 64))
        tt(R("tt", 0, 64), R("pF", 0, 64), R("dif"), mu_)
        tt(ind(Iw, R("land3", 8 * t, 8 * t + 4)), R("tt", 0, 64), R("ol3"), ad)
    dma("Y", T.yg[:, :], T.cR[0:128:16, :], [R("cR")], [], 2000)
    for j in list(range(N16, 16)) + list(range(N16)):
        o = R("pA", 0, 256)
        if j < N16:
            ts(R("Ih", 256 * j, 256 * j + 256), R("Iw", 256 * j, 256 * j + 256), -2048.0, ad)
            mms([(o, R("Zh", 15 - j, 143 - j), R("Ih", 256 * j, 256 * j + 256), False, j == N16 - 1)])
        else:
            mms([(o, R("Zf", 15 - j, 143 - j), R("Iw", 256 * j, 256 * j + 256), j == N16, False)])
    ts(R("ycs"), R("pA", 0, 256), P(14), ad)
    dma("Y", T.yc[:, :], T.ycs[:, :], [R("ycs")], [], 2000)
    return ops, nsent[0]


def window(ops, pre, suc, st, t0, t1, passes, rand):
    n = len(ops)
    dur = [o["cost"] + o["lat"] for o in ops]
    tail, nxt, qe = [0.0] * n, {}, {}
    for i in sorted(range(n), key=lambda x: -st[x]):
        if st[i] < t1:
            break
        e = ops[i]["eng"]
        tail[i] = max([dur[i] + h + tail[j] for j, h in suc[i]] + [dur[i], ops[i]["cost"] + (nxt.get(e, 0.0) if e != "-" else 0.0)])
        nxt[e] = qe[e] = tail[i]
    qe.pop("-", None)
    w = [i for i in range(n) if t0 <= st[i] < t1]
    at = {i: k for k, i in enumerate(w)}
    sub = [ops[i] for i in w]
    p2 = [[(at[j], h) for j, h in pre[i] if j in at] for i in w]
    s2 = [[(at[j], h) for j, h in suc[i] if j in at] for i in w]
    rel = [max([st[j] + dur[j] + h for j, h in pre[i] if j not in at] + [0.0]) for i in w]
    out = [max([tail[j] + h for j, h in suc[i] if j not in at] + [0.0]) for i in w]
    free = {}
    for i in range(n):
        if st[i] < t0 and ops[i]["eng"] != "-":
            free[ops[i]["eng"]] = max(free.get(ops[i]["eng"], 0.0), st[i] + ops[i]["cost"])
    m = len(w)
    if m < 2:
        return st
    seq = topo_order(m, p2, s2, [st[i] for i in w])
    best = None
    if passes < 0:
        best = anneal(sub, seq, p2, s2, rel, out, free, qe, -passes, rand)
    for it in range(passes):
        s = place(sub, seq, p2, False, rel, free)
        v = max(max(s[k] + dur[i] + out[k], s[k] + sub[k]["cost"] + qe.get(sub[k]["eng"], 0.0)) for k, i in enumerate(w))
        if best is None or v < best[1]:
            best = (s, v)
        elif it % 2 == 0:
            s = best[0]
        a = NOISE * rand() * rand() * (it % 2 == 0)
        bt = place(sub, topo_order(m, s2, p2, [-s[k] - dur[i] + a * rand() for k, i in enumerate(w)]), s2, True, out, qe)
        seq = topo_order(m, p2, s2, [-(bt[k] + sub[k]["cost"]) + a * rand() for k in range(m)])
    key = [st[i] + (1e7 if st[i] >= t1 else 0.0) for i in range(n)]
    for k, i in enumerate(w):
        key[i] = max(t0, best[0][k])
    return place(ops, topo_order(n, pre, suc, key), pre, False)


def tabu(ops, seq, pre, suc, rel, out, free, qe, steps, rand):
    n = len(ops)
    c = [o["cost"] for o in ops]
    d = [o["cost"] + o["lat"] for o in ops]
    pa = [[(j, d[j] + h) for j, h in pre[i]] for i in range(n)]
    sa = [[(j, d[i] + h) for j, h in suc[i]] for i in range(n)]
    fixed = [set(j for j, _h in suc[i]) for i in range(n)]
    before, after, last = [-1] * n, [-1] * n, {}
    for i in seq:
        e = ops[i]["eng"]
        if e != "-":
            if e in last:
                before[i] = last[e]; after[last[e]] = i
            last[e] = i
    r0 = [max(rel[i], free.get(ops[i]["eng"], 0.0)) for i in range(n)]
    q0 = [max(d[i] + out[i], c[i] + qe.get(ops[i]["eng"], 0.0)) for i in range(n)]
    deg = [len(p) for p in pre]
    best, banned, since = None, {}, 0
    for it in range(steps):
        left = [deg[i] + (before[i] >= 0) for i in range(n)]
        order = [i for i in range(n) if not left[i]]
        r = list(r0)
        for i in order:
            ri = r[i]
            for j, w in sa[i]:
                if ri + w > r[j]:
                    r[j] = ri + w
                left[j] -= 1
                if not left[j]:
                    order.append(j)
            j = after[i]
            if j >= 0:
                if ri + c[i] > r[j]:
                    r[j] = ri + c[i]
                left[j] -= 1
                if not left[j]:
                    order.append(j)
        q = list(q0)
        for i in reversed(order):
            v = q[i]
            for j, w in sa[i]:
                if w + q[j] > v:
                    v = w + q[j]
            j = after[i]
            if j >= 0 and c[i] + q[j] > v:
                v = c[i] + q[j]
            q[i] = v
        end = max(r[i] + q[i] for i in range(n))
        since += 1
        if best is None or end < best[1] - 0.01:
            best, since = (r, end, list(before), list(after)), 0
        elif since > STALL:
            before, after, since, banned = list(best[2]), list(best[3]), 0, {}
            continue
        pick = None
        for u in range(n):
            v = after[u]
            if v < 0 or r[u] + q[u] < end - 0.01 or r[u] + c[u] + q[v] < end - 0.01 or v in fixed[u]:
                continue
            a, b = before[u], after[v]
            rv = max([r0[v], r[a] + c[a] if a >= 0 else 0.0] + [r[j] + w for j, w in pa[v]])
            ru = max([r0[u], rv + c[v]] + [r[j] + w for j, w in pa[u]])
            qu = max([q0[u], c[u] + q[b] if b >= 0 else 0.0] + [w + q[j] for j, w in sa[u]])
            qv = max([q0[v], c[v] + qu] + [w + q[j] for j, w in sa[v]])
            val = max(rv + qv, ru + qu)
            if banned.get((u, v), -1) > it and val >= best[1]:
                val += 1e6
            val += JITTER * rand()
            if pick is None or val < pick[0]:
                pick = (val, u, v)
        if pick is None:
            break
        _val, u, v = pick
        a, b = before[u], after[v]
        if a >= 0:
            after[a] = v
        if b >= 0:
            before[b] = u
        before[v], after[v], before[u], after[u] = a, u, v, b
        banned[(v, u)] = it + 8 + int(12 * rand())
    return best


def anneal(ops, seq, pre, suc, rel, out, free, qe, steps, rand):
    n = len(ops)
    c = [o["cost"] for o in ops]
    d = [o["cost"] + o["lat"] for o in ops]
    sa = [[(j, d[i] + h) for j, h in suc[i]] for i in range(n)]
    r0 = [max(rel[i], free.get(ops[i]["eng"], 0.0)) for i in range(n)]
    q0 = [max(d[i] + out[i], c[i] + qe.get(ops[i]["eng"], 0.0)) for i in range(n)]
    deg = [len(p) for p in pre]
    qs = {}
    for i in seq:
        if ops[i]["eng"] != "-":
            qs.setdefault(ops[i]["eng"], []).append(i)

    def times():
        left, after = list(deg), [-1] * n
        for l in qs.values():
            for a, b in zip(l, l[1:]):
                after[a] = b; left[b] += 1
        order = [i for i in range(n) if not left[i]]
        r, by = list(r0), [-1] * n
        for i in order:
            ri = r[i]
            for j, w in sa[i]:
                if ri + w > r[j]:
                    r[j] = ri + w; by[j] = i
                left[j] -= 1
                if not left[j]:
                    order.append(j)
            j = after[i]
            if j >= 0:
                if ri + c[i] > r[j]:
                    r[j] = ri + c[i]; by[j] = i
                left[j] -= 1
                if not left[j]:
                    order.append(j)
        if len(order) < n:
            return None
        i = max(range(n), key=lambda x: r[x] + q0[x])
        return r, r[i] + q0[i] + TIE * sum(r) / n, by, i, after
    cur = best = times()
    held = None
    for it in range(steps):
        if held is None:
            held, i = [], cur[3]
            while cur[2][i] >= 0:
                if cur[4][cur[2][i]] == i:
                    held.append((cur[2][i], i))
                i = cur[2][i]
        if not held:
            break
        a, b = held[int(rand() * len(held))]
        l = qs[ops[a]["eng"]]
        x = a if rand() < 0.5 else b
        k = l.index(x)
        s = 1 + int(REACH * rand() ** 2)
        k2 = min(len(l) - 1, k + s) if x == a else max(0, k - s)
        l.insert(k2, l.pop(k))
        new = times()
        if new is not None and new[1] <= cur[1] + HEAT * (1.0 - it / steps) * rand() ** 3:
            cur, held = new, None
            if new[1] < best[1]:
                best = new
        else:
            l.insert(k, l.pop(k2))
    return best


def place(ops, seq, pre, back, rel=None, free=None):
    st = [0.0] * len(ops)
    busy = {e: ([-1.0], [f]) for e, f in (free or {}).items()}
    for i in seq:
        o = ops[i]
        if back:
            r = max([st[j] + ops[j]["cost"] + h for j, h in pre[i]] + [rel[i] if rel else 0.0]) + o["lat"]
        else:
            r = max([st[j] + ops[j]["cost"] + ops[j]["lat"] + h for j, h in pre[i]] + [rel[i] if rel else 0.0])
        if o["eng"] != "-":
            a, b = busy.setdefault(o["eng"], ([], []))
            lo, hi = 0, len(b)
            while lo < hi:
                m = (lo + hi) // 2
                if b[m] <= r:
                    lo = m + 1
                else:
                    hi = m
            while lo < len(a) and a[lo] < r + o["cost"]:
                r = max(r, b[lo]); lo += 1
            a.insert(lo, r); b.insert(lo, r + o["cost"])
        st[i] = r
    return st


def schedule(ops):
    if "order" in REPORT:
        return REPORT["order"]
    n = len(ops)
    pre = [[] for _ in ops]; suc = [[] for _ in ops]
    reach = [0] * n
    for i, o in enumerate(ops):
        far = 0
        for j in o["hard"]:
            far |= reach[j]
        near = [(j, HOP) for j in o["hard"] if ops[j]["lat"] or not far >> j & 1] + [(j, -ops[j]["lat"]) for j in o["soft"] if not far >> j & 1]
        for j in o["hard"]:
            far |= 1 << j
        reach[i] = far
        pre[i] = near
        for j, h in near:
            suc[j].append((i, h))
    state = [SEED * 2654435761 % (1 << 31) + 1]

    def rand():
        state[0] = state[0] * 48271 % 2147483647
        return state[0] / 2147483647.0
    best = None
    seq = topo_order(n, pre, suc, list(range(n)))
    for it in range(PASSES):
        st = place(ops, seq, pre, False)
        end = max(st[i] + ops[i]["cost"] + ops[i]["lat"] for i in range(n))
        if best is None or end < best[1]:
            best = (st, end)
        elif it % 2 == 0:
            st = best[0]
        fin = [st[i] + ops[i]["cost"] + ops[i]["lat"] for i in range(n)]
        c, w, a = rand() * best[1], 3000 + 12000 * rand(), NOISE * rand() * (it % 2 == 0)
        bt = place(ops, topo_order(n, suc, pre, [-f + (a * rand() if abs(f - c) < w else 0.0) for f in fin]), suc, True)
        seq = topo_order(n, pre, suc, [-(bt[i] + ops[i]["cost"]) + (a * rand() if abs(fin[i] - c) < w else 0.0) for i in range(n)])
    for it in range(SWEEPS):
        for wide, tries in ((WIDE, TRIES), (WIDE2, -STEPS)):
            t0 = -wide * rand()
            while t0 < best[1] and tries:
                st = window(ops, pre, suc, best[0], t0, t0 + wide, tries, rand)
                end = max(st[i] + ops[i]["cost"] + ops[i]["lat"] for i in range(n))
                if end <= best[1]:
                    best = (st, end)
                t0 += wide / 2
    REPORT["order"] = (topo_order(n, pre, suc, best[0]), best[1], best[0])
    return REPORT["order"]


def topo_order(n, pre, suc, key):
    left = [len(p) for p in pre]
    out, seen = [], [False] * n
    for i in sorted(range(n), key=lambda x: key[x]):
        seen[i] = True
        if left[i] == 0:
            todo = [i]
            while todo:
                k = todo.pop()
                out.append(k)
                for j, _h in suc[k]:
                    left[j] -= 1
                    if left[j] == 0 and seen[j]:
                        todo.append(j)
    return out


def rank_program(g, core, T, topo):
    if T.rank_of(core) is None:
        return
    ops, nsent = build(g, core, T, topo)
    order, end, st = schedule(ops)
    for i, o in enumerate(ops):
        o["t"] = st[i]
    REPORT["ops"] = ops; REPORT["end"] = end
    q = {"V": g.vector, "S": g.scalar, "P": g.tensor, "G": g, "Y": g.sync}
    cnt = {e: 0 for e in CNT}
    known = {e: {} for e in q}
    mark = {}
    for i in order:
        o = ops[i]; e = o["eng"]
        if o["kind"] == "a":
            mark[i] = (o["sem"][0], o["sem"][1], {})
            continue
        kn = known[e]
        need = {}
        for j in o["hard"]:
            if ops[j]["kind"] == "r":
                continue
            s, v, _k = mark[j]
            if kn.get(s, 0) < v and need.get(s, (0, None))[0] < v:
                need[s] = (v, j)
        for s, (v, j) in sorted(need.items(), key=lambda x: -ops[x[1][1]]["t"]):
            if kn.get(s, 0) >= v:
                continue
            q[e].wait_ge(T.sem[s], v)
            kn[s] = v
            for s2, v2 in mark[j][2].items():
                kn[s2] = max(kn.get(s2, 0), v2)
        if o["kind"] == "c":
            for f in o["fns"]:
                f().then_inc(T.sem[CNT[e]], 1)
                cnt[e] += 1
            mark[i] = (CNT[e], cnt[e], dict(kn))
        elif o["kind"] == "d":
            o["fns"][0]().then_inc(T.sem[o["sem"]], 16)
            mark[i] = (o["sem"], 16, dict(kn))
        else:
            o["fns"][0]()
    for e in CNT:
        g.wait_ge(T.sem[CNT[e]], cnt[e])
    for o in ops:
        if o["kind"] == "d":
            g.wait_ge(T.sem[o["sem"]], 16)
        elif o["kind"] == "a":
            g.wait_ge(T.sem[o["sem"][0]], o["sem"][1])
    g.wait_ge(T.sem.sent, nsent)
